import numpy as np, ml_dtypes
CORES = [36,164,52,180,100,228,116,244]
N = 8
BF = ml_dtypes.bfloat16
M, L, KH, CAP, RO, OC = 4096, 512, 8, 64, 3, 1024
S = 8
def pack(b, o, w):
    return {"ball": np.ascontiguousarray(b.reshape(N, 128, M)).astype(np.float32).astype(BF), "stk": np.ascontiguousarray(o.reshape(N, 128, L)).astype(np.int32),
            "wt": np.ascontiguousarray(w.reshape(N, 128, 1)).astype(np.float32).astype(BF)}
def halves(rng):
    bright = np.argsort(rng.random((N, 8, M)), axis=-1) < M // 2
    return np.where(bright[:, :, None], rng.integers(140, 256, (N, 8, 16, M)), rng.integers(0, 120, (N, 8, 16, M))), bright
def stacks(rng, kk, bright):
    br, di = np.flatnonzero(bright), np.flatnonzero(~bright); dep = np.arange(16)[:, None]
    o = rng.integers(0, M, (16, L)); top = np.where(kk > 0, rng.choice(br, L), rng.choice(di, L))
    o = np.where((dep > 0) & (dep <= kk), rng.choice(di, (16, L)), o)
    o = np.where(dep == kk + 1, np.where(kk > 0, top, rng.choice(br, L)), o)
    o[0] = top
    return o
def later(rng, z):
    kk = np.concatenate([np.full(L // 2, 15), np.zeros(z, np.int64), rng.integers(1, KH, L - L // 2 - z)])
    kk[:int(np.sum(kk)) % S] = 14
    kk = rng.permutation(kk); dep = np.arange(16)[:, None]
    kind = rng.permutation(np.arange(M - L) % 3)
    b = rng.integers(0, 256, (16, M))
    b[:, L:] = np.where(kind == 0, rng.integers(0, 40, (16, M - L)), np.where(kind == 1, rng.integers(60, 200, (16, M - L)), 255))
    low, mid, top = L + np.flatnonzero(kind == 0), L + np.flatnonzero(kind == 1), L + np.flatnonzero(kind == 2)
    o = np.where((dep > 0) & (dep <= kk), rng.choice(mid, (16, L)), rng.integers(0, M, (16, L)))
    o = np.where(dep == kk + 1, rng.choice(top, (16, L)), o)
    o[0] = rng.choice(low, L)
    return b, o
def quiet(rng, a):
    c = np.arange(M) // L; free = rng.permutation(np.flatnonzero((c > 0) & (c != a)))
    low, top = free[:16], free[16:M // 2]
    b = rng.integers(0, 256, (16, M)); b[:, low] = 0; b[:, top] = 255
    o = rng.integers(0, M, (16, L)); one = rng.permutation(L) < a
    o[0] = np.where(one, rng.choice(top, L), o[0]); o[1] = np.where(one, rng.choice(low, L), rng.choice(top, L)); o[2] = np.where(one, rng.choice(top, L), o[2])
    return b, o
def setup_inputs(rng):
    lev = rng.integers(0, 256, (N, 8, 1, M))
    b = np.clip(lev + np.rint(24 * rng.standard_normal((N, 8, 16, M), dtype=np.float32)).astype(np.int64), 0, 255)
    o = rng.integers(0, M, (N, 8, 16, L)); high = np.argsort(lev[:, :, 0], axis=-1)[..., M - M // 8:]
    pick = np.take_along_axis(high, rng.integers(0, M // 8, (N, 8, L)), 2); share = rng.choice(np.array([0.0, 0.1, 0.3, 0.5]), (N, 8, 1))
    o[:, :, 0] = np.where(rng.random((N, 8, L)) < share, pick, o[:, :, 0])
    return pack(b, o, rng.integers(0, 256, (N, 8, 16, 1)))
def setup_inputs_room(rng):
    b, bright = halves(rng); o = np.zeros((N, 8, 16, L), np.int64); c = np.array([0, 1, CAP - 1, CAP, CAP + 1, L])
    for q in range(N):
        for g in range(8):
            n, z = int(rng.choice(c)), int(rng.choice(c))
            if q in (0, 2): n = (CAP, CAP + 1, L, CAP - 1, 1, 0, CAP, CAP + 1)[g]
            if q in (1, 3):
                z = (CAP, CAP + 1, CAP, CAP, 0, L, CAP - 1, 1)[g]; n = min(n, L - z)
            z = min(z, L - n)
            kk = np.concatenate([rng.choice(np.array([KH, KH, KH + 1, 15]), n), np.zeros(z, np.int64), rng.choice(np.array([1, KH // 2, KH - 1, KH - 1]), L - n - z)])
            kk = rng.permutation(kk)
            if q in (0, 2) and g == 0:
                i = int(np.flatnonzero(kk >= KH)[0]); kk[[i, L - 1]] = kk[[L - 1, i]]
            if q in (1, 3) and g < 3: kk = kk[np.argsort(kk > 0, kind="stable")]
            o[q, g] = stacks(rng, kk, bright[q, g])
    return pack(b, o, rng.integers(0, 256, (N, 8, 16, 1)))
def setup_inputs_votes(rng):
    base = rng.integers(1, 255, (N, 8, 16, 1)); j = rng.choice(np.array([7, 8, 9, 10, 16]), (N, 8, 1, M), p=[0.04, 0.06, 0.5, 0.2, 0.2])
    place = np.argsort(rng.random((N, 8, 16, M)), axis=2)
    b = base - (place < j) + (place >= j) * rng.integers(0, 2, (N, 8, 16, M))
    b[..., ::4] = base
    o = 4 * rng.integers(0, M // 4, (N, 8, 16, L)) + rng.integers(1, 4, (N, 8, 16, L))
    o[:, :, 0] = np.where(rng.random((N, 8, L)) < 0.7, 4 * rng.integers(0, M // 4, (N, 8, L)), o[:, :, 0])
    return pack(b, o, rng.integers(0, 256, (N, 8, 16, 1)))
def setup_inputs_ends(rng):
    b, bright = halves(rng); b[..., 0] = 255; b[..., M - 1] = 0; bright[..., 0] = True; bright[..., M - 1] = False
    b[:, 4, :, 1023] = 255; b[:, 4, :, M - 16] = 0; bright[:, 4, 1023] = True; bright[:, 4, M - 16] = False
    o = np.zeros((N, 8, 16, L), np.int64); w = rng.integers(0, 256, (N, 8, 16, 1)); w[:, 0::2] = 255; w[:, 1] = 0; w[:, 5:] = 0
    for q in range(N):
        for g in range(8):
            kk = rng.integers(0, 16, L); kk[0] = 15 * (q % 2); kk[L - 1] = 15 * (1 - q % 2)
            if g == 4: kk[:] = 15
            if g == 6: b[q, g], o[q, g] = quiet(rng, int(rng.integers(1, S)))
            elif g in (5, 7): b[q, g], o[q, g] = later(rng, (0, 1, CAP // 2, CAP - 1)[(q + g) % 4])
            else: o[q, g] = stacks(rng, kk, bright[q, g])
    o[:, 0] = rng.choice(np.array([M - 1, M - 1, M - 1, M - 1, M - 1, M - 1, 0]), (N, 16, L))
    o[:, 0, 0] = rng.choice(np.array([0, 0, M - 1]), (N, L))
    o[:, 2] = o[:, 2, :1]
    far = np.where(np.arange(16)[:, None] == 0, 1023, rng.choice(np.array([M - 1, M - 16]), (N, 16, L)))
    o[:, 4] = np.where(rng.random((N, 1, L)) < 0.25, far, o[:, 4])
    return pack(b, o, w)
def setup_inputs_spread(rng):
    b = np.minimum(np.exp2(8.5 * rng.random((N, 8, 1, M))) * rng.random((N, 8, 16, M)), 255.0).astype(np.int64) * (rng.random((N, 8, 1, M)) > 0.0625)
    w = np.exp2(8 * rng.random((N, 8, 16, 1))).astype(np.int64) - 1
    o = (M * rng.random((N, 8, 16, L)) ** rng.choice(np.array([1, 2, 4]), (N, 8, 1, 1))).astype(np.int64)
    return pack(b, o, w)
def check_inputs(d):
    bad = []
    for k, hi in (("ball", 255), ("stk", M - 1), ("wt", 255)):
        v = np.asarray(d[k]).astype(np.float64)
        if not (np.min(v) >= 0 and np.max(v) <= hi): bad.append("range of " + k)
        elif np.any(v != np.floor(v)): bad.append("whole numbers in " + k)
    return bad
def reference(ball, stk, wt):
    b = ball.astype(np.float32).astype(np.int64).reshape(N, 8, 16, M)
    o = stk.astype(np.int64).reshape(N, 8, 16, L)
    w = wt.astype(np.float32).astype(np.int64).reshape(N, 8, 16, 1)
    lane = np.arange(L); dep = np.arange(16)[:, None]
    for t in range(RO):
        p = np.take_along_axis(b, o.reshape(N, 8, 1, 16 * L), 3).reshape(N, 8, 16, 16, L)
        x, rest = p[:, :, :, 0], p[:, :, :, 1:]
        won = np.add.reduce((x[:, :, :, None] > rest).astype(np.int64), axis=2) >= 9
        crossed = np.multiply.accumulate(won.astype(np.int64), axis=2)
        k = np.add.reduce(crossed, axis=2)
        top = np.where(k[:, :, None] == 0, 255, np.max(rest * crossed[:, :, None], axis=3))
        y = np.abs(x - top)
        A = np.add.reduce(k, axis=2)
        v = L * ((np.add.reduce(w * y, axis=2) + A[:, :, None]) & (S - 1)) + lane
        new = (((o * (2 * (o[:, :, :1] & 1023) + 1)) >> 4) + A[:, :, None, None]) & (M - 1)
        up = np.concatenate([new[:, :, 1:], new[:, :, :1]], axis=2)
        o = np.where(dep < k[:, :, None], up, np.where(dep == k[:, :, None], v[:, :, None], o))
        z = y.copy()
        for r in range(N):
            q = (r - 1 - t) % N
            for g in range(8):
                src = np.flatnonzero(k[q, g] >= KH)[:CAP]; dst = np.flatnonzero(k[r, g] == 0)[:len(src)]
                z[r, g][:, dst] = y[q, g][:, src[:len(dst)]]
        np.put_along_axis(b, v[:, :, None, :], z, 3)
    return {"yo": o.reshape(N, 128, L).astype(np.float32), "yb": b.reshape(N, 128, M)[:, :, :OC].astype(np.float32).astype(BF)}

@@ -1,0 +1,460 @@
+from concourse.mybir import AluOpType, ActivationFunctionType
+
+F, B, I, U = "float32", "bfloat16", "int32", "uint16"
+
+
+def sb(n, d):
+    return ("sbuf", [128, n], d)
+
+
+SCRATCH = {
+    "bl": sb(4160, B), "P": sb(8192, B), "PM": sb(8192, B), "C": sb(3840, B),
+    "si": sb(512, I), "off": sb(512, U), "o": sb(512, F), "w": sb(1, B),
+    "ci": sb(1, I), "cgi": sb(1, I), "cai": sb(1, I), "cG": sb(1, F), "cA": sb(1, F), "cP": sb(1, F), "dh": sb(1, F), "dm": sb(1, F),
+    "c15": sb(1, F), "c16": sb(1, F), "z0": sb(1, F), "wi": sb(1, I), "wf": sb(1, F),
+    "rG": sb(128, B), "rA": sb(128, B), "rP": sb(144, F), "r8": sb(8, B), "dd16": sb(2048, B),
+    "BO": sb(128, B), "BOf": sb(128, F), "M16": sb(128, B), "ID": sb(128, B), "IDf": sb(128, F), "TRI": sb(128, B),
+    "UP": sb(128, B), "W": sb(144, B), "SHf": sb(128, F), "SHn": sb(128, B), "SHI": sb(128, B), "BC0": sb(128, F),
+    "BCn": sb(128, B), "WS": sb(128, B), "DBn": sb(8, B), "DBf": sb(8, F), "RM": sb(2048, B), "R16": sb(128, B), "RR": sb(64, B),
+    "ones": sb(512, B), "hi": sb(512, B), "lo": sb(512, B), "r256": sb(8, B), "a16": sb(128, B), "lt15": sb(128, B), "e15": sb(128, B),
+    "iw": sb(32, F), "il": sb(32, F), "il8": sb(32, F), "ix": sb(32, F), "cpos": sb(64, F), "nd": sb(4, F), "LN": sb(512, F),
+    "DF": sb(64, F), "rr": sb(64, F),
+    "fl": sb(512, B), "E2": sb(512, F), "T1": sb(512, I), "q": sb(512, I), "qA": sb(512, F), "Xn": sb(512, F), "tt": sb(512, F),
+    "Ui": sb(512, I), "sg": sb(512, B), "nX": sb(512, B), "acc": sb(4, F), "km": sb(512, B), "lu": sb(32, U),
+    "df": sb(512, B), "y": sb(576, B), "ym": sb(512, F), "Rr": sb(576, F), "A": sb(1, F), "A5": sb(1, F), "FZ": sb(64, B),
+    "sc": sb(64, F), "ri": sb(64, F), "tm": sb(64, F), "po": sb(32, F), "pu": sb(32, U), "IDb": sb(1536, F),
+    "idm": sb(128, F), "ids": sb(128, F), "idu": sb(4, U), "idv": sb(4, U), "iwA": sb(32, F), "vi": sb(32, I),
+    "vu": sb(32, U), "zf": sb(4, F), "cb": sb(4, F), "cc": sb(4, F), "Rz": sb(64, F), "zm": sb(64, F), "zs": sb(64, F), "zi": sb(4, I),
+    "zo": sb(4, F), "zu": sb(4, U),
+}
+for _t in range(3):
+    SCRATCH["ty%d" % _t] = sb(64, B)
+    SCRATCH["ry%d" % _t] = sb(64, B)
+    SCRATCH["tf%d" % _t] = sb(4, F)
+    SCRATCH["rf%d" % _t] = sb(4, F)
+for _b in range(8):
+    SCRATCH["b%d" % _b] = ("psum", [128, 512], F)
+
+SEMAPHORES = ["sV", "sS", "sP", "sG", "dstk", "dball", "dwt", "dyo", "dyb", "loc"]
+for _t in range(3):
+    SEMAPHORES += ["aY%d" % _t, "aF%d" % _t]
+
+PIECE = [(0, 64), (64, 128), (128, 256), (256, 384), (384, 512)]
+VX = 160
+
+
+def rank_program(g, core, T, topo):
+    rank = T.rank_of(core)
+    if rank is None:
+        return
+    N = len(T.cores)
+    OP, ACT = AluOpType, ActivationFunctionType
+    eng = {"V": g.vector, "S": g.scalar, "P": g.tensor, "G": g, "Y": g.sync}
+    cnt = {}
+    known = {q: {} for q in eng}
+    clk = {}
+    hist = {}
+
+    def r(name, a=0, b=None, s=1, n=128):
+        return (name, a, SCRATCH[name][1][1] if b is None else b, s, n)
+
+    def ap(x):
+        t = T[x[0]]
+        if x[3] == 1:
+            return t[:, x[1]:x[2]] if x[4] == 128 else t[0:x[4], x[1]:x[2]]
+        return t[:, x[1]:x[2]:x[3]]
+
+    def meet(x, y):
+        if x[2] <= y[1] or y[2] <= x[1]:
+            return False
+        if x[3] == y[3] and x[3] > 1 and (x[1] - y[1]) % x[3]:
+            return False
+        return True
+
+    def inside(x, y):
+        return y[3] == 1 and y[1] <= x[1] and x[2] <= y[2]
+
+    def learn(q, sem, n):
+        k = known[q]
+        for e, v in clk.get((sem, n), {sem: n}).items():
+            if v > k.get(e, 0):
+                k[e] = v
+
+    def need(q, sem, n):
+        if known[q].get(sem, 0) < n:
+            eng[q].wait_ge(T.sem[sem], n)
+            learn(q, sem, n)
+
+    def deps(q, reads, writes, group=False):
+        want = {}
+        for x, w in [(x, False) for x in reads] + [(x, True) for x in writes]:
+            psum = SCRATCH[x[0]][0] == "psum"
+            for (q2, sem, n, y, w2) in hist.get(x[0], []):
+                if q2 == q and (not w2 or group):
+                    continue
+                if not (q2 != q and psum) and (not (w or w2) or not meet(x, y)):
+                    continue
+                want[sem] = max(want.get(sem, 0), n)
+        for sem in sorted(want, key=lambda e: -want[e]):
+            need(q, sem, want[sem])
+
+    def note(q, sem, n, reads, writes):
+        for x, w in [(x, False) for x in reads] + [(x, True) for x in writes]:
+            h = hist.setdefault(x[0], [])
+            if w:
+                psum = SCRATCH[x[0]][0] == "psum"
+                h[:] = [e for e in h if not (inside(e[3], x) and (not psum or e[0] == q or known[q].get(e[1], 0) >= e[2]))]
+            else:
+                h[:] = [e for e in h if not (e[0] == q and not e[4] and e[3] == x)]
+            h.append((q, sem, n, x, w))
+        c = dict(known[q])
+        c[sem] = n
+        clk[(sem, n)] = c
+
+    def op(q, reads, writes, call, group=False):
+        deps(q, reads, writes, group)
+        sem = "s" + q
+        cnt[sem] = cnt.get(sem, 0) + 1
+        call().then_inc(T.sem[sem], 1)
+        note(q, sem, cnt[sem], reads, writes)
+
+    def isr(x):
+        return isinstance(x, tuple)
+
+    def val(x):
+        return ap(x) if isr(x) else x
+
+    def tt(out, a, b, o):
+        op("V", [a, b], [out], lambda: g.vector.tensor_tensor(ap(out), ap(a), ap(b), o))
+
+    def ts(out, a, s1, o0, s2=None, o1=None):
+        rd = [a] + [x for x in (s1, s2) if isr(x)]
+        if o1 is None:
+            op("V", rd, [out], lambda: g.vector.tensor_scalar(ap(out), ap(a), val(s1), None, o0))
+        else:
+            op("V", rd, [out], lambda: g.vector.tensor_scalar(ap(out), ap(a), val(s1), val(s2), o0, o1))
+
+    def cp(out, a):
+        op("V", [a], [out], lambda: g.vector.tensor_copy(ap(out), ap(a)))
+
+    def ms(out, v):
+        op("V", [], [out], lambda: g.vector.memset(ap(out), v))
+
+    def scan(out, d0, d1, o0, o1):
+        op("V", [d0, d1], [out], lambda: g.vector.tensor_tensor_scan(ap(out), ap(d0), ap(d1), 0.0, o0, o1))
+
+    def act(out, a, f, bias=0.0, scale=1.0, acc=None):
+        rd = [a] + [x for x in (bias, scale) if isr(x)]
+        if acc is None:
+            op("S", rd, [out], lambda: g.scalar.activation(ap(out), ap(a), f, bias=val(bias), scale=val(scale)))
+        else:
+            op("S", rd, [out, acc], lambda: g.scalar.activation(ap(out), ap(a), f, bias=val(bias), scale=val(scale), accum_out=ap(acc)))
+
+    def mm(out, l, rhs, start=True, stop=True):
+        op("P", [l, rhs], [out], lambda: g.tensor.matmul(ap(out), ap(l), ap(rhs), start, stop), group=not start)
+
+    def iota(out, pat, base=0, cm=0):
+        if SCRATCH[out[0]][2] == I:
+            op("G", [], [out], lambda: g.iota(ap(out), pat, base, cm))
+        else:
+            op("G", [], [out], lambda: g.iota(ap(out), pat, base, cm, allow_small_or_imprecise_dtypes=True))
+
+    def gather(q, out, win, offs):
+        if q == "V":
+            op("V", [win, offs], [out], lambda: g.vector.tensor_copy(ap(out), ap(win).indirect(ap(offs))))
+        else:
+            op("S", [win, offs], [out], lambda: g.scalar.activation(ap(out), ap(win).indirect(ap(offs)), ACT.Copy))
+
+    def scatter(win, offs, a):
+        op("V", [a, offs], [win], lambda: g.vector.tensor_copy(ap(win).indirect(ap(offs)), ap(a)))
+
+    def dma(q, out, a, sem, rd, wr):
+        deps(q, rd, wr)
+        eng[q].dma_start(out, a).then_inc(T.sem[sem], 16)
+        cnt[sem] = 16
+        for x in rd:
+            hist.setdefault(x[0], []).append((sem, sem, 16, x, False))
+        for x in wr:
+            hist.setdefault(x[0], []).append((sem, sem, 16, x, True))
+        c = dict(known[q])
+        c[sem] = 16
+        clk[(sem, 16)] = c
+
+    def send(src, dst_buf, to, sem):
+        deps("G", [src], [])
+        rid, pid = topo.addr(to, core)
+        g.remote_dma(ap((dst_buf,) + src[1:]), ap(src), T.sem[sem], T.sem["loc"], pid, rid, topo.mask(core, to))
+        cnt["loc"] = cnt.get("loc", 0) + len(topo.engines(core, to))
+
+    dma("Y", ap(r("w")), T.wt[:, :], "dwt", [], [r("w")])
+    dma("Y", ap(r("si")), T.stk[:, :], "dstk", [], [r("si")])
+    dma("S", ap(r("bl", 0, 4096)), T.ball[:, :], "dball", [], [r("bl", 0, 4096)])
+
+    iota(r("ci"), [[0, 1]], 0, 1)
+    iota(r("rA"), [[0, 8], [1, 16]])
+    iota(r("rG"), [[1, 8], [0, 16]])
+    iota(r("rP"), [[1, 144]])
+    iota(r("r8"), [[1, 8]])
+    iota(r("r256"), [[256, 8]])
+    iota(r("a16"), [[0, 8], [16, 16]], 15)
+    iota(r("iw"), [[16, 32]])
+    iota(r("il"), [[0, 4], [256, 8]])
+    iota(r("rr"), [[0, 2], [1, 32]])
+    iota(r("dd16"), [[0, 128], [1, 16]])
+    iota(r("hi"), [[256, 2], [0, 256]])
+    iota(r("lo"), [[0, 2], [1, 256]])
+    iota(r("LN"), [[1, 512]], 32)
+    iota(r("DF"), [[1, 64]], 544)
+    ms(r("ones"), 1.0)
+    ms(r("y", 512, 576), 0.0)
+    ms(r("Rr", 512, 576), 0.0)
+    ts(r("cgi"), r("ci"), 4, OP.arith_shift_right)
+    ts(r("cai"), r("ci"), 15, OP.bitwise_and)
+    cp(r("cG"), r("cgi"))
+    cp(r("cA"), r("cai"))
+    cp(r("cP"), r("ci"))
+    ts(r("BO"), r("rG"), r("cG"), OP.is_equal)
+    cp(r("BOf"), r("BO"))
+    ts(r("M16"), r("rA"), r("cA"), OP.is_equal)
+    tt(r("ID"), r("BO"), r("M16"), OP.mult)
+    cp(r("IDf"), r("ID"))
+    ts(r("dh"), r("cA"), 0.5, OP.mult)
+    ts(r("dm"), r("cA"), 1.0, OP.is_ge)
+    ts(r("c15"), r("cG"), 16.0, OP.mult, 15.0, OP.add)
+    ts(r("z0"), r("cA"), 0.0, OP.is_equal)
+    ts(r("W"), r("rP"), r("c15"), OP.is_equal)
+    ts(r("SHf"), r("rP", 1, 129), r("cP"), OP.is_equal, r("dm"), OP.mult)
+    ts(r("SHn"), r("SHf"), -1.0, OP.mult)
+    tt(r("SHI"), r("SHf"), r("ID"), OP.subtract)
+    ts(r("BC0"), r("BO"), r("z0"), OP.mult, 2.0, OP.mult)
+    ts(r("BCn"), r("BC0"), -1024.0, OP.mult)
+    ts(r("TRI"), r("rA"), r("cA"), OP.is_ge, r("dm"), OP.mult)
+    ts(r("TRI"), r("TRI"), 0.5, OP.mult)
+    tt(r("TRI"), r("TRI"), r("BO"), OP.mult)
+    ts(r("UP"), r("rA"), r("cA"), OP.is_lt, -1.0, OP.mult)
+    tt(r("UP"), r("UP"), r("BO"), OP.mult)
+    ts(r("DBn"), r("r8"), r("cG"), OP.is_equal, -1.0, OP.mult)
+    ts(r("DBf"), r("r8"), r("cG"), OP.is_equal)
+    ts(r("lt15"), r("rA"), 15.0, OP.is_lt)
+    ts(r("e15"), r("rA"), 15.0, OP.is_equal)
+    ts(r("R16"), r("rA"), 1.0, OP.is_ge)
+    ts(r("RR"), r("rr"), 1.0, OP.is_ge)
+    ts(r("iw"), r("iw"), r("cA"), OP.add)
+    ts(r("c16"), r("cA"), 16.0, OP.mult)
+    ts(r("il"), r("il"), r("c16"), OP.add)
+    ts(r("il8"), r("il"), 8.0, OP.add)
+    ts(r("ix"), r("iw"), 1024.0, OP.add)
+    ts(r("cpos", 0, 32), r("iw"), -1.0, OP.mult, -1025.0, OP.add)
+    ts(r("cpos", 32, 64), r("iw"), -1.0, OP.mult, -513.0, OP.add)
+    ts(r("nd"), r("iw", 0, 4), 4096.0, OP.add)
+    cp(r("off"), r("si"))
+    ts(r("wi"), r("w"), 4.0, OP.add)
+    ts(r("wi"), r("wi"), 7, OP.bitwise_and)
+    ts(r("wf"), r("wi"), -4.0, OP.add, 512.0, OP.mult)
+    ts(r("WS"), r("BO"), r("wf"), OP.mult)
+    ts(r("RM"), r("dd16"), 2.0, OP.is_ge)
+
+    def bank(n, a=0, b=512):
+        return r("b%d" % n, a, b)
+
+    def one(name, n):
+        return r(name, 0, n, 1, 1)
+
+    def gat(q, a, b):
+        if b > a:
+            gather(q, r("P", 16 * a, 16 * b), r("bl", 0, 4096), r("off", a, b))
+
+    def cn(c, k):
+        return bank(2 + c % 2, 128 * k, 128 * k + 128)
+
+    def col(c, n=128):
+        return n * c, n * c + n
+
+    def xcopy(p):
+        a, b = PIECE[p]
+        mm(bank(p % 2, 0, b - a), r("ID"), r("P", 16 * a, 16 * b, 16))
+
+    def comp(p):
+        a, b = PIECE[p]
+        c, n = a // 128, b - a
+        for d in range(1, 16):
+            k = 1920 * (c % 2) + 128 * (d - 1) + a % 128
+            tt(r("C", k, k + n), r("P", 16 * a + d, 16 * b, 16), bank(p % 2, 0, n), OP.is_lt)
+            mm(bank(2 + c % 2, a % 128, a % 128 + n), r("W", 15 - d, 143 - d), r("C", k, k + n), d == 1, d == 15)
+
+    def pmax(c):
+        a, b = col(c, 2048)
+        scan(r("PM", a, b), r("RM"), r("P", a, b), OP.mult, OP.max)
+        iota(r("PM", a, b, 16), [[0, 128]], 255)
+
+    def vote(c):
+        act(r("sg", *col(c)), cn(c, 0), ACT.Sign, bias=8.5, scale=-1.0)
+
+    def tri(c):
+        mm(cn(c, 1), r("TRI"), r("sg", *col(c)))
+
+    def over(c):
+        act(r("nX", *col(c)), cn(c, 1), ACT.Sign, bias=r("dh"), acc=r("acc", c, c + 1))
+
+    def kexp(c):
+        mm(bank(4, *col(c % 2)), r("nX", *col(c)), r("BO"))
+
+    def kmask(c):
+        tt(r("km", *col(c)), bank(4, *col(c % 2)), r("M16"), OP.mult)
+        o = bank(5, *col(c, 8))
+        mm(o, one("ones", 128), one("r256", 8), True, False)
+        mm(o, one("a16", 128), one("ones", 8), False, False)
+        mm(o, r("km", *col(c)), r("DBn"), False, True)
+
+    def sel(c):
+        cp(r("lu", *col(c, 8)), bank(5, *col(c, 8)))
+        a, b = col(c, 2048)
+        win, offs, x, out = r("PM", a, b), r("lu", *col(c, 8)), r("P", a, b, 16), r("df", *col(c))
+        op("V", [win, offs, x], [out], lambda: g.vector.tensor_tensor(ap(out), ap(win).indirect(ap(offs)), ap(x), OP.subtract))
+
+    def yabs(c):
+        act(r("y", *col(c)), r("df", *col(c)), ACT.Abs)
+        mm(cn(c, 2 + c // 2), r("y", *col(c)), r("WS"))
+
+    def ymask(c):
+        tt(r("ym", *col(c)), cn(c, 2 + c // 2), r("M16"), OP.mult)
+        mm(bank(5, 192 + 8 * c, 200 + 8 * c), r("ym", *col(c)), r("DBf"))
+
+    for t in range(3):
+        last = t == 2
+        to, frm = T.cores[(rank + t + 1) % N], T.cores[(rank - t - 1) % N]
+        for name, sem in (("ry%d" % t, "aY%d" % t), ("rf%d" % t, "aF%d" % t)):
+            n = len(topo.engines(frm, core))
+            hist[name] = [(sem, sem, n, r(name), True)]
+            cnt[sem] = n
+        gat("V", 0, 32)
+        gat("S", 32, 64)
+        xcopy(0)
+        gat("S", 64, 128)
+        comp(0)
+        cp(r("o"), r("Ui" if t else "si"))
+        xcopy(1)
+        gat("S", VX, 192)
+        comp(1)
+        gat("V", 128, VX)
+        gat("S", 192, 256)
+        pmax(0)
+        vote(0)
+        xcopy(2)
+        tri(0)
+        mm(bank(7), r("SHf"), r("o"))
+        act(r("fl"), r("o"), ACT.Identity, bias=128.5005, scale=1.0 / 1024)
+        gat("S", 256, 320)
+        over(0)
+        comp(2)
+        kexp(0)
+        pmax(1)
+        gat("S", 320, 384)
+        xcopy(3)
+        mm(bank(6), r("BC0"), r("o"), True, False)
+        mm(bank(6), r("BCn"), r("fl"), False, True)
+        vote(1)
+        tri(1)
+        gat("S", 384, 448)
+        over(1)
+        kmask(0)
+        comp(3)
+        kexp(1)
+        pmax(2)
+        sel(0)
+        kmask(1)
+        gat("S", 448, 512)
+        xcopy(4)
+        vote(2)
+        tri(2)
+        over(2)
+        yabs(0)
+        act(r("E2"), bank(6), ACT.Identity, bias=float(2048 * 129 + 1))
+        act(r("IDb", 0, 64), r("DF"), ACT.Silu)
+        act(r("IDb", 512, 576), r("DF"), ACT.Silu)
+        comp(4)
+        kexp(2)
+        vote(3)
+        tri(3)
+        over(3)
+        sel(1)
+        tt(r("T1"), bank(7), r("E2"), OP.mult)
+        kmask(2)
+        kexp(3)
+        yabs(1)
+        sel(2)
+        kmask(3)
+        yabs(2)
+        tt(r("FZ", 0, 32), bank(5, 0, 32), r("il8"), OP.is_ge)
+        tt(r("FZ", 32, 64), bank(5, 0, 32), r("il"), OP.is_equal)
+        ts(r("q"), r("T1"), 4, OP.arith_shift_right)
+        mm(bank(4, 256, 320), r("BO"), r("FZ"))
+        mm(bank(4, 320, 384), r("IDf"), r("cpos"), True, False)
+        mm(bank(4, 320, 384), r("UP"), r("FZ"), False, True)
+        for c in range(4):
+            mm(bank(5, 64, 65), r("BOf"), r("acc", c, c + 1), c == 0, c == 3)
+        scan(r("sc"), r("RR"), bank(4, 256, 320), OP.mult, OP.add)
+        tt(r("ri"), r("sc"), bank(4, 320, 384), OP.add)
+        tt(r("tm"), r("ri"), r("FZ"), OP.mult)
+        tt(r("po"), r("tm", 0, 32), r("tm", 32, 64), OP.add)
+        tt(r("po"), r("po"), r("ix"), OP.add)
+        cp(r("pu"), r("po"))
+        op("S", [r("LN"), r("pu")], [r("IDb")],
+           lambda: g.scalar.activation(ap(r("IDb")).indirect(ap(r("pu"))), ap(r("LN")), ACT.Silu))
+        pmax(3)
+        ts(r("tf%d" % t), r("iw", 0, 4), r("sc", 31, 32), OP.is_ge, 8192.0, OP.mult)
+        send(r("tf%d" % t), "rf%d" % t, to, "aF%d" % t)
+        ts(r("zf"), r("iw", 0, 4), r("sc", 63, 64), OP.is_ge, 8192.0, OP.mult)
+        ts(r("A"), bank(5, 64, 65), -1.0, OP.mult, 7680.0, OP.add)
+        ts(r("A5"), bank(5, 64, 65), -512.0, OP.mult, 512.0 * 7680.0, OP.add)
+        ts(r("iwA"), r("iw"), r("A5"), OP.add)
+        sel(3)
+        mm(bank(7), r("ID"), r("nX"))
+        mm(bank(6), r("SHn"), r("nX"), True, False)
+        mm(bank(6), one("lt15", 128), one("ones", 512), False, True)
+        mm(bank(1), one("ones", 128), one("hi", 512), True, False)
+        mm(bank(1), one("ones", 128), one("lo", 512), False, False)
+        yabs(3)
+        mm(bank(1), r("WS"), r("y", 0, 512), False, True)
+        act(r("Rr", 0, 512), bank(1), ACT.Identity, bias=r("A5"))
+        ts(r("qA"), r("q"), r("A"), OP.add)
+        tt(bank(7), bank(7), r("o"), OP.mult)
+        tt(r("Xn"), bank(6), r("qA"), OP.mult)
+        for c in range(4):
+            ymask(c)
+        mm(bank(0), r("SHI"), r("nX"), True, False)
+        mm(bank(0), one("e15", 128), one("ones", 512), False, True)
+        tt(r("vi"), bank(5, 192, 224), r("iwA"), OP.add)
+        tt(r("idm", 0, 64), r("IDb", 0, 64), r("M16", 0, 64), OP.mult)
+        scan(r("ids", 0, 64), r("R16", 0, 64), r("idm", 0, 64), OP.mult, OP.add)
+        ts(r("idu", 0, 4), r("ids", 15, 64, 16), -31.75, OP.add)
+        gather("S", r("ty%d" % t), r("y"), r("idu", 0, 4))
+        send(r("ty%d" % t), "ry%d" % t, to, "aY%d" % t)
+        ts(r("vi"), r("vi"), 4095, OP.bitwise_and)
+        cp(r("vu"), r("vi"))
+        tt(bank(7), bank(7), r("Xn"), OP.add)
+        tt(r("tt"), bank(0), r("Rr", 0, 512), OP.mult)
+        tt(r("idm", 64, 128), r("IDb", 512, 576), r("M16", 0, 64), OP.mult)
+        scan(r("ids", 64, 128), r("R16", 64, 128), r("idm", 64, 128), OP.mult, OP.add)
+        ts(r("idv", 0, 4), r("ids", 79, 128, 16), -31.75, OP.add)
+        gather("S", r("Rz"), r("Rr"), r("idv", 0, 4))
+        tt(r("Ui"), bank(7), r("tt"), OP.add)
+        ts(r("Ui"), r("Ui"), 4095, OP.bitwise_and)
+        if last:
+            cp(r("o"), r("Ui"))
+            dma("Y", T.yo[:, :], ap(r("o")), "dyo", [r("o")], [])
+        else:
+            cp(r("off"), r("Ui"))
+        scatter(r("bl", 0, 4096), r("vu"), r("y", 0, 512))
+        tt(r("zm"), r("Rz"), r("M16", 0, 64), OP.mult)
+        scan(r("zs"), r("R16", 0, 64), r("zm"), OP.mult, OP.add)
+        cp(r("zi"), r("zs", 15, 64, 16))
+        ts(r("zi"), r("zi"), 4095, OP.bitwise_and)
+        tt(r("cb"), r("zf"), r("rf%d" % t), OP.max)
+        tt(r("cc"), r("cb"), r("nd"), OP.min)
+        tt(r("zo"), r("zi"), r("cc"), OP.max)
+        cp(r("zu"), r("zo"))
+        scatter(r("bl"), r("zu"), r("ry%d" % t))
+    dma("Y", T.yb[:, :], ap(r("bl", 0, 1024)), "dyb", [r("bl", 0, 1024)], [])
+    for sem in cnt:
+        need("Y", sem, cnt[sem])

@@ -1,4 +1,4 @@
-from concourse.mybir import AluOpType, ActivationFunctionType
+from concourse.mybir import AluOpType, ActivationFunctionType, AxisListType
 
 F, B, I, U = "float32", "bfloat16", "int32", "uint16"
 
@@ -9,29 +9,26 @@ def sb(n, d):
 
 SCRATCH = {
     "bl": sb(4160, B), "P": sb(8192, B), "PM": sb(8192, B), "C": sb(3840, B),
-    "si": sb(512, I), "off": sb(512, U), "o": sb(512, F), "w": sb(1, B),
-    "ci": sb(1, I), "cgi": sb(1, I), "cai": sb(1, I), "cG": sb(1, F), "cA": sb(1, F), "cP": sb(1, F), "dh": sb(1, F), "dm": sb(1, F),
-    "c15": sb(1, F), "c16": sb(1, F), "z0": sb(1, F), "wi": sb(1, I), "wf": sb(1, F),
-    "rG": sb(128, B), "rA": sb(128, B), "rP": sb(144, F), "r8": sb(8, B), "dd16": sb(2048, B),
-    "BO": sb(128, B), "BOf": sb(128, F), "M16": sb(128, B), "ID": sb(128, B), "IDf": sb(128, F), "TRI": sb(128, B),
-    "UP": sb(128, B), "W": sb(144, B), "SHf": sb(128, F), "SHn": sb(128, B), "SHI": sb(128, B), "BC0": sb(128, F),
-    "BCn": sb(128, B), "WS": sb(128, B), "DBn": sb(8, B), "DBf": sb(8, F), "RM": sb(2048, B), "R16": sb(128, B), "RR": sb(64, B),
-    "ones": sb(512, B), "hi": sb(512, B), "lo": sb(512, B), "r256": sb(8, B), "a16": sb(128, B), "lt15": sb(128, B), "e15": sb(128, B),
-    "iw": sb(32, F), "il": sb(32, F), "il8": sb(32, F), "ix": sb(32, F), "cpos": sb(64, F), "nd": sb(4, F), "LN": sb(512, F),
-    "DF": sb(64, F), "rr": sb(64, F),
-    "fl": sb(512, B), "E2": sb(512, F), "T1": sb(512, I), "q": sb(512, I), "qA": sb(512, F), "Xn": sb(512, F), "tt": sb(512, F),
-    "Ui": sb(512, I), "sg": sb(512, B), "nX": sb(512, B), "acc": sb(4, F), "km": sb(512, B), "lu": sb(32, U),
-    "df": sb(512, B), "y": sb(576, B), "ym": sb(512, F), "Rr": sb(576, F), "A": sb(1, F), "A5": sb(1, F), "FZ": sb(64, B),
-    "sc": sb(64, F), "ri": sb(64, F), "tm": sb(64, F), "po": sb(32, F), "pu": sb(32, U), "IDb": sb(1536, F),
-    "idm": sb(128, F), "ids": sb(128, F), "idu": sb(4, U), "idv": sb(4, U), "iwA": sb(32, F), "vi": sb(32, I),
-    "vu": sb(32, U), "zf": sb(4, F), "cb": sb(4, F), "cc": sb(4, F), "Rz": sb(64, F), "zm": sb(64, F), "zs": sb(64, F), "zi": sb(4, I),
-    "zo": sb(4, F), "zu": sb(4, U),
+    "Ui": sb(512, I), "off": sb(512, U), "o": sb(512, F), "w": sb(1, B),
+    "cP": sb(1, F), "cQ": sb(1, F), "cG": sb(1, B), "cA": sb(1, F), "c15": sb(1, F), "z": sb(3, F), "dm": sb(1, F), "wi": sb(1, I),
+    "wf": sb(1, F), "bo": sb(1, F), "fs": sb(1, F), "fb": sb(1, F), "s2": sb(1, F), "u": sb(16, F),
+    "rG": sb(128, B), "rA": sb(128, B), "rP": sb(144, B), "r8": sb(8, B), "ones": sb(128, B),
+    "BO": sb(128, B), "BOf": sb(128, F), "BOd": sb(128, B), "BOm": sb(128, B), "M16": sb(128, B), "MN": sb(128, B), "DB": sb(8, B),
+    "ID": sb(128, B), "ID8": sb(128, F), "TRI": sb(128, B), "UP": sb(128, B), "UPz": sb(128, B), "W": sb(144, B), "Wk": sb(144, B),
+    "Ww": sb(144, B), "SH": sb(128, B), "SHf": sb(128, F), "BC0": sb(128, F), "BCn": sb(128, B), "WS": sb(128, B), "MA": sb(128, B),
+    "MB": sb(128, B), "km": sb(128, B), "m": sb(1024, B), "RM": sb(2048, B), "R16": sb(64, B), "RR": sb(80, B),
+    "hA": sb(512, B), "hB": sb(512, B), "hW": sb(32, B), "r256": sb(32, B), "a16": sb(128, B),
+    "il": sb(32, F), "il8": sb(32, F), "nb": sb(4, F), "nd": sb(4, F), "nr": sb(64, F), "nh": sb(64, F),
+    "fl": sb(512, B), "T1": sb(512, F), "s1": sb(512, F), "sg": sb(512, B), "X": sb(512, B), "acc": sb(8, F), "ac": sb(1, F),
+    "LA": sb(128, B), "lu": sb(32, U), "df": sb(512, B), "y": sb(576, B), "FZ": sb(80, B), "sc": sb(80, F), "ri": sb(80, F),
+    "jk": sb(32, B), "cb": sb(8, F), "cu": sb(4, U), "cz": sb(4, U), "ind": sb(64, B), "idu": sb(4, U), "vi": sb(40, I), "vu": sb(32, U),
+    "iz": sb(64, B), "vz": sb(64, F), "zm": sb(64, F), "zs": sb(64, F), "zo": sb(4, F), "zu": sb(4, U),
 }
 for _t in range(3):
     SCRATCH["ty%d" % _t] = sb(64, B)
     SCRATCH["ry%d" % _t] = sb(64, B)
-    SCRATCH["tf%d" % _t] = sb(4, F)
-    SCRATCH["rf%d" % _t] = sb(4, F)
+    SCRATCH["tf%d" % _t] = sb(64, B)
+    SCRATCH["rf%d" % _t] = sb(64, B)
 for _b in range(8):
     SCRATCH["b%d" % _b] = ("psum", [128, 512], F)
 
@@ -39,8 +36,11 @@ SEMAPHORES = ["sV", "sS", "sP", "sG", "dstk", "dball", "dwt", "dyo", "dyb", "loc
 for _t in range(3):
     SEMAPHORES += ["aY%d" % _t, "aF%d" % _t]
 
-PIECE = [(0, 64), (64, 128), (128, 256), (256, 384), (384, 512)]
-VX = 160
+CH = [(0, 64), (64, 192), (192, 320), (320, 448), (448, 512)]
+L1 = CH[-1][0]
+VG = [[32, 32, 16, 0, 0], [0, 32, 16, 0, 0], [0, 32, 16, 0, 0]]
+VD = [(1, 4), (2, 4), (3, 4), (4, 8), (8, 16)]
+S0 = 128
 
 
 def rank_program(g, core, T, topo):
@@ -53,15 +53,16 @@ def rank_program(g, core, T, topo):
     cnt = {}
     known = {q: {} for q in eng}
     clk = {}
+    part = [False]
     hist = {}
 
-    def r(name, a=0, b=None, s=1, n=128):
-        return (name, a, SCRATCH[name][1][1] if b is None else b, s, n)
+    def r(name, a=0, b=None, s=1, n=128, p=0):
+        return (name, a, SCRATCH[name][1][1] if b is None else b, s, n, p)
 
     def ap(x):
         t = T[x[0]]
         if x[3] == 1:
-            return t[:, x[1]:x[2]] if x[4] == 128 else t[0:x[4], x[1]:x[2]]
+            return t[:, x[1]:x[2]] if x[4] == 128 else t[x[5]:x[5] + x[4], x[1]:x[2]]
         return t[:, x[1]:x[2]:x[3]]
 
     def meet(x, y):
@@ -72,7 +73,7 @@ def rank_program(g, core, T, topo):
         return True
 
     def inside(x, y):
-        return y[3] == 1 and y[1] <= x[1] and x[2] <= y[2]
+        return y[3] == 1 and y[4] == 128 and y[1] <= x[1] and x[2] <= y[2]
 
     def learn(q, sem, n):
         k = known[q]
@@ -114,6 +115,10 @@ def rank_program(g, core, T, topo):
     def op(q, reads, writes, call, group=False):
         deps(q, reads, writes, group)
         sem = "s" + q
+        if q == "G":
+            if part[0] or writes[0][4] < 128:
+                need(q, sem, cnt.get(sem, 0))
+            part[0] = writes[0][4] < 128
         cnt[sem] = cnt.get(sem, 0) + 1
         call().then_inc(T.sem[sem], 1)
         note(q, sem, cnt[sem], reads, writes)
@@ -143,6 +148,9 @@ def rank_program(g, core, T, topo):
     def scan(out, d0, d1, o0, o1):
         op("V", [d0, d1], [out], lambda: g.vector.tensor_tensor_scan(ap(out), ap(d0), ap(d1), 0.0, o0, o1))
 
+    def rowsum(out, a):
+        op("V", [a], [out], lambda: g.vector.tensor_reduce(ap(out), ap(a), AxisListType.X, OP.add))
+
     def act(out, a, f, bias=0.0, scale=1.0, acc=None):
         rd = [a] + [x for x in (bias, scale) if isr(x)]
         if acc is None:
@@ -150,20 +158,26 @@ def rank_program(g, core, T, topo):
         else:
             op("S", rd, [out, acc], lambda: g.scalar.activation(ap(out), ap(a), f, bias=val(bias), scale=val(scale), accum_out=ap(acc)))
 
+    def lin(out, a, scale=1.0, bias=0.0):
+        act(out, a, ACT.Identity, bias=bias, scale=scale)
+
     def mm(out, l, rhs, start=True, stop=True):
         op("P", [l, rhs], [out], lambda: g.tensor.matmul(ap(out), ap(l), ap(rhs), start, stop), group=not start)
 
     def iota(out, pat, base=0, cm=0):
-        if SCRATCH[out[0]][2] == I:
-            op("G", [], [out], lambda: g.iota(ap(out), pat, base, cm))
-        else:
-            op("G", [], [out], lambda: g.iota(ap(out), pat, base, cm, allow_small_or_imprecise_dtypes=True))
+        op("G", [], [out], lambda: g.iota(ap(out), pat, base, cm, allow_small_or_imprecise_dtypes=True))
+
+    def keep(out, a, cmp, fill, sign):
+        op("G", [a], [out], lambda: g.affine_select(ap(out), ap(a), [[sign, 128]], cmp, fill, 0, -sign))
 
     def gather(q, out, win, offs):
         if q == "V":
             op("V", [win, offs], [out], lambda: g.vector.tensor_copy(ap(out), ap(win).indirect(ap(offs))))
         else:
             op("S", [win, offs], [out], lambda: g.scalar.activation(ap(out), ap(win).indirect(ap(offs)), ACT.Copy))
+
+    def gtt(out, win, offs, b, o):
+        op("V", [win, offs, b], [out], lambda: g.vector.tensor_tensor(ap(out), ap(win).indirect(ap(offs)), ap(b), o))
 
     def scatter(win, offs, a):
         op("V", [a, offs], [win], lambda: g.vector.tensor_copy(ap(win).indirect(ap(offs)), ap(a)))
@@ -186,139 +200,220 @@ def rank_program(g, core, T, topo):
         g.remote_dma(ap((dst_buf,) + src[1:]), ap(src), T.sem[sem], T.sem["loc"], pid, rid, topo.mask(core, to))
         cnt["loc"] = cnt.get("loc", 0) + len(topo.engines(core, to))
 
-    dma("Y", ap(r("w")), T.wt[:, :], "dwt", [], [r("w")])
-    dma("Y", ap(r("si")), T.stk[:, :], "dstk", [], [r("si")])
-    dma("S", ap(r("bl", 0, 4096)), T.ball[:, :], "dball", [], [r("bl", 0, 4096)])
-
-    iota(r("ci"), [[0, 1]], 0, 1)
-    iota(r("rA"), [[0, 8], [1, 16]])
-    iota(r("rG"), [[1, 8], [0, 16]])
-    iota(r("rP"), [[1, 144]])
-    iota(r("r8"), [[1, 8]])
-    iota(r("r256"), [[256, 8]])
-    iota(r("a16"), [[0, 8], [16, 16]], 15)
-    iota(r("iw"), [[16, 32]])
-    iota(r("il"), [[0, 4], [256, 8]])
-    iota(r("rr"), [[0, 2], [1, 32]])
-    iota(r("dd16"), [[0, 128], [1, 16]])
-    iota(r("hi"), [[256, 2], [0, 256]])
-    iota(r("lo"), [[0, 2], [1, 256]])
-    iota(r("LN"), [[1, 512]], 32)
-    iota(r("DF"), [[1, 64]], 544)
-    ms(r("ones"), 1.0)
-    ms(r("y", 512, 576), 0.0)
-    ms(r("Rr", 512, 576), 0.0)
-    ts(r("cgi"), r("ci"), 4, OP.arith_shift_right)
-    ts(r("cai"), r("ci"), 15, OP.bitwise_and)
-    cp(r("cG"), r("cgi"))
-    cp(r("cA"), r("cai"))
-    cp(r("cP"), r("ci"))
-    ts(r("BO"), r("rG"), r("cG"), OP.is_equal)
-    cp(r("BOf"), r("BO"))
-    ts(r("M16"), r("rA"), r("cA"), OP.is_equal)
-    tt(r("ID"), r("BO"), r("M16"), OP.mult)
-    cp(r("IDf"), r("ID"))
-    ts(r("dh"), r("cA"), 0.5, OP.mult)
-    ts(r("dm"), r("cA"), 1.0, OP.is_ge)
-    ts(r("c15"), r("cG"), 16.0, OP.mult, 15.0, OP.add)
-    ts(r("z0"), r("cA"), 0.0, OP.is_equal)
-    ts(r("W"), r("rP"), r("c15"), OP.is_equal)
-    ts(r("SHf"), r("rP", 1, 129), r("cP"), OP.is_equal, r("dm"), OP.mult)
-    ts(r("SHn"), r("SHf"), -1.0, OP.mult)
-    tt(r("SHI"), r("SHf"), r("ID"), OP.subtract)
-    ts(r("BC0"), r("BO"), r("z0"), OP.mult, 2.0, OP.mult)
-    ts(r("BCn"), r("BC0"), -1024.0, OP.mult)
-    ts(r("TRI"), r("rA"), r("cA"), OP.is_ge, r("dm"), OP.mult)
-    ts(r("TRI"), r("TRI"), 0.5, OP.mult)
-    tt(r("TRI"), r("TRI"), r("BO"), OP.mult)
-    ts(r("UP"), r("rA"), r("cA"), OP.is_lt, -1.0, OP.mult)
-    tt(r("UP"), r("UP"), r("BO"), OP.mult)
-    ts(r("DBn"), r("r8"), r("cG"), OP.is_equal, -1.0, OP.mult)
-    ts(r("DBf"), r("r8"), r("cG"), OP.is_equal)
-    ts(r("lt15"), r("rA"), 15.0, OP.is_lt)
-    ts(r("e15"), r("rA"), 15.0, OP.is_equal)
-    ts(r("R16"), r("rA"), 1.0, OP.is_ge)
-    ts(r("RR"), r("rr"), 1.0, OP.is_ge)
-    ts(r("iw"), r("iw"), r("cA"), OP.add)
-    ts(r("c16"), r("cA"), 16.0, OP.mult)
-    ts(r("il"), r("il"), r("c16"), OP.add)
-    ts(r("il8"), r("il"), 8.0, OP.add)
-    ts(r("ix"), r("iw"), 1024.0, OP.add)
-    ts(r("cpos", 0, 32), r("iw"), -1.0, OP.mult, -1025.0, OP.add)
-    ts(r("cpos", 32, 64), r("iw"), -1.0, OP.mult, -513.0, OP.add)
-    ts(r("nd"), r("iw", 0, 4), 4096.0, OP.add)
-    cp(r("off"), r("si"))
-    ts(r("wi"), r("w"), 4.0, OP.add)
-    ts(r("wi"), r("wi"), 7, OP.bitwise_and)
-    ts(r("wf"), r("wi"), -4.0, OP.add, 512.0, OP.mult)
-    ts(r("WS"), r("BO"), r("wf"), OP.mult)
-    ts(r("RM"), r("dd16"), 2.0, OP.is_ge)
-
-    def bank(n, a=0, b=512):
-        return r("b%d" % n, a, b)
+    def bank(n, a=0, b=512, s=1, k=128):
+        return r("b%d" % n, a, b, s, k)
 
     def one(name, n):
         return r(name, 0, n, 1, 1)
+
+    dma("Y", ap(r("Ui")), T.stk[:, :], "dstk", [], [r("Ui")])
+    dma("S", ap(r("bl", 0, 4096)), T.ball[:, :], "dball", [], [r("bl", 0, 4096)])
+    dma("Y", ap(r("w")), T.wt[:, :], "dwt", [], [r("w")])
+
+    c1 = L1 // 16
+    U16, BIG = 65536.0, 1048576.0
+
+    def u(j):
+        return r("u", j, j + 1)
+
+    def z(j):
+        return r("z", j, j + 1)
+
+    def m(j):
+        return r("m", 128 * j, 128 * j + 128)
+
+    def row(name, p):
+        return r(name, 0, None, 1, 1, p)
+
+    def total(out, n, parts):
+        for j, x in enumerate(parts):
+            mm(bank(n, 0, 128), r("ID"), x, j == 0, j == len(parts) - 1)
+        lin(out, bank(n, 0, 128))
+
+    iota(r("cP"), [[0, 1]], 0, 1)
+    iota(r("cQ"), [[0, 1]], 2064, 1)
+    iota(r("rA"), [[0, 8], [1, 16]])
+    iota(r("rP"), [[1, 144]])
+    iota(r("rG"), [[1, 8], [0, 16]], 129)
+    iota(r("r256", 0, c1), [[256, c1]])
+    iota(r("r256", c1, 32), [[256, 32 - c1]])
+    iota(r("r8"), [[1, 8]], 129)
+    iota(r("nb"), [[16, 4]])
+    iota(r("nr"), [[1, 64]])
+    iota(r("a16"), [[0, 8], [16, 16]])
+    ms(r("ones"), 1.0)
+    ms(r("RM"), 1.0)
+    ts(r("cG"), r("cP"), 0.0625, OP.mult, 129.0 - 15.0 / 32, OP.add)
+    ms(r("RM", 0, 2048, 16), 0.0)
+    ts(r("cA"), r("cG"), -16.0, OP.mult, r("cQ"), OP.add)
+    ts(r("c15"), r("cG"), 16.0, OP.mult, 15.0 - 2064, OP.add)
+    ms(r("RM", 1, 2048, 16), 0.0)
+    ts(r("z"), r("rA", 0, 3), r("cA"), OP.is_equal)
+    ts(r("dm"), r("cA"), 1.0, OP.is_ge)
+    ts(u(0), r("cA"), 1.0, OP.is_le)
+    ts(u(1), r("cA"), 2.0, OP.is_ge, -192 * U16, OP.mult)
+    ts(u(2), r("cA"), 1.0, OP.is_ge, -0.5, OP.mult)
+    ts(u(3), r("cA"), 1.0, OP.is_le, -BIG, OP.mult)
+    ts(r("ID"), r("rP", 0, 128), r("cP"), OP.is_equal)
+    ts(r("SH"), r("rP", 1, 129), r("cP"), OP.is_equal, r("dm"), OP.mult)
+    ts(r("BO"), r("rG"), r("cG"), OP.is_equal)
+    ts(r("W"), r("rP"), r("c15"), OP.is_equal)
+    ts(r("M16"), r("rA"), r("cA"), OP.is_equal)
+    ts(r("wi"), r("w"), 4.0, OP.add)
+    ms(r("y", 512, 576), 0.0)
+    ts(r("wi"), r("wi"), 7, OP.bitwise_and)
+    ms(r("FZ"), 0.0)
+    ts(r("wf"), r("wi"), -4.0, OP.add, 512.0, OP.mult)
+    ms(r("vi"), 0)
+    lin(m(0), r("BO"), u(2))
+    lin(m(1), r("BO"), -1.0)
+    keep(m(0), m(0), OP.is_ge, 0.0, 1)
+    keep(r("UP"), m(1), OP.is_gt, 0.0, -1)
+    keep(r("UPz"), r("UP"), OP.not_equal, 32.0, 1)
+    lin(r("WS"), r("BO"), r("wf"))
+    mm(bank(7, 0, 1), r("WS"), r("ones", 0, 1))
+    cp(r("off"), r("Ui"))
+    ts(r("o"), r("Ui"), -16384.0, OP.add)
+    ts(u(4), bank(7, 0, 1), -128.0, OP.mult, -96 * U16, OP.add)
+    ms(r("acc"), 0.0)
+    ms(r("RR"), 1.0)
+    ms(r("s2"), 0.0)
+    tt(u(4), u(4), u(0), OP.mult)
+    ms(r("acc", 7, 8), -256.0)
+    ms(r("RR", 0, 80, 40), 0.0)
+    ms(row("s2", 0), 1.0 / 32)
+    ms(row("s2", 32), 1.0)
+    ts(u(5), r("cA"), 16.0, OP.mult)
+    ts(r("MN"), r("M16"), 64.0, OP.mult, -64.0, OP.add)
+    ts(r("il"), r("r256"), u(5), OP.add)
+    ts(r("il8"), r("r256"), u(5), OP.add, 8.0, OP.add)
+    ts(r("DB"), r("r8"), r("cG"), OP.is_equal)
+    ts(r("R16"), r("rA", 0, 64), 1.0, OP.is_ge)
+    ts(r("nd"), r("nb"), r("cA"), OP.add, -4096.0, OP.add)
+    ts(r("nb"), r("nb"), r("cA"), OP.add, 0.5, OP.add)
+    ts(m(2), r("ID"), 192 * U16, OP.mult)
+    ts(m(3), r("SH"), BIG, OP.mult)
+    ts(r("BOm"), r("BO"), -8192.0, OP.mult)
+    lin(r("fs"), z(0), 1.0 / 1024)
+    lin(u(6), z(0), 144.5005, z(2))
+    lin(u(7), z(0), 0.125)
+    lin(u(8), z(2), 0.0625)
+    lin(u(9), z(1), 0.5)
+    lin(u(10), r("cA"), -0.5, 1.0)
+    lin(r("fb"), z(1), 145.0, u(6))
+    lin(u(11), z(1), 128.0, u(8))
+    lin(r("bo"), z(0), -0.5, u(10))
+    lin(m(4), r("SH"), u(9))
+    lin(u(12), z(0), -128.0, u(11))
+    lin(r("BC0"), r("BO"), u(7))
+    lin(r("BCn"), r("BO"), u(12))
+    total(r("TRI"), 5, [m(0), m(4)])
+    lin(m(5), r("SH"), u(1))
+    lin(m(6), r("BO"), u(4))
+    lin(m(7), r("BO"), u(3))
+    lin(r("Wk"), r("W"), r("dm"))
+    lin(r("Ww"), r("W"), r("wf"))
+    total(r("MA"), 6, [m(2), m(5), m(6)])
+    total(r("MB"), 7, [m(3), m(7)])
+    lin(r("ID8"), r("ID"), 8.0)
+    lin(r("BOf"), r("BO"))
+    lin(r("BOd"), r("BO"), r("dm"))
+    lin(r("SHf"), r("SH"))
+    lin(r("nh"), r("nr"), 1.0, 0.5)
+    iota(r("hW"), [[0, 32]], 512)
+    iota(row("hW", 0), [[512, 32]])
+    iota(row("hW", 32), [[0, 32]])
+    iota(r("hA"), [[0, 512]], 512)
+    iota(row("hA", 0), [[8192, 2], [0, 256]])
+    iota(row("hA", 32), [[0, 2], [1, 256]])
+    iota(r("hB"), [[0, 512]], 1)
+    iota(row("hB", 0), [[0, 512]], -15)
+    iota(row("hB", 32), [[0, 512]], -4352)
 
     def gat(q, a, b):
         if b > a:
             gather(q, r("P", 16 * a, 16 * b), r("bl", 0, 4096), r("off", a, b))
 
-    def cn(c, k):
-        return bank(2 + c % 2, 128 * k, 128 * k + 128)
+    def wrap(out, name, src, a, b, js=range(16)):
+        for j in js:
+            mm(out, r(name, 15 - j, 143 - j), r(src, a + j, b, 16), False, j == 15)
 
-    def col(c, n=128):
-        return n * c, n * c + n
+    def xcopy(c):
+        a, b = CH[c]
+        for j in range(4):
+            mm(bank(c % 2, j, 4 * (b - a), 4), r("ID"), r("P", 16 * a, 16 * b, 16))
 
-    def xcopy(p):
-        a, b = PIECE[p]
-        mm(bank(p % 2, 0, b - a), r("ID"), r("P", 16 * a, 16 * b, 16))
+    def comp(c, d0, s):
+        a, b = CH[c]
+        n, k = b - a, 16 // s
+        at = 1920 * (c % 2) + (512 * (d0 - 1) if d0 < 8 else 1792)
+        tt(r("C", at, at + k * n), r("P", 16 * a + d0, 16 * b, s), bank(c % 2, 0, 4 * n, s // 4), OP.is_lt)
+        for j in range(k):
+            d = d0 + s * j
+            mm(bank(2 + c % 2, 0, n), r("W", 15 - d, 143 - d), r("C", at + j, at + k * n, k), d == VD[0][0], d == VD[-1][0])
 
-    def comp(p):
-        a, b = PIECE[p]
-        c, n = a // 128, b - a
-        for d in range(1, 16):
-            k = 1920 * (c % 2) + 128 * (d - 1) + a % 128
-            tt(r("C", k, k + n), r("P", 16 * a + d, 16 * b, 16), bank(p % 2, 0, n), OP.is_lt)
-            mm(bank(2 + c % 2, a % 128, a % 128 + n), r("W", 15 - d, 143 - d), r("C", k, k + n), d == 1, d == 15)
+    def comps(c, a=0, b=len(VD)):
+        for d0, s in VD[a:b]:
+            comp(c, d0, s)
 
     def pmax(c):
-        a, b = col(c, 2048)
-        scan(r("PM", a, b), r("RM"), r("P", a, b), OP.mult, OP.max)
-        iota(r("PM", a, b, 16), [[0, 128]], 255)
+        a, b = CH[c]
+        scan(r("PM", 16 * a, 16 * b), r("RM", 0, 16 * (b - a)), r("P", 16 * a, 16 * b), OP.mult, OP.max)
+        if b < 512:
+            iota(r("PM", 16 * a, 16 * b, 16), [[0, b - a]], 255)
+        else:
+            ms(r("PM", 16 * a, 16 * b, 16), 255.0)
 
     def vote(c):
-        act(r("sg", *col(c)), cn(c, 0), ACT.Sign, bias=8.5, scale=-1.0)
-
-    def tri(c):
-        mm(cn(c, 1), r("TRI"), r("sg", *col(c)))
+        a, b = CH[c]
+        act(r("sg", a, b), bank(2 + c % 2, 0, b - a), ACT.Sign, bias=8.5, scale=-1.0)
+        mm(bank(2 + c % 2, 128, 128 + b - a), r("TRI"), r("sg", a, b))
 
     def over(c):
-        act(r("nX", *col(c)), cn(c, 1), ACT.Sign, bias=r("dh"), acc=r("acc", c, c + 1))
+        a, b = CH[c]
+        act(r("X", a, b), bank(2 + c % 2, 128, 128 + b - a), ACT.Relu, bias=r("bo"), acc=r("acc", c, c + 1))
 
-    def kexp(c):
-        mm(bank(4, *col(c % 2)), r("nX", *col(c)), r("BO"))
+    def kconst(a, b):
+        o = bank(4, a // 16, b // 16)
+        mm(o, one("ones", 128), r("r256", a // 16, b // 16, 1, 1), True, False)
+        mm(o, one("a16", 128), one("ones", (b - a) // 16), False, False)
 
-    def kmask(c):
-        tt(r("km", *col(c)), bank(4, *col(c % 2)), r("M16"), OP.mult)
-        o = bank(5, *col(c, 8))
-        mm(o, one("ones", 128), one("r256", 8), True, False)
-        mm(o, one("a16", 128), one("ones", 8), False, False)
-        mm(o, r("km", *col(c)), r("DBn"), False, True)
+    def kwrap(a, b):
+        kconst(a, b)
+        wrap(bank(4, a // 16, b // 16), "Wk", "X", a, b)
 
-    def sel(c):
-        cp(r("lu", *col(c, 8)), bank(5, *col(c, 8)))
-        a, b = col(c, 2048)
-        win, offs, x, out = r("PM", a, b), r("lu", *col(c, 8)), r("P", a, b, 16), r("df", *col(c))
-        op("V", [win, offs, x], [out], lambda: g.vector.tensor_tensor(ap(out), ap(win).indirect(ap(offs)), ap(x), OP.subtract))
+    def kfast(a, b):
+        n = b - a
+        mm(bank(7, 0, 128, 1, n), r("ID", 0, n), r("MN"), True, False)
+        kconst(a, b)
+        mm(bank(7, 0, 128, 1, n), r("X", a, b), r("BOd"), False, True)
+        act(r("km", 0, 128, 1, n), bank(7, 0, 128, 1, n), ACT.Relu)
+        mm(bank(4, a // 16, b // 16), r("km", 0, 128, 1, n), r("DB", 0, n // 16, 1, n), False, True)
 
-    def yabs(c):
-        act(r("y", *col(c)), r("df", *col(c)), ACT.Abs)
-        mm(cn(c, 2 + c // 2), r("y", *col(c)), r("WS"))
+    def sel(a, b):
+        gtt(r("df", a, b), r("PM", 16 * a, 16 * b), r("lu", a // 16, b // 16), r("P", 16 * a, 16 * b, 16), OP.subtract)
 
-    def ymask(c):
-        tt(r("ym", *col(c)), cn(c, 2 + c // 2), r("M16"), OP.mult)
-        mm(bank(5, 192 + 8 * c, 200 + 8 * c), r("ym", *col(c)), r("DBf"))
+    def yabs(a, b):
+        act(r("y", a, b), r("df", a, b), ACT.Abs)
+
+    def stack_calls(a, b, last=False):
+        return [lambda: tt(r("s1", a, b), bank(5, a, b), r("o", a, b), OP.max),
+                lambda: tt(r("Ui", a, b), bank(6, a, b), r("s1", a, b), OP.max),
+                lambda: ts(r("Ui", a, b), r("Ui", a, b), 4095, OP.bitwise_and),
+                lambda: cp(r("o" if last else "off", a, b), r("Ui", a, b))]
+
+    def stacks(a, b, last=False):
+        for f in stack_calls(a, b, last):
+            f()
+
+    def eq(j):
+        a, b = 128 * j, 128 * j + 128
+        mm(bank(6, a, b), r("BCn"), r("fl", a, b), True, False)
+        mm(bank(6, a, b), r("BC0"), r("o", a, b), False, True)
+
+    def blocks(h):
+        for j in range(4):
+            act(r("jk"), r("sc", 40 * h, 40 * h + 32), ACT.Sign, bias=r("nb", j, j + 1), scale=-1.0, acc=r("cb", 4 * h + j, 4 * h + j + 1))
 
     for t in range(3):
         last = t == 2
@@ -327,134 +422,128 @@ def rank_program(g, core, T, topo):
             n = len(topo.engines(frm, core))
             hist[name] = [(sem, sem, n, r(name), True)]
             cnt[sem] = n
-        gat("V", 0, 32)
-        gat("S", 32, 64)
+
+        def sg1(c):
+            a, b = CH[c]
+            gat("S", a + VG[t][c], (a + b) // 2)
+
+        def sg2(c):
+            a, b = CH[c]
+            gat("S", (a + b) // 2, b)
+
+        def vg(c):
+            gat("V", CH[c][0], CH[c][0] + VG[t][c])
+
+        gat("S", VG[t][0], CH[0][1])
+        vg(0)
+        sg1(1)
+        if t:
+            stacks(S0, 512)
+            ts(r("o"), r("Ui"), -16384.0, OP.add)
         xcopy(0)
-        gat("S", 64, 128)
-        comp(0)
-        cp(r("o"), r("Ui" if t else "si"))
-        xcopy(1)
-        gat("S", VX, 192)
-        comp(1)
-        gat("V", 128, VX)
-        gat("S", 192, 256)
+        sg2(1)
+        comps(0)
+        vg(1)
         pmax(0)
+        xcopy(1)
         vote(0)
-        xcopy(2)
-        tri(0)
-        mm(bank(7), r("SHf"), r("o"))
-        act(r("fl"), r("o"), ACT.Identity, bias=128.5005, scale=1.0 / 1024)
-        gat("S", 256, 320)
+        act(r("fl"), r("o"), ACT.Identity, bias=r("fb"), scale=r("fs"))
+        sg1(2)
         over(0)
-        comp(2)
-        kexp(0)
+        sg2(2)
+        comps(1)
+        eq(0)
+        eq(1)
+        vg(2)
         pmax(1)
-        gat("S", 320, 384)
-        xcopy(3)
-        mm(bank(6), r("BC0"), r("o"), True, False)
-        mm(bank(6), r("BCn"), r("fl"), False, True)
+        xcopy(2)
         vote(1)
-        tri(1)
-        gat("S", 384, 448)
+        sg1(3)
         over(1)
-        kmask(0)
-        comp(3)
-        kexp(1)
+        sg2(3)
+        comps(2)
+        eq(2)
+        eq(3)
+        vg(3)
         pmax(2)
-        sel(0)
-        kmask(1)
-        gat("S", 448, 512)
-        xcopy(4)
+        xcopy(3)
         vote(2)
-        tri(2)
+        gat("S", L1, 512)
         over(2)
-        yabs(0)
-        act(r("E2"), bank(6), ACT.Identity, bias=float(2048 * 129 + 1))
-        act(r("IDb", 0, 64), r("DF"), ACT.Silu)
-        act(r("IDb", 512, 576), r("DF"), ACT.Silu)
-        comp(4)
-        kexp(2)
+        comps(3, 0, 2)
+        xcopy(4)
+        comps(3, 2)
         vote(3)
-        tri(3)
+        kwrap(0, 320)
         over(3)
-        sel(1)
-        tt(r("T1"), bank(7), r("E2"), OP.mult)
-        kmask(2)
-        kexp(3)
-        yabs(1)
-        sel(2)
-        kmask(3)
-        yabs(2)
-        tt(r("FZ", 0, 32), bank(5, 0, 32), r("il8"), OP.is_ge)
-        tt(r("FZ", 32, 64), bank(5, 0, 32), r("il"), OP.is_equal)
-        ts(r("q"), r("T1"), 4, OP.arith_shift_right)
-        mm(bank(4, 256, 320), r("BO"), r("FZ"))
-        mm(bank(4, 320, 384), r("IDf"), r("cpos"), True, False)
-        mm(bank(4, 320, 384), r("UP"), r("FZ"), False, True)
-        for c in range(4):
-            mm(bank(5, 64, 65), r("BOf"), r("acc", c, c + 1), c == 0, c == 3)
-        scan(r("sc"), r("RR"), bank(4, 256, 320), OP.mult, OP.add)
-        tt(r("ri"), r("sc"), bank(4, 320, 384), OP.add)
-        tt(r("tm"), r("ri"), r("FZ"), OP.mult)
-        tt(r("po"), r("tm", 0, 32), r("tm", 32, 64), OP.add)
-        tt(r("po"), r("po"), r("ix"), OP.add)
-        cp(r("pu"), r("po"))
-        op("S", [r("LN"), r("pu")], [r("IDb")],
-           lambda: g.scalar.activation(ap(r("IDb")).indirect(ap(r("pu"))), ap(r("LN")), ACT.Silu))
+        comps(4)
+        vote(4)
+        kfast(320, L1)
         pmax(3)
-        ts(r("tf%d" % t), r("iw", 0, 4), r("sc", 31, 32), OP.is_ge, 8192.0, OP.mult)
+        over(4)
+        kfast(L1, 512)
+        pmax(4)
+        tt(r("T1"), bank(6), r("Ui"), OP.mult)
+        rowsum(r("ac"), r("acc"))
+        tt(r("FZ", 0, 32), bank(4, 0, 32), r("il8"), OP.is_ge)
+        tt(r("FZ", 40, 72), bank(4, 0, 32), r("il"), OP.is_equal)
+        mm(bank(1, 0, 80), r("BO"), r("FZ"))
+        mm(bank(1, 80, 120), r("UP"), r("FZ", 0, 40))
+        mm(bank(1, 120, 160), r("UPz"), r("FZ", 40, 80))
+        cp(r("lu"), bank(4, 0, 32))
+        mm(bank(6), r("MB"), r("X"), True, False)
+        mm(bank(5), r("MA"), r("X"), True, False)
+        ts(r("LA"), r("BOd"), r("ac"), OP.mult, r("s2"), OP.add)
+        scan(r("sc"), r("RR"), bank(1, 0, 80), OP.mult, OP.add)
+        blocks(0)
+        sel(0, L1)
+        yabs(0, L1)
+        tt(r("ri"), r("sc"), bank(1, 80, 160), OP.add)
+        ts(r("cu"), r("cb", 0, 4), 0.5, OP.mult, 16.0, OP.add)
+        mm(bank(2, 0, 4), r("ID8"), r("cb", 0, 4), True, False)
+        mm(bank(3, 0, 128, 1, 64), r("ID", 0, 64), r("MN"), True, False)
+        mm(bank(7, 0, 32), one("rA", 128), one("ones", 32), True, False)
+        mm(bank(7, 0, 32), r("LA"), r("hW"), False, False)
+        sel(L1, 512)
+        gtt(r("ind"), r("ri", 0, 40), r("cu"), r("nr"), OP.is_le)
+        yabs(L1, 512)
+        mm(bank(3, 0, 128, 1, 64), r("ind"), r("BO"), False, True)
+        ts(r("tf%d" % t), r("nh"), r("sc", 31, 32), OP.min, 32.5, OP.add)
         send(r("tf%d" % t), "rf%d" % t, to, "aF%d" % t)
-        ts(r("zf"), r("iw", 0, 4), r("sc", 63, 64), OP.is_ge, 8192.0, OP.mult)
-        ts(r("A"), bank(5, 64, 65), -1.0, OP.mult, 7680.0, OP.add)
-        ts(r("A5"), bank(5, 64, 65), -512.0, OP.mult, 512.0 * 7680.0, OP.add)
-        ts(r("iwA"), r("iw"), r("A5"), OP.add)
-        sel(3)
-        mm(bank(7), r("ID"), r("nX"))
-        mm(bank(6), r("SHn"), r("nX"), True, False)
-        mm(bank(6), one("lt15", 128), one("ones", 512), False, True)
-        mm(bank(1), one("ones", 128), one("hi", 512), True, False)
-        mm(bank(1), one("ones", 128), one("lo", 512), False, False)
-        yabs(3)
-        mm(bank(1), r("WS"), r("y", 0, 512), False, True)
-        act(r("Rr", 0, 512), bank(1), ACT.Identity, bias=r("A5"))
-        ts(r("qA"), r("q"), r("A"), OP.add)
-        tt(bank(7), bank(7), r("o"), OP.mult)
-        tt(r("Xn"), bank(6), r("qA"), OP.mult)
-        for c in range(4):
-            ymask(c)
-        mm(bank(0), r("SHI"), r("nX"), True, False)
-        mm(bank(0), one("e15", 128), one("ones", 512), False, True)
-        tt(r("vi"), bank(5, 192, 224), r("iwA"), OP.add)
-        tt(r("idm", 0, 64), r("IDb", 0, 64), r("M16", 0, 64), OP.mult)
-        scan(r("ids", 0, 64), r("R16", 0, 64), r("idm", 0, 64), OP.mult, OP.add)
-        ts(r("idu", 0, 4), r("ids", 15, 64, 16), -31.75, OP.add)
-        gather("S", r("ty%d" % t), r("y"), r("idu", 0, 4))
+        act(r("km", 0, 128, 1, 64), bank(3, 0, 128, 1, 64), ACT.Relu)
+        wrap(bank(7, 0, 32), "Ww", "y", 0, 512, range(4))
+        mm(bank(2, 0, 4), r("km", 0, 128, 1, 64), r("DB", 0, 4, 1, 64), False, True)
+        wrap(bank(7, 0, 32), "Ww", "y", 0, 512, range(4, 16))
+        ts(r("idu"), bank(2, 0, 4), 256.0, OP.add)
+        gather("S", r("ty%d" % t), r("y"), r("idu"))
         send(r("ty%d" % t), "ry%d" % t, to, "aY%d" % t)
-        ts(r("vi"), r("vi"), 4095, OP.bitwise_and)
-        cp(r("vu"), r("vi"))
-        tt(bank(7), bank(7), r("Xn"), OP.add)
-        tt(r("tt"), bank(0), r("Rr", 0, 512), OP.mult)
-        tt(r("idm", 64, 128), r("IDb", 512, 576), r("M16", 0, 64), OP.mult)
-        scan(r("ids", 64, 128), r("R16", 64, 128), r("idm", 64, 128), OP.mult, OP.add)
-        ts(r("idv", 0, 4), r("ids", 79, 128, 16), -31.75, OP.add)
-        gather("S", r("Rz"), r("Rr"), r("idv", 0, 4))
-        tt(r("Ui"), bank(7), r("tt"), OP.add)
-        ts(r("Ui"), r("Ui"), 4095, OP.bitwise_and)
-        if last:
-            cp(r("o"), r("Ui"))
-            dma("Y", T.yo[:, :], ap(r("o")), "dyo", [r("o")], [])
-        else:
-            cp(r("off"), r("Ui"))
+        blocks(1)
+        mm(bank(5), r("WS"), r("y", 0, 512), False, False)
+        mm(bank(5), r("LA"), r("hA"), False, True)
+        mm(bank(6), r("SHf"), r("T1"), False, False)
+        mm(bank(6), r("LA"), r("hB"), False, True)
+        cp(r("vi", 0, 32), bank(7, 0, 32))
+        ts(r("vi", 0, 32), r("vi", 0, 32), 4095, OP.bitwise_and)
+        cp(r("vu"), r("vi", 0, 32))
         scatter(r("bl", 0, 4096), r("vu"), r("y", 0, 512))
-        tt(r("zm"), r("Rz"), r("M16", 0, 64), OP.mult)
-        scan(r("zs"), r("R16", 0, 64), r("zm"), OP.mult, OP.add)
-        cp(r("zi"), r("zs", 15, 64, 16))
-        ts(r("zi"), r("zi"), 4095, OP.bitwise_and)
-        tt(r("cb"), r("zf"), r("rf%d" % t), OP.max)
-        tt(r("cc"), r("cb"), r("nd"), OP.min)
-        tt(r("zo"), r("zi"), r("cc"), OP.max)
-        cp(r("zu"), r("zo"))
+        ts(r("cz"), r("cb", 4, 8), 0.5, OP.mult, 16.0, OP.add)
+        x = [] if last else stack_calls(0, S0)
+        zz = [lambda: gtt(r("iz"), r("ri", 40, 80), r("cz"), r("rf%d" % t), OP.is_equal),
+              lambda: gtt(r("vz"), r("vi"), r("cz"), r("iz"), OP.mult),
+              lambda: tt(r("zm"), bank(1, 256, 320), r("M16", 0, 64), OP.mult),
+              lambda: scan(r("zs"), r("R16"), r("zm"), OP.mult, OP.add),
+              lambda: tt(r("zo"), r("zs", 15, 64, 16), r("nd"), OP.min),
+              lambda: ts(r("zu"), r("zo"), 8192.0, OP.add)]
+        for j in range(6):
+            if j < len(x):
+                x[j]()
+            zz[j]()
+            if j == 1:
+                mm(bank(1, 256, 320), r("BOm"), r("iz"), True, False)
+                mm(bank(1, 256, 320), r("BOf"), r("vz"), False, True)
         scatter(r("bl"), r("zu"), r("ry%d" % t))
     dma("Y", T.yb[:, :], ap(r("bl", 0, 1024)), "dyb", [r("bl", 0, 1024)], [])
+    stacks(0, 512, True)
+    dma("S", T.yo[:, :], ap(r("o")), "dyo", [r("o")], [])
     for sem in cnt:
         need("Y", sem, cnt[sem])

@@ -11,36 +11,156 @@ SCRATCH = {
     "bl": sb(4160, B), "P": sb(8192, B), "PM": sb(8192, B), "C": sb(3840, B),
     "Ui": sb(512, I), "off": sb(512, U), "o": sb(512, F), "w": sb(1, B),
     "cP": sb(1, F), "cQ": sb(1, F), "cG": sb(1, B), "cA": sb(1, F), "c15": sb(1, F), "z": sb(3, F), "dm": sb(1, F), "wi": sb(1, I),
-    "wf": sb(1, F), "bo": sb(1, F), "fs": sb(1, F), "fb": sb(1, F), "s2": sb(1, F), "u": sb(16, F),
-    "rG": sb(128, B), "rA": sb(128, B), "rP": sb(144, B), "r8": sb(8, B), "ones": sb(128, B),
-    "BO": sb(128, B), "BOf": sb(128, F), "BOd": sb(128, B), "BOm": sb(128, B), "M16": sb(128, B), "MN": sb(128, B), "DB": sb(8, B),
-    "ID": sb(128, B), "ID8": sb(128, F), "TRI": sb(128, B), "UP": sb(128, B), "UPz": sb(128, B), "W": sb(144, B), "Wk": sb(144, B),
-    "Ww": sb(144, B), "SH": sb(128, B), "SHf": sb(128, F), "BC0": sb(128, F), "BCn": sb(128, B), "WS": sb(128, B), "MA": sb(128, B),
-    "MB": sb(128, B), "km": sb(128, B), "m": sb(1024, B), "RM": sb(2048, B), "R16": sb(64, B), "RR": sb(80, B),
-    "hA": sb(512, B), "hB": sb(512, B), "hW": sb(32, B), "r256": sb(32, B), "a16": sb(128, B),
-    "il": sb(32, F), "il8": sb(32, F), "nb": sb(4, F), "nd": sb(4, F), "nr": sb(64, F), "nh": sb(64, F),
+    "wf": sb(1, F), "bo": sb(1, F), "bv": sb(1, F), "fs": sb(1, F), "fb": sb(1, F), "s2": sb(1, F), "u": sb(16, F),
+    "rG": sb(128, B), "rA": sb(128, B), "rP": sb(144, B), "ones": sb(128, B), "zer": sb(128, B), "cap": sb(128, B),
+    "BO": sb(128, B), "BOf": sb(128, F), "BOd": sb(128, B), "BOm": sb(128, B), "M16": sb(64, B),
+    "ID": sb(128, B), "IDn": sb(128, B), "ID8": sb(128, F), "IDh": sb(128, F), "TRI": sb(128, B), "T8": sb(128, B), "UP": sb(128, B),
+    "UPz": sb(128, B), "W": sb(144, B), "Wh": sb(144, B), "Wk": sb(144, B), "Ww": sb(144, B), "SH": sb(128, B), "SHf": sb(128, F),
+    "BC0": sb(128, F), "BCn": sb(128, B), "WS": sb(128, B), "MA": sb(128, B), "MB": sb(128, B), "m": sb(1024, B), "RM": sb(2048, B),
+    "R16": sb(64, B), "hA": sb(512, B), "hB": sb(512, B), "hW": sb(32, B), "r256": sb(32, B), "a16": sb(128, B),
+    "il": sb(32, F), "il8": sb(32, F), "nb": sb(4, F), "nd": sb(4, F), "nr": sb(64, F), "nh": sb(64, F), "nn": sb(64, B),
+    "n64": sb(64, B), "k4": sb(64, B),
     "fl": sb(512, B), "T1": sb(512, F), "s1": sb(512, F), "sg": sb(512, B), "X": sb(512, B), "acc": sb(8, F), "ac": sb(1, F),
-    "LA": sb(128, B), "lu": sb(32, U), "df": sb(512, B), "y": sb(576, B), "FZ": sb(80, B), "sc": sb(80, F), "ri": sb(80, F),
-    "jk": sb(32, B), "cb": sb(8, F), "cu": sb(4, U), "cz": sb(4, U), "ind": sb(64, B), "idu": sb(4, U), "vi": sb(40, I), "vu": sb(32, U),
-    "iz": sb(64, B), "vz": sb(64, F), "zm": sb(64, F), "zs": sb(64, F), "zo": sb(4, F), "zu": sb(4, U),
+    "LA": sb(128, B), "lu": sb(32, U), "mx": sb(512, B), "y": sb(576, B), "FZ": sb(80, B), "sc": sb(80, F), "ri": sb(80, F),
+    "pf": sb(192, B), "cn": sb(192, B), "ca": sb(8, F), "jk": sb(1024, B), "cb": sb(8, F), "cu": sb(4, U), "cz": sb(4, U),
+    "ind": sb(64, B), "idu": sb(4, U), "vi": sb(40, I), "vu": sb(32, U),
+    "iz": sb(64, B), "izn": sb(64, B), "vz": sb(64, F), "zm": sb(64, F), "zs": sb(64, F), "zo": sb(4, F), "zu": sb(4, U),
 }
 for _t in range(3):
     SCRATCH["ty%d" % _t] = sb(64, B)
     SCRATCH["ry%d" % _t] = sb(64, B)
-    SCRATCH["tf%d" % _t] = sb(64, B)
-    SCRATCH["rf%d" % _t] = sb(64, B)
+    SCRATCH["tf%d" % _t] = sb(4, F)
+    SCRATCH["rf%d" % _t] = sb(4, F)
 for _b in range(8):
     SCRATCH["b%d" % _b] = ("psum", [128, 512], F)
 
-SEMAPHORES = ["sV", "sS", "sP", "sG", "dstk", "dball", "dwt", "dyo", "dyb", "loc"]
+SEMAPHORES = ["sV", "sS", "sP", "sG", "dstk", "dball", "dwt", "dyo0", "dyo1", "dyb", "loc"]
 for _t in range(3):
     SEMAPHORES += ["aY%d" % _t, "aF%d" % _t]
 
 CH = [(0, 64), (64, 192), (192, 320), (320, 448), (448, 512)]
-L1 = CH[-1][0]
-VG = [[32, 32, 16, 0, 0], [0, 32, 16, 0, 0], [0, 32, 16, 0, 0]]
+L0, L1 = CH[2][0], CH[3][0]
+VG = [[(0, 32), (64, 96), (192, 224)], [(64, 96), (192, 208)], [(64, 96), (192, 208)]]
 VD = [(1, 4), (2, 4), (3, 4), (4, 8), (8, 16)]
-S0 = 128
+S0, SL = 128, 256
+ORDER, PASSES, MOVES = [], 400, 3000
+CYC, WAKE, DMA, REMOTE, FIRST, GATHER, SCATTER = 0.87, 150, 1800, 3270, 1500, 1.56, 3.8
+FIX = {"V": 10, "S": 10, "P": 0, "G": 130}
+
+
+def order(calls, meet, inside):
+    n = len(calls)
+    Q, D, L = [c[0] for c in calls], [c[4] for c in calls], [c[5] for c in calls]
+    before = [{} for _ in calls]
+    seen, lastq = {}, {}
+    for i, (q, reads, writes, _, _, _) in enumerate(calls):
+        for x, w in [(x, False) for x in reads] + [(x, True) for x in writes]:
+            h = seen.setdefault(x[0], [])
+            if SCRATCH[x[0]][0] == "psum":
+                near = h[-1:] + [e for e in h[-20:] if (w or e[2]) and meet(x, e[1])]
+            else:
+                near = [e for e in h if (w or e[2]) and meet(x, e[1])]
+                if w:
+                    h[:] = [e for e in h if not inside(e[1], x)]
+            for j, y, w2 in near:
+                wait = Q[j] != q or ((w or w2) and meet(x, y))
+                t = D[j] if not wait else L[j] + (0 if Q[j] == q == "P" else WAKE)
+                before[i][j] = max(before[i].get(j, 0), t)
+            h.append((i, x, w))
+        if q in "GY" and q in lastq:
+            before[i].setdefault(lastq[q], D[lastq[q]])
+        lastq[q] = i
+        before[i].pop(i, None)
+    gb = [list(b.items()) for b in before]
+    gf = [[] for _ in calls]
+    for i in range(n):
+        for j, t in gb[i]:
+            gf[j].append((i, t))
+    ga = [[(k, D[k] + t - D[i]) for k, t in gf[i]] for i in range(n)]
+    seed = [12345]
+
+    def rnd():
+        seed[0] = (seed[0] * 1103515245 + 12345) % 2147483648
+        return seed[0] / 2147483648
+
+    def place(seq, back):
+        at, busy = [0.0] * n, {q: ([], []) for q in set(Q)}
+        for i in seq:
+            d = D[i]
+            e = L[i] - d if back else 0.0
+            for j, w in (ga if back else gb)[i]:
+                if at[j] + w > e:
+                    e = at[j] + w
+            s, f = busy[Q[i]]
+            k = len(s)
+            while k and f[k - 1] > e:
+                k -= 1
+            while k < len(s) and s[k] < e + d:
+                e = max(e, f[k])
+                k += 1
+            s.insert(k, e)
+            f.insert(k, e + d)
+            at[i] = e
+        return at
+
+    def both(seq):
+        at = place(seq, False)
+        at = place(sorted(range(n), key=lambda i: (-at[i] - D[i], -i)), True)
+        at = place(sorted(range(n), key=lambda i: (-at[i] - D[i], i)), False)
+        return max(at[i] + L[i] for i in range(n)), at
+    best = both(list(range(n)))
+    for _ in range(PASSES):
+        c, w, a = best[0] * rnd(), 1000 + 4000 * rnd(), 2500 * rnd() ** 2
+        key = [best[1][i] + (a * (rnd() - 0.5) if abs(best[1][i] - c) < w else 0) for i in range(n)]
+        for i in range(n):
+            for j, _w in gb[i]:
+                if key[j] >= key[i]:
+                    key[i] = key[j] + 1e-3
+        new = both(sorted(range(n), key=lambda i: key[i]))
+        if new[0] <= best[0]:
+            best = new
+    first = sorted(range(n), key=lambda i: (best[1][i], i))
+    line = {q: [i for i in first if Q[i] == q] for q in sorted(set(Q))}
+
+    def times():
+        nxt, left = [-1] * n, [len(b) for b in gb]
+        for l in line.values():
+            for a, b in zip(l, l[1:]):
+                nxt[a] = b
+                left[b] += 1
+        at, why, todo = [0.0] * n, [-1] * n, [i for i in range(n) if not left[i]]
+        for i in todo:
+            for k, w in gf[i] + [(nxt[i], D[i])] * (nxt[i] >= 0):
+                if at[i] + w > at[k]:
+                    at[k], why[k] = at[i] + w, i
+                left[k] -= 1
+                if not left[k]:
+                    todo.append(k)
+        if len(todo) < n:
+            return None
+        e = max(range(n), key=lambda i: at[i] + L[i])
+        return at[e] + L[e], at, why, e
+    best, pairs = times(), None
+    for _ in range(MOVES):
+        if pairs is None:
+            path, i = [], best[3]
+            while i >= 0:
+                path.append(i)
+                i = best[2][i]
+            pairs = [b for a, b in zip(path, path[1:]) if Q[a] == Q[b] and b not in before[a]]
+        i = pairs[int(rnd() * len(pairs))]
+        l = line[Q[i]]
+        old, p, k = list(l), l.index(i), 1 + int(5 * rnd() ** 2)
+        if rnd() < 0.5:
+            l.insert(max(p + 1 - k, 0), l.pop(p + 1))
+        else:
+            l.insert(p + k, l.pop(p))
+        new = times()
+        if new is not None and new[0] <= best[0]:
+            best, pairs = new, None
+        else:
+            l[:] = old
+    return sorted(range(n), key=lambda i: (best[1][i], i))
 
 
 def rank_program(g, core, T, topo):
@@ -91,7 +211,7 @@ def rank_program(g, core, T, topo):
         for x, w in [(x, False) for x in reads] + [(x, True) for x in writes]:
             psum = SCRATCH[x[0]][0] == "psum"
             for (q2, sem, n, y, w2) in hist.get(x[0], []):
-                if q2 == q and (not w2 or group):
+                if q2 == q and group:
                     continue
                 if not (q2 != q and psum) and (not (w or w2) or not meet(x, y)):
                     continue
@@ -112,7 +232,7 @@ def rank_program(g, core, T, topo):
         c[sem] = n
         clk[(sem, n)] = c
 
-    def op(q, reads, writes, call, group=False):
+    def issue(q, reads, writes, call, group):
         deps(q, reads, writes, group)
         sem = "s" + q
         if q == "G":
@@ -123,6 +243,19 @@ def rank_program(g, core, T, topo):
         call().then_inc(T.sem[sem], 1)
         note(q, sem, cnt[sem], reads, writes)
 
+    calls = []
+
+    def size(x):
+        return len(range(x[1], x[2], x[3]))
+
+    def op(q, reads, writes, call, group=False, cyc=None):
+        n = size(writes[0])
+        if cyc is None:
+            short = all(SCRATCH[x[0]][2] in (B, U) for x in reads + writes if size(x) > 1)
+            cyc = n / 2 if short and q == "V" else n
+        d = CYC * cyc / 2 if q == "P" else max(FIX[q] + CYC * cyc, 55)
+        calls.append((q, reads, writes, lambda: issue(q, reads, writes, call, group), d, d))
+
     def isr(x):
         return isinstance(x, tuple)
 
@@ -130,7 +263,8 @@ def rank_program(g, core, T, topo):
         return ap(x) if isr(x) else x
 
     def tt(out, a, b, o):
-        op("V", [a, b], [out], lambda: g.vector.tensor_tensor(ap(out), ap(a), ap(b), o))
+        op("V", [a, b], [out], lambda: g.vector.tensor_tensor(ap(out), ap(a), ap(b), o),
+           cyc=size(out) * (1 if "psum" in (SCRATCH[a[0]][0], SCRATCH[b[0]][0]) else 2))
 
     def ts(out, a, s1, o0, s2=None, o1=None):
         rd = [a] + [x for x in (s1, s2) if isr(x)]
@@ -145,8 +279,9 @@ def rank_program(g, core, T, topo):
     def ms(out, v):
         op("V", [], [out], lambda: g.vector.memset(ap(out), v))
 
-    def scan(out, d0, d1, o0, o1):
-        op("V", [d0, d1], [out], lambda: g.vector.tensor_tensor_scan(ap(out), ap(d0), ap(d1), 0.0, o0, o1))
+    def scan(out, d0, d1, o0, o1, first=0.0):
+        op("V", [d0, d1] + [x for x in (first,) if isr(x)], [out],
+           lambda: g.vector.tensor_tensor_scan(ap(out), ap(d0), ap(d1), val(first), o0, o1))
 
     def rowsum(out, a):
         op("V", [a], [out], lambda: g.vector.tensor_reduce(ap(out), ap(a), AxisListType.X, OP.add))
@@ -156,52 +291,61 @@ def rank_program(g, core, T, topo):
         if acc is None:
             op("S", rd, [out], lambda: g.scalar.activation(ap(out), ap(a), f, bias=val(bias), scale=val(scale)))
         else:
-            op("S", rd, [out, acc], lambda: g.scalar.activation(ap(out), ap(a), f, bias=val(bias), scale=val(scale), accum_out=ap(acc)))
+            op("S", rd, [out, acc], lambda: g.scalar.activation(ap(out), ap(a), f, bias=val(bias), scale=val(scale), accum_out=ap(acc)),
+               cyc=max(size(out), 52) + 23)
 
     def lin(out, a, scale=1.0, bias=0.0):
         act(out, a, ACT.Identity, bias=bias, scale=scale)
 
     def mm(out, l, rhs, start=True, stop=True):
-        op("P", [l, rhs], [out], lambda: g.tensor.matmul(ap(out), ap(l), ap(rhs), start, stop), group=not start)
+        op("P", [l, rhs], [out], lambda: g.tensor.matmul(ap(out), ap(l), ap(rhs), start, stop), group=not start,
+           cyc=max(min(64, size(l)), size(rhs)) * (4 if SCRATCH[l[0]][2] == F else 1))
 
     def iota(out, pat, base=0, cm=0):
-        op("G", [], [out], lambda: g.iota(ap(out), pat, base, cm, allow_small_or_imprecise_dtypes=True))
+        op("G", [], [out], lambda: g.iota(ap(out), pat, base, cm, allow_small_or_imprecise_dtypes=True), cyc=2 * size(out))
 
     def keep(out, a, cmp, fill, sign):
-        op("G", [a], [out], lambda: g.affine_select(ap(out), ap(a), [[sign, 128]], cmp, fill, 0, -sign))
+        op("G", [a], [out], lambda: g.affine_select(ap(out), ap(a), [[sign, 128]], cmp, fill, 0, -sign), cyc=300)
 
-    def gather(q, out, win, offs):
+    def gather(q, out, win, offs, f=ACT.Copy):
         if q == "V":
-            op("V", [win, offs], [out], lambda: g.vector.tensor_copy(ap(out), ap(win).indirect(ap(offs))))
+            op("V", [win, offs], [out], lambda: g.vector.tensor_copy(ap(out), ap(win).indirect(ap(offs))), cyc=55 + GATHER * size(out))
         else:
-            op("S", [win, offs], [out], lambda: g.scalar.activation(ap(out), ap(win).indirect(ap(offs)), ACT.Copy))
+            op("S", [win, offs], [out], lambda: g.scalar.activation(ap(out), ap(win).indirect(ap(offs)), f), cyc=60 + GATHER * size(out))
 
     def gtt(out, win, offs, b, o):
-        op("V", [win, offs, b], [out], lambda: g.vector.tensor_tensor(ap(out), ap(win).indirect(ap(offs)), ap(b), o))
+        op("V", [win, offs, b], [out], lambda: g.vector.tensor_tensor(ap(out), ap(win).indirect(ap(offs)), ap(b), o),
+           cyc=55 + GATHER * size(out))
 
     def scatter(win, offs, a):
-        op("V", [a, offs], [win], lambda: g.vector.tensor_copy(ap(win).indirect(ap(offs)), ap(a)))
+        op("V", [a, offs], [win], lambda: g.vector.tensor_copy(ap(win).indirect(ap(offs)), ap(a)), cyc=45 + SCATTER * size(a))
 
     def dma(q, out, a, sem, rd, wr):
-        deps(q, rd, wr)
-        eng[q].dma_start(out, a).then_inc(T.sem[sem], 16)
-        cnt[sem] = 16
-        for x in rd:
-            hist.setdefault(x[0], []).append((sem, sem, 16, x, False))
-        for x in wr:
-            hist.setdefault(x[0], []).append((sem, sem, 16, x, True))
-        c = dict(known[q])
-        c[sem] = 16
-        clk[(sem, 16)] = c
+        def go():
+            deps(q, rd, wr)
+            eng[q].dma_start(out, a).then_inc(T.sem[sem], 16)
+            cnt[sem] = 16
+            for x, w in [(x, False) for x in rd] + [(x, True) for x in wr]:
+                hist.setdefault(x[0], []).append((sem, sem, 16, x, w))
+            c = dict(known[q])
+            c[sem] = 16
+            clk[(sem, 16)] = c
+        x = (rd + wr)[0]
+        calls.append((q, rd, wr, go, 50, DMA + size(x) * (1 if SCRATCH[x[0]][2] == B else 2)))
 
-    def send(src, dst_buf, to, sem):
-        deps("G", [src], [])
-        rid, pid = topo.addr(to, core)
-        g.remote_dma(ap((dst_buf,) + src[1:]), ap(src), T.sem[sem], T.sem["loc"], pid, rid, topo.mask(core, to))
-        cnt["loc"] = cnt.get("loc", 0) + len(topo.engines(core, to))
+    def send(src, dst, to, frm, sem):
+        def go():
+            deps("G", [src], [])
+            rid, pid = topo.addr(to, core)
+            g.remote_dma(ap(dst), ap(src), T.sem[sem], T.sem["loc"], pid, rid, topo.mask(core, to))
+            cnt["loc"] = cnt.get("loc", 0) + len(topo.engines(core, to))
+            cnt[sem] = len(topo.engines(frm, core))
+            hist[dst[0]] = [(sem, sem, cnt[sem], dst, True)]
+        more = FIRST if sem == "aF0" else 0
+        calls.append(("G", [src], [dst], go, 500 + more, REMOTE + more))
 
-    def bank(n, a=0, b=512, s=1, k=128):
-        return r("b%d" % n, a, b, s, k)
+    def bank(n, a=0, b=512, s=1):
+        return r("b%d" % n, a, b, s)
 
     def one(name, n):
         return r(name, 0, n, 1, 1)
@@ -210,7 +354,7 @@ def rank_program(g, core, T, topo):
     dma("S", ap(r("bl", 0, 4096)), T.ball[:, :], "dball", [], [r("bl", 0, 4096)])
     dma("Y", ap(r("w")), T.wt[:, :], "dwt", [], [r("w")])
 
-    c1 = L1 // 16
+    c0, c1 = L0 // 16, L1 // 16
     U16, BIG = 65536.0, 1048576.0
 
     def u(j):
@@ -235,11 +379,13 @@ def rank_program(g, core, T, topo):
     iota(r("rA"), [[0, 8], [1, 16]])
     iota(r("rP"), [[1, 144]])
     iota(r("rG"), [[1, 8], [0, 16]], 129)
-    iota(r("r256", 0, c1), [[256, c1]])
+    iota(r("r256", 0, c0), [[256, c0]])
+    iota(r("r256", c0, c1), [[256, c1 - c0]])
     iota(r("r256", c1, 32), [[256, 32 - c1]])
-    iota(r("r8"), [[1, 8]], 129)
     iota(r("nb"), [[16, 4]])
     iota(r("nr"), [[1, 64]])
+    iota(r("n64"), [[1, 64]])
+    iota(r("k4"), [[0, 64]], 4096)
     iota(r("a16"), [[0, 8], [16, 16]])
     ms(r("ones"), 1.0)
     ms(r("RM"), 1.0)
@@ -250,15 +396,13 @@ def rank_program(g, core, T, topo):
     ms(r("RM", 1, 2048, 16), 0.0)
     ts(r("z"), r("rA", 0, 3), r("cA"), OP.is_equal)
     ts(r("dm"), r("cA"), 1.0, OP.is_ge)
-    ts(u(0), r("cA"), 1.0, OP.is_le)
-    ts(u(1), r("cA"), 2.0, OP.is_ge, -192 * U16, OP.mult)
     ts(u(2), r("cA"), 1.0, OP.is_ge, -0.5, OP.mult)
-    ts(u(3), r("cA"), 1.0, OP.is_le, -BIG, OP.mult)
+    ts(u(3), r("cA"), 0.0, OP.is_equal, -BIG, OP.mult)
     ts(r("ID"), r("rP", 0, 128), r("cP"), OP.is_equal)
     ts(r("SH"), r("rP", 1, 129), r("cP"), OP.is_equal, r("dm"), OP.mult)
     ts(r("BO"), r("rG"), r("cG"), OP.is_equal)
     ts(r("W"), r("rP"), r("c15"), OP.is_equal)
-    ts(r("M16"), r("rA"), r("cA"), OP.is_equal)
+    ts(r("M16"), r("rA", 0, 64), r("cA"), OP.is_equal)
     ts(r("wi"), r("w"), 4.0, OP.add)
     ms(r("y", 512, 576), 0.0)
     ts(r("wi"), r("wi"), 7, OP.bitwise_and)
@@ -267,7 +411,7 @@ def rank_program(g, core, T, topo):
     ms(r("vi"), 0)
     lin(m(0), r("BO"), u(2))
     lin(m(1), r("BO"), -1.0)
-    keep(m(0), m(0), OP.is_ge, 0.0, 1)
+    keep(r("TRI"), m(0), OP.is_ge, 0.0, 1)
     keep(r("UP"), m(1), OP.is_gt, 0.0, -1)
     keep(r("UPz"), r("UP"), OP.not_equal, 32.0, 1)
     lin(r("WS"), r("BO"), r("wf"))
@@ -276,39 +420,38 @@ def rank_program(g, core, T, topo):
     ts(r("o"), r("Ui"), -16384.0, OP.add)
     ts(u(4), bank(7, 0, 1), -128.0, OP.mult, -96 * U16, OP.add)
     ms(r("acc"), 0.0)
-    ms(r("RR"), 1.0)
     ms(r("s2"), 0.0)
-    tt(u(4), u(4), u(0), OP.mult)
+    tt(u(4), u(4), z(0), OP.mult)
     ms(r("acc", 7, 8), -256.0)
-    ms(r("RR", 0, 80, 40), 0.0)
     ms(row("s2", 0), 1.0 / 32)
     ms(row("s2", 32), 1.0)
     ts(u(5), r("cA"), 16.0, OP.mult)
-    ts(r("MN"), r("M16"), 64.0, OP.mult, -64.0, OP.add)
     ts(r("il"), r("r256"), u(5), OP.add)
     ts(r("il8"), r("r256"), u(5), OP.add, 8.0, OP.add)
-    ts(r("DB"), r("r8"), r("cG"), OP.is_equal)
     ts(r("R16"), r("rA", 0, 64), 1.0, OP.is_ge)
-    ts(r("nd"), r("nb"), r("cA"), OP.add, -4096.0, OP.add)
+    ts(r("nd"), r("nb"), r("cA"), OP.add, 4096.0, OP.add)
     ts(r("nb"), r("nb"), r("cA"), OP.add, 0.5, OP.add)
     ts(m(2), r("ID"), 192 * U16, OP.mult)
     ts(m(3), r("SH"), BIG, OP.mult)
-    ts(r("BOm"), r("BO"), -8192.0, OP.mult)
+    ts(r("BOm"), r("BO"), -4096.0, OP.mult)
+    ts(u(10), r("cA"), 8.0, OP.is_le, u(2), OP.mult)
+    ms(r("cap"), 255.0)
+    ms(r("zer"), 0.0)
+    ms(r("ri"), 1000.0)
+    cp(r("wi"), r("cA"))
+    ts(r("wi"), r("wi"), 3, OP.bitwise_and)
+    ts(u(9), r("wi"), 0.0, OP.is_equal, -8.0, OP.mult)
     lin(r("fs"), z(0), 1.0 / 1024)
     lin(u(6), z(0), 144.5005, z(2))
     lin(u(7), z(0), 0.125)
     lin(u(8), z(2), 0.0625)
-    lin(u(9), z(1), 0.5)
-    lin(u(10), r("cA"), -0.5, 1.0)
+    lin(r("bo"), r("cA"), -0.5, 1.0)
     lin(r("fb"), z(1), 145.0, u(6))
     lin(u(11), z(1), 128.0, u(8))
-    lin(r("bo"), z(0), -0.5, u(10))
-    lin(m(4), r("SH"), u(9))
     lin(u(12), z(0), -128.0, u(11))
     lin(r("BC0"), r("BO"), u(7))
     lin(r("BCn"), r("BO"), u(12))
-    total(r("TRI"), 5, [m(0), m(4)])
-    lin(m(5), r("SH"), u(1))
+    lin(m(5), r("SH"), -192 * U16)
     lin(m(6), r("BO"), u(4))
     lin(m(7), r("BO"), u(3))
     lin(r("Wk"), r("W"), r("dm"))
@@ -316,10 +459,16 @@ def rank_program(g, core, T, topo):
     total(r("MA"), 6, [m(2), m(5), m(6)])
     total(r("MB"), 7, [m(3), m(7)])
     lin(r("ID8"), r("ID"), 8.0)
+    lin(r("IDn"), r("ID"), -1.0)
+    lin(r("IDh"), r("ID"), 0.5)
+    lin(r("Wh"), r("W"), 0.5)
+    lin(r("T8"), r("BO"), u(10))
+    lin(r("bv"), u(9), 1.0, 8.5)
+    lin(r("SHf"), r("SH"))
     lin(r("BOf"), r("BO"))
     lin(r("BOd"), r("BO"), r("dm"))
-    lin(r("SHf"), r("SH"))
-    lin(r("nh"), r("nr"), 1.0, 0.5)
+    lin(r("nh"), r("nr"), 1.0, 33.0)
+    lin(r("nn"), r("nr"), -1.0)
     iota(r("hW"), [[0, 32]], 512)
     iota(row("hW", 0), [[512, 32]])
     iota(row("hW", 32), [[0, 32]])
@@ -331,42 +480,67 @@ def rank_program(g, core, T, topo):
     iota(row("hB", 32), [[0, 512]], -4352)
 
     def gat(q, a, b):
-        if b > a:
-            gather(q, r("P", 16 * a, 16 * b), r("bl", 0, 4096), r("off", a, b))
+        gather(q, r("P", 16 * a, 16 * b), r("bl", 0, 4096), r("off", a, b))
 
-    def wrap(out, name, src, a, b, js=range(16)):
+    def gats(t, a, b):
+        for x, y in VG[t]:
+            if x == a:
+                for k in range(x, y, 16):
+                    gat("V", k, k + 16)
+                a = y
+        gat("S", a, b)
+
+    def wrap(out, name, src, a, b, js=range(16), stop=True):
         for j in js:
-            mm(out, r(name, 15 - j, 143 - j), r(src, a + j, b, 16), False, j == 15)
+            mm(out, r(name, 15 - j, 143 - j), r(src, a + j, b, 16), False, stop and j == 15)
 
     def xcopy(c):
         a, b = CH[c]
         for j in range(4):
             mm(bank(c % 2, j, 4 * (b - a), 4), r("ID"), r("P", 16 * a, 16 * b, 16))
 
-    def comp(c, d0, s):
-        a, b = CH[c]
-        n, k = b - a, 16 // s
-        at = 1920 * (c % 2) + (512 * (d0 - 1) if d0 < 8 else 1792)
-        tt(r("C", at, at + k * n), r("P", 16 * a + d0, 16 * b, s), bank(c % 2, 0, 4 * n, s // 4), OP.is_lt)
-        for j in range(k):
-            d = d0 + s * j
-            mm(bank(2 + c % 2, 0, n), r("W", 15 - d, 143 - d), r("C", at + j, at + k * n, k), d == VD[0][0], d == VD[-1][0])
+    done = {}
 
-    def comps(c, a=0, b=len(VD)):
-        for d0, s in VD[a:b]:
-            comp(c, d0, s)
+    def count(c, d, w, src):
+        done[c] = done.get(c, 0) % 15 + 1
+        mm(bank(2 + c % 2, 0, CH[c][1] - CH[c][0]), r(w, 15 - d, 143 - d), src, done[c] == 1, done[c] == 15)
 
-    def pmax(c):
+    def comps(c, j0=0, j1=len(VD)):
         a, b = CH[c]
+        for d0, s in VD[j0:j1]:
+            n, k = b - a, 16 // s
+            at = 1920 * (c % 2) + (512 * (d0 - 1) if d0 < 8 else 1792)
+            tt(r("C", at, at + k * n), r("P", 16 * a + d0, 16 * b, s), bank(c % 2, 0, 4 * n, s // 4), OP.is_lt)
+            for j in range(k):
+                count(c, d0 + s * j, "W", r("C", at + j, at + k * n, k))
+
+    def diffs(c):
+        a, b = CH[c]
+        n = b - a
+        for j in range(3):
+            o = bank(7 - 2 * (c % 2), n * j, n * j + n)
+            mm(o, r("ID"), r("P", 16 * a, 16 * b, 16), True, False)
+            mm(o, r("IDn"), r("P", 16 * a + 4 * j + 4, 16 * b, 16), False, True)
+
+    def signs(c):
+        n, at = CH[c][1] - CH[c][0], 1920 * (c % 2) + 1536
+        act(r("C", at, at + 3 * n), bank(7 - 2 * (c % 2), 0, 3 * n), ACT.Sign, bias=-0.5)
+
+    def scount(c):
+        n, at = CH[c][1] - CH[c][0], 1920 * (c % 2) + 1536
+        for j in range(3):
+            count(c, 4 * j + 4, "Wh", r("C", at + n * j, at + n * j + n))
+
+    def pmax(a, b):
         scan(r("PM", 16 * a, 16 * b), r("RM", 0, 16 * (b - a)), r("P", 16 * a, 16 * b), OP.mult, OP.max)
-        if b < 512:
+        if b <= L1:
             iota(r("PM", 16 * a, 16 * b, 16), [[0, b - a]], 255)
-        else:
-            ms(r("PM", 16 * a, 16 * b, 16), 255.0)
 
     def vote(c):
         a, b = CH[c]
-        act(r("sg", a, b), bank(2 + c % 2, 0, b - a), ACT.Sign, bias=8.5, scale=-1.0)
+        act(r("sg", a, b), bank(2 + c % 2, 0, b - a), ACT.Sign, bias=8.5 if c < 3 else r("bv"), scale=-1.0)
+        if c > 2:
+            mm(bank(2 + c % 2, 256, 256 + b - a), r("T8"), r("sg", a, b))
         mm(bank(2 + c % 2, 128, 128 + b - a), r("TRI"), r("sg", a, b))
 
     def over(c):
@@ -379,171 +553,238 @@ def rank_program(g, core, T, topo):
         mm(o, one("a16", 128), one("ones", (b - a) // 16), False, False)
 
     def kwrap(a, b):
-        kconst(a, b)
         wrap(bank(4, a // 16, b // 16), "Wk", "X", a, b)
 
-    def kfast(a, b):
-        n = b - a
-        mm(bank(7, 0, 128, 1, n), r("ID", 0, n), r("MN"), True, False)
-        kconst(a, b)
-        mm(bank(7, 0, 128, 1, n), r("X", a, b), r("BOd"), False, True)
-        act(r("km", 0, 128, 1, n), bank(7, 0, 128, 1, n), ACT.Relu)
-        mm(bank(4, a // 16, b // 16), r("km", 0, 128, 1, n), r("DB", 0, n // 16, 1, n), False, True)
+    def pick(a, b):
+        gather("S", r("mx", a, b), r("PM", 16 * a, 16 * b), r("lu", a // 16, b // 16))
 
-    def sel(a, b):
-        gtt(r("df", a, b), r("PM", 16 * a, 16 * b), r("lu", a // 16, b // 16), r("P", 16 * a, 16 * b, 16), OP.subtract)
+    def less(a, b, n):
+        mm(bank(n, a, b), r("IDn"), r("P", 16 * a, 16 * b, 16), True, False)
+        mm(bank(n, a, b), r("ID"), r("mx", a, b), False, True)
 
-    def yabs(a, b):
-        act(r("y", a, b), r("df", a, b), ACT.Abs)
+    def places(a, b, n):
+        a, b = a // 16, b // 16
+        mm(bank(n, a, b), one("rA", 128), one("ones", b - a), True, False)
+        mm(bank(n, a, b), r("LA"), r("hW", a, b), False, False)
+        wrap(bank(n, a, b), "Ww", "y", 16 * a, 16 * b)
+        return [lambda: cp(r("vi", a, b), bank(n, a, b)),
+                lambda: ts(r("vi", a, b), r("vi", a, b), 4095, OP.bitwise_and),
+                lambda: cp(r("vu", a, b), r("vi", a, b))]
 
-    def stack_calls(a, b, last=False):
+    def own(a, b):
+        scatter(r("bl", 0, 4096), r("vu", a // 16, b // 16), r("y", a, b))
+
+    def eq(*js):
+        for j in js:
+            mm(bank(6, 64 * j, 64 * j + 64), r("BC0"), r("o", 64 * j, 64 * j + 64), False, j == 7)
+
+    def up(*js):
+        for j in js:
+            mm(bank(6, 64 * j, 64 * j + 64), r("SHf"), r("T1", 64 * j, 64 * j + 64), False, False)
+
+    def ra(a, b):
+        for j, (l, x) in enumerate((("MA", "X"), ("WS", "y"), ("LA", "hA"))):
+            mm(bank(5, a, b), r(l), r(x, a, b), j == 0, j == 2)
+
+    def stacks(a, b, last=False):
         return [lambda: tt(r("s1", a, b), bank(5, a, b), r("o", a, b), OP.max),
                 lambda: tt(r("Ui", a, b), bank(6, a, b), r("s1", a, b), OP.max),
                 lambda: ts(r("Ui", a, b), r("Ui", a, b), 4095, OP.bitwise_and),
                 lambda: cp(r("o" if last else "off", a, b), r("Ui", a, b))]
 
-    def stacks(a, b, last=False):
-        for f in stack_calls(a, b, last):
-            f()
-
-    def eq(j):
-        a, b = 128 * j, 128 * j + 128
-        mm(bank(6, a, b), r("BCn"), r("fl", a, b), True, False)
-        mm(bank(6, a, b), r("BC0"), r("o", a, b), False, True)
-
-    def blocks(h):
+    def under(src, out, at):
+        k = size(src)
         for j in range(4):
-            act(r("jk"), r("sc", 40 * h, 40 * h + 32), ACT.Sign, bias=r("nb", j, j + 1), scale=-1.0, acc=r("cb", 4 * h + j, 4 * h + j + 1))
+            act(r("jk", at + k * j, at + k * j + k), src, ACT.Sign, bias=r("nb", j, j + 1), scale=-1.0,
+                acc=r(out[0], out[1] + j, out[1] + j + 1))
 
+    def sums(h, k, n, name):
+        mm(bank(n, 64, 65 + k), r("BO"), r("FZ", 40 * h, 40 * h + k + 1))
+        mm(bank(n, 128, 129 + k), r(name), r("FZ", 40 * h, 40 * h + k + 1))
+
+    def ends(h, k, n):
+        scan(r("sc", 40 * h, 40 * h + k + 1), r("ones", 0, k + 1), bank(n, 64, 65 + k), OP.mult, OP.add)
+
+    def ranks(h, k, n):
+        tt(r("ri", 40 * h, 40 * h + k + h), r("sc", 40 * h, 40 * h + k + h), bank(n, 128, 128 + k + h), OP.add)
+
+    def flags(c):
+        a, b = CH[c]
+        act(r("pf", a - L1, b - L1), bank(2 + c % 2, 256, 256 + b - a), ACT.Relu, bias=-3.0)
+
+    def passing(c):
+        a, b = CH[c]
+        scan(r("cn", a - L1, b - L1), r("pf", a - L1, b - L1), r("cap", 0, b - a), OP.add, OP.min,
+             r("sc", c1 - 1, c1) if a == L1 else r("cn", a - L1 - 1, a - L1))
+
+    def passed(c):
+        a, b = CH[c]
+        under(r("cn", a - L1, b - L1), r("ca", 4 * (c - 3)), 256 + 4 * (a - L1))
+        mm(bank(1, 0, 4), r("IDh"), r("ca", 4 * (c - 3), 4 * (c - 2)), False, c == 4)
+
+    rest = []
     for t in range(3):
         last = t == 2
         to, frm = T.cores[(rank + t + 1) % N], T.cores[(rank - t - 1) % N]
-        for name, sem in (("ry%d" % t, "aY%d" % t), ("rf%d" % t, "aF%d" % t)):
-            n = len(topo.engines(frm, core))
-            hist[name] = [(sem, sem, n, r(name), True)]
-            cnt[sem] = n
-
-        def sg1(c):
-            a, b = CH[c]
-            gat("S", a + VG[t][c], (a + b) // 2)
-
-        def sg2(c):
-            a, b = CH[c]
-            gat("S", (a + b) // 2, b)
-
-        def vg(c):
-            gat("V", CH[c][0], CH[c][0] + VG[t][c])
-
-        gat("S", VG[t][0], CH[0][1])
-        vg(0)
-        sg1(1)
-        if t:
-            stacks(S0, 512)
-            ts(r("o"), r("Ui"), -16384.0, OP.add)
+        gats(t, 0, 64)
+        gats(t, 64, 128)
+        for f in rest:
+            f()
         xcopy(0)
-        sg2(1)
-        comps(0)
-        vg(1)
-        pmax(0)
+        comps(0, 0, 1)
+        if t:
+            ts(r("o"), r("Ui"), -16384.0, OP.add)
+        gats(t, 128, 192)
+        comps(0, 1)
+        pmax(*CH[0])
         xcopy(1)
         vote(0)
         act(r("fl"), r("o"), ACT.Identity, bias=r("fb"), scale=r("fs"))
-        sg1(2)
+        gats(t, 192, 256)
         over(0)
-        sg2(2)
-        comps(1)
-        eq(0)
-        eq(1)
-        vg(2)
-        pmax(1)
+        gats(t, 256, 320)
+        comps(1, 0, 1)
+        mm(bank(6), r("BCn"), r("fl"), True, False)
+        for j in range(1, 5):
+            comps(1, j, j + 1)
+            eq(2 * j - 2, 2 * j - 1)
+        pmax(*CH[1])
         xcopy(2)
         vote(1)
-        sg1(3)
+        tt(r("T1"), bank(6), r("Ui"), OP.mult)
+        gats(t, 320, 384)
         over(1)
-        sg2(3)
-        comps(2)
-        eq(2)
-        eq(3)
-        vg(3)
-        pmax(2)
+        gats(t, 384, 448)
+        mm(bank(6), one("zer", 128), one("hA", 512), True, False)
+        comps(2, 0, 1)
+        up(0, 1)
+        comps(2, 1, 2)
+        kconst(0, L0)
+        kwrap(0, L0)
+        comps(2, 2, 3)
+        up(2, 3)
+        comps(2, 3, 4)
+        cp(r("lu", 0, c0), bank(4, 0, c0))
+        comps(2, 4)
+        pmax(*CH[2])
         xcopy(3)
         vote(2)
-        gat("S", L1, 512)
+        diffs(3)
+        up(4, 5)
+        gats(t, 448, 480)
         over(2)
-        comps(3, 0, 2)
+        pick(0, L0)
+        gats(t, 480, 512)
+        kconst(L0, L1)
+        comps(3, 0, 1)
+        kwrap(L0, L1)
+        less(0, L0, 7)
+        comps(3, 1, 2)
+        tt(r("FZ", 0, c1), bank(4, 0, c1), r("il8", 0, c1), OP.is_ge)
+        cp(r("lu", c0, c1), bank(4, c0, c1))
+        sums(0, c1, 4, "UP")
+        act(r("y", 0, L0), bank(7, 0, L0), ACT.Abs)
+        signs(3)
         xcopy(4)
-        comps(3, 2)
+        comps(3, 2, 3)
+        scount(3)
+        diffs(4)
+        ends(0, c1, 4)
+        under(r("sc", 0, c1), r("cb", 0), 0)
         vote(3)
-        kwrap(0, 320)
+        signs(4)
+        pmax(L1, 384)
+        ranks(0, c1, 4)
+        comps(4, 0, 2)
+        scount(4)
+        flags(3)
         over(3)
-        comps(4)
+        comps(4, 2, 3)
+        pmax(384, 448)
+        ts(r("cu"), r("cb", 0, 4), 0.5, OP.mult, c1 / 2, OP.add)
+        mm(bank(1, 0, 4), r("ID8"), r("cb", 0, 4), True, False)
+        kconst(L1, 512)
         vote(4)
-        kfast(320, L1)
-        pmax(3)
-        over(4)
-        kfast(L1, 512)
-        pmax(4)
-        tt(r("T1"), bank(6), r("Ui"), OP.mult)
-        rowsum(r("ac"), r("acc"))
-        tt(r("FZ", 0, 32), bank(4, 0, 32), r("il8"), OP.is_ge)
-        tt(r("FZ", 40, 72), bank(4, 0, 32), r("il"), OP.is_equal)
-        mm(bank(1, 0, 80), r("BO"), r("FZ"))
-        mm(bank(1, 80, 120), r("UP"), r("FZ", 0, 40))
-        mm(bank(1, 120, 160), r("UPz"), r("FZ", 40, 80))
-        cp(r("lu"), bank(4, 0, 32))
-        mm(bank(6), r("MB"), r("X"), True, False)
-        mm(bank(5), r("MA"), r("X"), True, False)
-        ts(r("LA"), r("BOd"), r("ac"), OP.mult, r("s2"), OP.add)
-        scan(r("sc"), r("RR"), bank(1, 0, 80), OP.mult, OP.add)
-        blocks(0)
-        sel(0, L1)
-        yabs(0, L1)
-        tt(r("ri"), r("sc"), bank(1, 80, 160), OP.add)
-        ts(r("cu"), r("cb", 0, 4), 0.5, OP.mult, 16.0, OP.add)
-        mm(bank(2, 0, 4), r("ID8"), r("cb", 0, 4), True, False)
-        mm(bank(3, 0, 128, 1, 64), r("ID", 0, 64), r("MN"), True, False)
-        mm(bank(7, 0, 32), one("rA", 128), one("ones", 32), True, False)
-        mm(bank(7, 0, 32), r("LA"), r("hW"), False, False)
-        sel(L1, 512)
+        pick(L0, L1)
+        passing(3)
         gtt(r("ind"), r("ri", 0, 40), r("cu"), r("nr"), OP.is_le)
-        yabs(L1, 512)
-        mm(bank(3, 0, 128, 1, 64), r("ind"), r("BO"), False, True)
-        ts(r("tf%d" % t), r("nh"), r("sc", 31, 32), OP.min, 32.5, OP.add)
-        send(r("tf%d" % t), "rf%d" % t, to, "aF%d" % t)
-        act(r("km", 0, 128, 1, 64), bank(3, 0, 128, 1, 64), ACT.Relu)
-        wrap(bank(7, 0, 32), "Ww", "y", 0, 512, range(4))
-        mm(bank(2, 0, 4), r("km", 0, 128, 1, 64), r("DB", 0, 4, 1, 64), False, True)
-        wrap(bank(7, 0, 32), "Ww", "y", 0, 512, range(4, 16))
-        ts(r("idu"), bank(2, 0, 4), 256.0, OP.add)
-        gather("S", r("ty%d" % t), r("y"), r("idu"))
-        send(r("ty%d" % t), "ry%d" % t, to, "aY%d" % t)
-        blocks(1)
-        mm(bank(5), r("WS"), r("y", 0, 512), False, False)
-        mm(bank(5), r("LA"), r("hA"), False, True)
-        mm(bank(6), r("SHf"), r("T1"), False, False)
+        pmax(*CH[4])
+        ms(r("PM", 16 * L1, 8192, 16), 255.0)
+        flags(4)
+        over(4)
+        less(L0, L1, 5)
+        wrap(bank(1, 0, 4), "W", "ind", 0, 64, range(6), False)
+        kwrap(L1, 512)
+        passing(4)
+        rowsum(r("ac"), r("acc"))
+        ts(r("zo"), r("nb"), r("cn", 191, 192), OP.is_gt, 8192.0, OP.mult)
+        tt(r("tf%d" % t), r("zo"), r("nd"), OP.min)
+        send(r("tf%d" % t), r("rf%d" % t), to, frm, "aF%d" % t)
+        ts(r("LA"), r("BOd"), r("ac"), OP.mult, r("s2"), OP.add)
+        act(r("y", L0, L1), bank(5, L0, L1), ACT.Abs)
+        passed(3)
+        v = places(0, L1, 7)
+        wrap(bank(1, 0, 4), "W", "ind", 0, 64, range(6, 16), False)
+        passed(4)
+        cp(r("lu", c1, 32), bank(4, c1, 32))
+        tt(r("FZ", 40, 72), bank(4, 0, 32), r("il"), OP.is_equal)
+        gtt(r("y", L1, 512), r("PM", 16 * L1, 8192), r("lu", c1, 32), r("P", 16 * L1, 8192, 16), OP.subtract)
+        v[0]()
+        sums(1, 32, 3, "UPz")
+        ends(1, 32, 3)
+        v[1]()
+        ts(r("idu"), bank(1, 0, 4), 8.0 * c1 + 96, OP.add)
+        v[2]()
+        gather("S", r("ty%d" % t), r("y"), r("idu"), ACT.Abs)
+        send(r("ty%d" % t), r("ry%d" % t), to, frm, "aY%d" % t)
+        act(r("y", L1, 512), r("y", L1, 512), ACT.Abs)
+        up(6, 7)
+        mm(bank(6), r("MB"), r("X"), False, False)
+        ranks(1, 32, 3)
+        under(r("sc", 40, 72), r("cb", 4), 128)
+        v = places(L1, 512, 0)
+        s0 = SL if last else S0
         mm(bank(6), r("LA"), r("hB"), False, True)
-        cp(r("vi", 0, 32), bank(7, 0, 32))
-        ts(r("vi", 0, 32), r("vi", 0, 32), 4095, OP.bitwise_and)
-        cp(r("vu"), r("vi", 0, 32))
-        scatter(r("bl", 0, 4096), r("vu"), r("y", 0, 512))
+        ra(0, s0)
+        own(0, 160)
+        v[0]()
         ts(r("cz"), r("cb", 4, 8), 0.5, OP.mult, 16.0, OP.add)
-        x = [] if last else stack_calls(0, S0)
-        zz = [lambda: gtt(r("iz"), r("ri", 40, 80), r("cz"), r("rf%d" % t), OP.is_equal),
-              lambda: gtt(r("vz"), r("vi"), r("cz"), r("iz"), OP.mult),
-              lambda: tt(r("zm"), bank(1, 256, 320), r("M16", 0, 64), OP.mult),
-              lambda: scan(r("zs"), r("R16"), r("zm"), OP.mult, OP.add),
-              lambda: tt(r("zo"), r("zs", 15, 64, 16), r("nd"), OP.min),
-              lambda: ts(r("zu"), r("zo"), 8192.0, OP.add)]
-        for j in range(6):
-            if j < len(x):
-                x[j]()
-            zz[j]()
-            if j == 1:
-                mm(bank(1, 256, 320), r("BOm"), r("iz"), True, False)
-                mm(bank(1, 256, 320), r("BOf"), r("vz"), False, True)
+        x = stacks(0, s0, last)
+        x[0]()
+        ra(s0, 512)
+        v[1]()
+        x[1]()
+        v[2]()
+        own(160, L1)
+        gtt(r("iz"), r("ri", 40, 80), r("cz"), r("nh"), OP.is_equal)
+        x[2]()
+        gtt(r("vz"), r("vi"), r("cz"), r("iz"), OP.mult)
+        tt(r("izn"), r("iz"), r("nn"), OP.mult)
+        zb = bank(3, 256, 320)
+        mm(zb, one("ones", 128), one("n64", 64), True, False)
+        mm(zb, one("ones", 128), one("k4", 64), False, False)
+        mm(zb, r("BOm"), r("iz"), False, False)
+        mm(zb, r("BOf"), r("vz"), False, False)
+        mm(zb, r("BO"), r("izn"), False, True)
+        x[3]()
+        if last:
+            dma("S", T.yo[:, 0:s0], ap(r("o", 0, s0)), "dyo0", [r("o", 0, s0)], [])
+        own(L1, 416)
+        tt(r("zm"), zb, r("M16"), OP.mult)
+        own(416, 512)
+        rest = stacks(s0, 512, last)
+        scan(r("zs"), r("R16"), r("zm"), OP.mult, OP.add)
+        rest.pop(0)()
+        tt(r("zo"), r("zs", 15, 64, 16), r("rf%d" % t), OP.max)
+        cp(r("zu"), r("zo"))
         scatter(r("bl"), r("zu"), r("ry%d" % t))
     dma("Y", T.yb[:, :], ap(r("bl", 0, 1024)), "dyb", [r("bl", 0, 1024)], [])
-    stacks(0, 512, True)
-    dma("S", T.yo[:, :], ap(r("o")), "dyo", [r("o")], [])
+    for f in rest:
+        f()
+    dma("S", T.yo[:, SL:512], ap(r("o", SL, 512)), "dyo1", [r("o", SL, 512)], [])
+    if not ORDER:
+        ORDER.extend(order(calls, meet, inside))
+    for i in ORDER:
+        calls[i][3]()
     for sem in cnt:
         need("Y", sem, cnt[sem])

@@ -8,7 +8,7 @@ def sb(n, d):
 
 
 SCRATCH = {
-    "bl": sb(4160, B), "P": sb(8192, B), "PM": sb(8192, B), "C": sb(3840, B),
+    "bl": sb(4160, B), "bf": sb(4160, F), "P": sb(8192, B), "PM": sb(8192, B), "C": sb(3840, B),
     "Ui": sb(512, I), "off": sb(512, U), "o": sb(512, F), "w": sb(1, B),
     "cP": sb(1, F), "cQ": sb(1, F), "cG": sb(1, B), "cA": sb(1, F), "c15": sb(1, F), "z": sb(3, F), "dm": sb(1, F), "wi": sb(1, I),
     "wf": sb(1, F), "bo": sb(1, F), "bv": sb(1, F), "fs": sb(1, F), "fb": sb(1, F), "s2": sb(1, F), "u": sb(16, F),
@@ -18,39 +18,41 @@ SCRATCH = {
     "UPz": sb(128, B), "W": sb(144, B), "Wh": sb(144, B), "Wk": sb(144, B), "Ww": sb(144, B), "SH": sb(128, B), "SHf": sb(128, F),
     "BC0": sb(128, F), "BCn": sb(128, B), "WS": sb(128, B), "MA": sb(128, B), "MB": sb(128, B), "m": sb(1024, B), "RM": sb(2048, B),
     "R16": sb(64, B), "hA": sb(512, B), "hB": sb(512, B), "hW": sb(32, B), "r256": sb(32, B), "a16": sb(128, B),
-    "il": sb(32, F), "il8": sb(32, F), "nb": sb(4, F), "nd": sb(4, F), "nr": sb(64, F), "nh": sb(64, F), "nn": sb(64, B),
-    "n64": sb(64, B), "k4": sb(64, B),
+    "il": sb(32, F), "il8": sb(32, F), "nb": sb(4, F), "nd": sb(4, F), "nr": sb(64, F), "nh": sb(64, F), "k4": sb(64, B),
     "fl": sb(512, B), "T1": sb(512, F), "s1": sb(512, F), "sg": sb(512, B), "X": sb(512, B), "acc": sb(8, F), "ac": sb(1, F),
-    "LA": sb(128, B), "lu": sb(32, U), "mx": sb(512, B), "y": sb(576, B), "FZ": sb(80, B), "sc": sb(80, F), "ri": sb(80, F),
-    "pf": sb(192, B), "cn": sb(192, B), "ca": sb(8, F), "jk": sb(1024, B), "cb": sb(8, F), "cu": sb(4, U), "cz": sb(4, U),
+    "LA": sb(128, B), "lu": sb(32, U), "mx": sb(512, B), "y": sb(576, B), "y33": sb(512, F), "FZ": sb(80, B), "sc": sb(80, F),
+    "ri": sb(80, F), "pf": sb(192, B), "ca": sb(8, F), "jk": sb(1024, B), "cb": sb(8, F), "cu": sb(4, U), "cz": sb(4, U),
     "ind": sb(64, B), "idu": sb(4, U), "vi": sb(40, I), "vu": sb(32, U),
-    "iz": sb(64, B), "izn": sb(64, B), "vz": sb(64, F), "zm": sb(64, F), "zs": sb(64, F), "zo": sb(4, F), "zu": sb(4, U),
+    "iz": sb(64, B), "vz": sb(64, F), "zm": sb(64, F), "zs": sb(64, F), "zf": sb(4, F), "zu": sb(4, U),
 }
 for _t in range(3):
-    SCRATCH["ty%d" % _t] = sb(64, B)
-    SCRATCH["ry%d" % _t] = sb(64, B)
-    SCRATCH["tf%d" % _t] = sb(4, F)
-    SCRATCH["rf%d" % _t] = sb(4, F)
+    SCRATCH["ty%d" % _t] = sb(64, B if _t == 2 else F)
+    SCRATCH["ry%d" % _t] = sb(64, B if _t == 2 else F)
+    SCRATCH["cn%d" % _t] = sb(192, B)
+    SCRATCH["rf%d" % _t] = sb(8, B)
 for _b in range(8):
     SCRATCH["b%d" % _b] = ("psum", [128, 512], F)
 
-SEMAPHORES = ["sV", "sS", "sP", "sG", "dstk", "dball", "dwt", "dyo0", "dyo1", "dyb", "loc"]
+SEMAPHORES = ["sV", "sS", "sP", "sG", "dstk", "dstk2", "dball", "dwt", "dyo0", "dyo1", "dyb", "dbf0", "dbf1", "loc"]
 for _t in range(3):
     SEMAPHORES += ["aY%d" % _t, "aF%d" % _t]
 
 CH = [(0, 64), (64, 192), (192, 320), (320, 448), (448, 512)]
-L0, L1 = CH[2][0], CH[3][0]
-VG = [[(0, 32), (64, 96), (192, 224)], [(64, 96), (192, 208)], [(64, 96), (192, 208)]]
+L1 = CH[3][0]
+VG = [[(0, 32), (64, 96), (192, 208)], [(0, 32), (64, 96), (192, 208)], [(0, 32), (64, 96), (192, 208)]]
 VD = [(1, 4), (2, 4), (3, 4), (4, 8), (8, 16)]
+CUT = [128, 256, 384, 512]
 S0, SL = 128, 256
-ORDER, PASSES, MOVES = [], 400, 3000
-CYC, WAKE, DMA, REMOTE, FIRST, GATHER, SCATTER = 0.87, 150, 1800, 3270, 1500, 1.56, 3.8
-FIX = {"V": 10, "S": 10, "P": 0, "G": 130}
+SLOW = [1.0, 1.25]
+MOVES = 30000
+ORDER, PASSES = [], 2500
+CYC, WAKE, DMA, REMOTE, FIRST, GATHER, SCATTER = 0.87, 150, 1800, 2970, 1500, 1.56, 3.8
+FIX = {"V": 10, "S": 10, "G": 130}
 
 
 def order(calls, meet, inside):
     n = len(calls)
-    Q, D, L = [c[0] for c in calls], [c[4] for c in calls], [c[5] for c in calls]
+    Q = [c[0] for c in calls]
     before = [{} for _ in calls]
     seen, lastq = {}, {}
     for i, (q, reads, writes, _, _, _) in enumerate(calls):
@@ -64,26 +66,31 @@ def order(calls, meet, inside):
                     h[:] = [e for e in h if not inside(e[1], x)]
             for j, y, w2 in near:
                 wait = Q[j] != q or ((w or w2) and meet(x, y))
-                t = D[j] if not wait else L[j] + (0 if Q[j] == q == "P" else WAKE)
-                before[i][j] = max(before[i].get(j, 0), t)
+                before[i][j] = before[i].get(j, False) or wait
             h.append((i, x, w))
-        if q in "GY" and q in lastq:
-            before[i].setdefault(lastq[q], D[lastq[q]])
+        if q == "Y" and q in lastq:
+            before[i].setdefault(lastq[q], False)
         lastq[q] = i
         before[i].pop(i, None)
-    gb = [list(b.items()) for b in before]
-    gf = [[] for _ in calls]
-    for i in range(n):
-        for j, t in gb[i]:
-            gf[j].append((i, t))
-    ga = [[(k, D[k] + t - D[i]) for k, t in gf[i]] for i in range(n)]
-    seed = [12345]
+
+    def costs(f):
+        D = [c[4] * (f if c[4] == c[5] else 1) for c in calls]
+        L = [c[5] * (f if c[4] == c[5] else 1) for c in calls]
+        gb = [[(j, L[j] + (0 if Q[j] == Q[i] == "P" else WAKE) if w else D[j]) for j, w in before[i].items()] for i in range(n)]
+        ga = [[] for _ in calls]
+        for i in range(n):
+            for j, t in gb[i]:
+                ga[j].append((i, D[i] + t - D[j]))
+        return D, L, gb, ga
+    cases = [costs(f) for f in SLOW]
+    seed = [1]
 
     def rnd():
         seed[0] = (seed[0] * 1103515245 + 12345) % 2147483648
         return seed[0] / 2147483648
 
-    def place(seq, back):
+    def place(seq, back, case):
+        D, L, gb, ga = case
         at, busy = [0.0] * n, {q: ([], []) for q in set(Q)}
         for i in seq:
             d = D[i]
@@ -103,63 +110,72 @@ def order(calls, meet, inside):
             at[i] = e
         return at
 
-    def both(seq):
-        at = place(seq, False)
-        at = place(sorted(range(n), key=lambda i: (-at[i] - D[i], -i)), True)
-        at = place(sorted(range(n), key=lambda i: (-at[i] - D[i], i)), False)
-        return max(at[i] + L[i] for i in range(n)), at
-    best = both(list(range(n)))
-    for _ in range(PASSES):
-        c, w, a = best[0] * rnd(), 1000 + 4000 * rnd(), 2500 * rnd() ** 2
+    def replay(seq, case, way=None):
+        D, L, gb, _ = case
+        at, free, last, why = [0.0] * n, {}, {}, [-1] * n
+        for i in seq:
+            q = Q[i]
+            e, why[i] = free.get(q, 0.0), last.get(q, -1)
+            for j, w in gb[i]:
+                if at[j] + w >= e:
+                    e, why[i] = at[j] + w, j
+            at[i] = e
+            free[q], last[q] = e + D[i], i
+        i = max(range(n), key=lambda i: at[i] + L[i])
+        if way is not None:
+            k = i
+            while why[k] >= 0:
+                if why[k] not in before[k]:
+                    way.append((why[k], k))
+                k = why[k]
+        return at[i] + L[i]
+
+    def both(seq, case):
+        D = case[0]
+        at = place(seq, False, case)
+        at = place(sorted(range(n), key=lambda i: (-at[i] - D[i], -i)), True, case)
+        at = place(sorted(range(n), key=lambda i: (-at[i] - D[i], i)), False, case)
+        seq = sorted(range(n), key=lambda i: (at[i], i))
+        return sum(replay(seq, c) / f for c, f in zip(cases, SLOW)), at
+    best = both(list(range(n)), cases[0])
+    for it in range(PASSES):
+        c, w, a = max(best[1]) * rnd(), 1000 + 4000 * rnd(), 2500 * rnd() ** 2
         key = [best[1][i] + (a * (rnd() - 0.5) if abs(best[1][i] - c) < w else 0) for i in range(n)]
         for i in range(n):
-            for j, _w in gb[i]:
+            for j in before[i]:
                 if key[j] >= key[i]:
                     key[i] = key[j] + 1e-3
-        new = both(sorted(range(n), key=lambda i: key[i]))
+        new = both(sorted(range(n), key=lambda i: key[i]), cases[it % len(cases)])
         if new[0] <= best[0]:
             best = new
-    first = sorted(range(n), key=lambda i: (best[1][i], i))
-    line = {q: [i for i in first if Q[i] == q] for q in sorted(set(Q))}
-
-    def times():
-        nxt, left = [-1] * n, [len(b) for b in gb]
-        for l in line.values():
-            for a, b in zip(l, l[1:]):
-                nxt[a] = b
-                left[b] += 1
-        at, why, todo = [0.0] * n, [-1] * n, [i for i in range(n) if not left[i]]
-        for i in todo:
-            for k, w in gf[i] + [(nxt[i], D[i])] * (nxt[i] >= 0):
-                if at[i] + w > at[k]:
-                    at[k], why[k] = at[i] + w, i
-                left[k] -= 1
-                if not left[k]:
-                    todo.append(k)
-        if len(todo) < n:
-            return None
-        e = max(range(n), key=lambda i: at[i] + L[i])
-        return at[e] + L[e], at, why, e
-    best, pairs = times(), None
-    for _ in range(MOVES):
-        if pairs is None:
-            path, i = [], best[3]
-            while i >= 0:
-                path.append(i)
-                i = best[2][i]
-            pairs = [b for a, b in zip(path, path[1:]) if Q[a] == Q[b] and b not in before[a]]
-        i = pairs[int(rnd() * len(pairs))]
-        l = line[Q[i]]
-        old, p, k = list(l), l.index(i), 1 + int(5 * rnd() ** 2)
-        if rnd() < 0.5:
-            l.insert(max(p + 1 - k, 0), l.pop(p + 1))
+    seq = sorted(range(n), key=lambda i: (best[1][i], i))
+    after = [set() for _ in calls]
+    for i in range(n):
+        for j in before[i]:
+            after[j].add(i)
+    now = best[0]
+    for it in range(MOVES):
+        if it % 20 == 0:
+            way = []
+            replay(seq, cases[it // 20 % len(cases)], way)
+        step = 1 if rnd() < 0.5 else -1
+        p = int(n * rnd()) if it % 2 else seq.index(way[int(len(way) * rnd())][step < 0])
+        i, k = seq[p], p
+        stop, left = after[i] if step > 0 else before[i], 1 + int(4 * rnd() ** 2)
+        while left and 0 <= k + step < n and seq[k + step] not in stop:
+            k += step
+            left -= Q[seq[k]] == Q[i]
+        if left:
+            continue
+        seq.insert(k, seq.pop(p))
+        new = sum(replay(seq, c) / f for c, f in zip(cases, SLOW))
+        if new <= now:
+            now = new
         else:
-            l.insert(p + k, l.pop(p))
-        new = times()
-        if new is not None and new[0] <= best[0]:
-            best, pairs = new, None
-        else:
-            l[:] = old
+            seq.insert(p, seq.pop(k))
+    best = (now, [0] * n)
+    for p, i in enumerate(seq):
+        best[1][i] = p
     return sorted(range(n), key=lambda i: (best[1][i], i))
 
 
@@ -256,6 +272,11 @@ def rank_program(g, core, T, topo):
         d = CYC * cyc / 2 if q == "P" else max(FIX[q] + CYC * cyc, 55)
         calls.append((q, reads, writes, lambda: issue(q, reads, writes, call, group), d, d))
 
+    def join(k):
+        x = calls[-k:]
+        d = sum(c[4] for c in x)
+        calls[-k:] = [(x[0][0], sum([c[1] for c in x], []), sum([c[2] for c in x], []), lambda: [c[3]() for c in x], d, d)]
+
     def isr(x):
         return isinstance(x, tuple)
 
@@ -307,31 +328,39 @@ def rank_program(g, core, T, topo):
     def keep(out, a, cmp, fill, sign):
         op("G", [a], [out], lambda: g.affine_select(ap(out), ap(a), [[sign, 128]], cmp, fill, 0, -sign), cyc=300)
 
-    def gather(q, out, win, offs, f=ACT.Copy):
+    def gather(q, out, win, offs, f=ACT.Identity, add=0.0):
         if q == "V":
-            op("V", [win, offs], [out], lambda: g.vector.tensor_copy(ap(out), ap(win).indirect(ap(offs))), cyc=55 + GATHER * size(out))
+            op("V", [win, offs], [out], lambda: g.vector.tensor_scalar(ap(out), ap(win).indirect(ap(offs)), add, None, OP.add),
+               cyc=55 + GATHER * size(out))
         else:
-            op("S", [win, offs], [out], lambda: g.scalar.activation(ap(out), ap(win).indirect(ap(offs)), f), cyc=60 + GATHER * size(out))
+            op("S", [win, offs], [out], lambda: g.scalar.activation(ap(out), ap(win).indirect(ap(offs)), f, bias=add),
+               cyc=60 + GATHER * size(out))
 
     def gtt(out, win, offs, b, o):
         op("V", [win, offs, b], [out], lambda: g.vector.tensor_tensor(ap(out), ap(win).indirect(ap(offs)), ap(b), o),
            cyc=55 + GATHER * size(out))
 
-    def scatter(win, offs, a):
-        op("V", [a, offs], [win], lambda: g.vector.tensor_copy(ap(win).indirect(ap(offs)), ap(a)), cyc=45 + SCATTER * size(a))
+    def scatter(q, win, offs, a, add=None):
+        if q == "S":
+            call = lambda: g.scalar.activation(ap(win).indirect(ap(offs)), ap(a), ACT.Silu)
+        elif add is None:
+            call = lambda: g.vector.tensor_copy(ap(win).indirect(ap(offs)), ap(a))
+        else:
+            call = lambda: g.vector.tensor_scalar(ap(win).indirect(ap(offs)), ap(a), 1.0, add, OP.mult, OP.add)
+        op(q, [a, offs], [win], call, cyc=50 + SCATTER * size(a))
 
-    def dma(q, out, a, sem, rd, wr):
+    def dma(q, out, a, sem, rd, wr, **how):
         def go():
             deps(q, rd, wr)
-            eng[q].dma_start(out, a).then_inc(T.sem[sem], 16)
+            eng[q].dma_start(out, a, **how).then_inc(T.sem[sem], 16)
             cnt[sem] = 16
             for x, w in [(x, False) for x in rd] + [(x, True) for x in wr]:
                 hist.setdefault(x[0], []).append((sem, sem, 16, x, w))
             c = dict(known[q])
             c[sem] = 16
             clk[(sem, 16)] = c
-        x = (rd + wr)[0]
-        calls.append((q, rd, wr, go, 50, DMA + size(x) * (1 if SCRATCH[x[0]][2] == B else 2)))
+        x = (wr + rd)[0]
+        calls.append((q, rd, wr, go, 1000 if q == "G" else 50, DMA + size(x) * (5 if q == "G" else 1 if SCRATCH[x[0]][2] == B else 2)))
 
     def send(src, dst, to, frm, sem):
         def go():
@@ -342,7 +371,7 @@ def rank_program(g, core, T, topo):
             cnt[sem] = len(topo.engines(frm, core))
             hist[dst[0]] = [(sem, sem, cnt[sem], dst, True)]
         more = FIRST if sem == "aF0" else 0
-        calls.append(("G", [src], [dst], go, 500 + more, REMOTE + more))
+        calls.append(("G", [src], [dst], go, 500 + more, REMOTE + more + size(src) * (5 if SCRATCH[src[0]][2] == B else 10)))
 
     def bank(n, a=0, b=512, s=1):
         return r("b%d" % n, a, b, s)
@@ -350,11 +379,12 @@ def rank_program(g, core, T, topo):
     def one(name, n):
         return r(name, 0, n, 1, 1)
 
-    dma("Y", ap(r("Ui")), T.stk[:, :], "dstk", [], [r("Ui")])
+    dma("Y", ap(r("Ui", 0, 128)), T.stk[:, 0:128], "dstk", [], [r("Ui", 0, 128)])
     dma("S", ap(r("bl", 0, 4096)), T.ball[:, :], "dball", [], [r("bl", 0, 4096)])
     dma("Y", ap(r("w")), T.wt[:, :], "dwt", [], [r("w")])
+    dma("S", ap(r("Ui", 128, 512)), T.stk[:, 128:512], "dstk2", [], [r("Ui", 128, 512)])
 
-    c0, c1 = L0 // 16, L1 // 16
+    c1 = L1 // 16
     U16, BIG = 65536.0, 1048576.0
 
     def u(j):
@@ -379,14 +409,17 @@ def rank_program(g, core, T, topo):
     iota(r("rA"), [[0, 8], [1, 16]])
     iota(r("rP"), [[1, 144]])
     iota(r("rG"), [[1, 8], [0, 16]], 129)
-    iota(r("r256", 0, c0), [[256, c0]])
-    iota(r("r256", c0, c1), [[256, c1 - c0]])
+    for h in range(2):
+        a, b = 2048 * h, 2048 * h + 2048
+        for k in range(a, b, 512):
+            iota(r("bf", k, k + 512), [[0, 512]], 33)
+        dma("G", ap(r("bf", a, b)), T.ball[:, a:b], "dbf%d" % h, [r("bl", 0, 1)], [r("bf", a, b)], accum_op=OP.add)
+    iota(r("r256", 0, c1), [[256, c1]])
     iota(r("r256", c1, 32), [[256, 32 - c1]])
     iota(r("nb"), [[16, 4]])
     iota(r("nr"), [[1, 64]])
-    iota(r("n64"), [[1, 64]])
-    iota(r("k4"), [[0, 64]], 4096)
-    iota(r("a16"), [[0, 8], [16, 16]])
+    lin(r("k4"), r("nr"), 0.0, 8192.0)
+    lin(r("a16"), r("rA"), 16.0)
     ms(r("ones"), 1.0)
     ms(r("RM"), 1.0)
     ts(r("cG"), r("cP"), 0.0625, OP.mult, 129.0 - 15.0 / 32, OP.add)
@@ -416,8 +449,9 @@ def rank_program(g, core, T, topo):
     keep(r("UPz"), r("UP"), OP.not_equal, 32.0, 1)
     lin(r("WS"), r("BO"), r("wf"))
     mm(bank(7, 0, 1), r("WS"), r("ones", 0, 1))
-    cp(r("off"), r("Ui"))
-    ts(r("o"), r("Ui"), -16384.0, OP.add)
+    for a, b in ((0, 128), (128, 512)):
+        cp(r("off", a, b), r("Ui", a, b))
+        ts(r("o", a, b), r("Ui", a, b), -16384.0, OP.add)
     ts(u(4), bank(7, 0, 1), -128.0, OP.mult, -96 * U16, OP.add)
     ms(r("acc"), 0.0)
     ms(r("s2"), 0.0)
@@ -425,17 +459,19 @@ def rank_program(g, core, T, topo):
     ms(r("acc", 7, 8), -256.0)
     ms(row("s2", 0), 1.0 / 32)
     ms(row("s2", 32), 1.0)
-    ts(u(5), r("cA"), 16.0, OP.mult)
-    ts(r("il"), r("r256"), u(5), OP.add)
-    ts(r("il8"), r("r256"), u(5), OP.add, 8.0, OP.add)
+    lin(u(5), r("cA"), 16.0)
+    lin(r("il"), r("r256"), 1.0, u(5))
+    lin(r("il8"), r("il"), 1.0, 8.0)
     ts(r("R16"), r("rA", 0, 64), 1.0, OP.is_ge)
-    ts(r("nd"), r("nb"), r("cA"), OP.add, 4096.0, OP.add)
-    ts(r("nb"), r("nb"), r("cA"), OP.add, 0.5, OP.add)
-    ts(m(2), r("ID"), 192 * U16, OP.mult)
-    ts(m(3), r("SH"), BIG, OP.mult)
-    ts(r("BOm"), r("BO"), -4096.0, OP.mult)
+    lin(r("nd"), r("nb"), 1.0, r("cA"))
+    lin(r("nb"), r("nd"), 1.0, 0.5)
+    lin(r("nd"), r("nd"), 1.0, 4096.0)
+    lin(m(2), r("ID"), 192 * U16)
+    lin(m(3), r("SH"), BIG)
+    lin(r("BOm"), r("BO"), -8192.0)
     ts(u(10), r("cA"), 8.0, OP.is_le, u(2), OP.mult)
     ms(r("cap"), 255.0)
+    act(r("cap"), r("cap"), ACT.Silu)
     ms(r("zer"), 0.0)
     ms(r("ri"), 1000.0)
     cp(r("wi"), r("cA"))
@@ -468,36 +504,38 @@ def rank_program(g, core, T, topo):
     lin(r("BOf"), r("BO"))
     lin(r("BOd"), r("BO"), r("dm"))
     lin(r("nh"), r("nr"), 1.0, 33.0)
-    lin(r("nn"), r("nr"), -1.0)
-    iota(r("hW"), [[0, 32]], 512)
+    ms(r("hW"), 512.0)
     iota(row("hW", 0), [[512, 32]])
-    iota(row("hW", 32), [[0, 32]])
-    iota(r("hA"), [[0, 512]], 512)
-    iota(row("hA", 0), [[8192, 2], [0, 256]])
+    ms(row("hW", 32), 0.0)
+    ms(r("hA"), 512.0)
+    ms(r("hA", 0, 256, 1, 1, 0), 0.0)
+    ms(r("hA", 256, 512, 1, 1, 0), 8192.0)
     iota(row("hA", 32), [[0, 2], [1, 256]])
-    iota(r("hB"), [[0, 512]], 1)
-    iota(row("hB", 0), [[0, 512]], -15)
-    iota(row("hB", 32), [[0, 512]], -4352)
+    ms(r("hB"), 1.0)
+    ms(row("hB", 0), -15.0)
+    ms(row("hB", 32), -4352.0)
 
-    def gat(q, a, b):
-        gather(q, r("P", 16 * a, 16 * b), r("bl", 0, 4096), r("off", a, b))
+    def gat(t, q, a, b):
+        gather(q, r("P", 16 * a, 16 * b), r("bf" if t else "bl", 0, 4096), r("off", a, b), add=-32.0 if t else 1.0)
 
     def gats(t, a, b):
         for x, y in VG[t]:
             if x == a:
-                for k in range(x, y, 16):
-                    gat("V", k, k + 16)
+                gat(t, "V", x, y)
                 a = y
-        gat("S", a, b)
+        gat(t, "S", a, b)
 
-    def wrap(out, name, src, a, b, js=range(16), stop=True):
-        for j in js:
+    def wrap(out, name, src, a, b, stop=True):
+        for j in range(16):
             mm(out, r(name, 15 - j, 143 - j), r(src, a + j, b, 16), False, stop and j == 15)
+            if j % 8 == 7:
+                join(8)
 
     def xcopy(c):
         a, b = CH[c]
         for j in range(4):
             mm(bank(c % 2, j, 4 * (b - a), 4), r("ID"), r("P", 16 * a, 16 * b, 16))
+        join(4)
 
     done = {}
 
@@ -513,6 +551,7 @@ def rank_program(g, core, T, topo):
             tt(r("C", at, at + k * n), r("P", 16 * a + d0, 16 * b, s), bank(c % 2, 0, 4 * n, s // 4), OP.is_lt)
             for j in range(k):
                 count(c, d0 + s * j, "W", r("C", at + j, at + k * n, k))
+            join(k)
 
     def diffs(c):
         a, b = CH[c]
@@ -521,6 +560,7 @@ def rank_program(g, core, T, topo):
             o = bank(7 - 2 * (c % 2), n * j, n * j + n)
             mm(o, r("ID"), r("P", 16 * a, 16 * b, 16), True, False)
             mm(o, r("IDn"), r("P", 16 * a + 4 * j + 4, 16 * b, 16), False, True)
+        join(6)
 
     def signs(c):
         n, at = CH[c][1] - CH[c][0], 1920 * (c % 2) + 1536
@@ -530,11 +570,12 @@ def rank_program(g, core, T, topo):
         n, at = CH[c][1] - CH[c][0], 1920 * (c % 2) + 1536
         for j in range(3):
             count(c, 4 * j + 4, "Wh", r("C", at + n * j, at + n * j + n))
+        join(3)
 
     def pmax(a, b):
         scan(r("PM", 16 * a, 16 * b), r("RM", 0, 16 * (b - a)), r("P", 16 * a, 16 * b), OP.mult, OP.max)
         if b <= L1:
-            iota(r("PM", 16 * a, 16 * b, 16), [[0, b - a]], 255)
+            iota(r("PM", 16 * a, 16 * b, 16), [[0, b - a]], 256)
 
     def vote(c):
         a, b = CH[c]
@@ -551,6 +592,7 @@ def rank_program(g, core, T, topo):
         o = bank(4, a // 16, b // 16)
         mm(o, one("ones", 128), r("r256", a // 16, b // 16, 1, 1), True, False)
         mm(o, one("a16", 128), one("ones", (b - a) // 16), False, False)
+        join(2)
 
     def kwrap(a, b):
         wrap(bank(4, a // 16, b // 16), "Wk", "X", a, b)
@@ -572,7 +614,7 @@ def rank_program(g, core, T, topo):
                 lambda: cp(r("vu", a, b), r("vi", a, b))]
 
     def own(a, b):
-        scatter(r("bl", 0, 4096), r("vu", a // 16, b // 16), r("y", a, b))
+        scatter("S", r("bf", 0, 4096), r("vu", a // 16, b // 16), r("y33", a, b))
 
     def eq(*js):
         for j in js:
@@ -601,6 +643,7 @@ def rank_program(g, core, T, topo):
     def sums(h, k, n, name):
         mm(bank(n, 64, 65 + k), r("BO"), r("FZ", 40 * h, 40 * h + k + 1))
         mm(bank(n, 128, 129 + k), r(name), r("FZ", 40 * h, 40 * h + k + 1))
+        join(2)
 
     def ends(h, k, n):
         scan(r("sc", 40 * h, 40 * h + k + 1), r("ones", 0, k + 1), bank(n, 64, 65 + k), OP.mult, OP.add)
@@ -612,14 +655,14 @@ def rank_program(g, core, T, topo):
         a, b = CH[c]
         act(r("pf", a - L1, b - L1), bank(2 + c % 2, 256, 256 + b - a), ACT.Relu, bias=-3.0)
 
-    def passing(c):
+    def passing(t, c):
         a, b = CH[c]
-        scan(r("cn", a - L1, b - L1), r("pf", a - L1, b - L1), r("cap", 0, b - a), OP.add, OP.min,
-             r("sc", c1 - 1, c1) if a == L1 else r("cn", a - L1 - 1, a - L1))
+        scan(r("cn%d" % t, a - L1, b - L1), r("pf", a - L1, b - L1), r("cap", 0, b - a), OP.add, OP.min,
+             r("sc", c1 - 1, c1) if a == L1 else r("cn%d" % t, a - L1 - 1, a - L1))
 
-    def passed(c):
+    def passed(t, c):
         a, b = CH[c]
-        under(r("cn", a - L1, b - L1), r("ca", 4 * (c - 3)), 256 + 4 * (a - L1))
+        under(r("cn%d" % t, a - L1, b - L1), r("ca", 4 * (c - 3)), 256 + 4 * (a - L1))
         mm(bank(1, 0, 4), r("IDh"), r("ca", 4 * (c - 3), 4 * (c - 2)), False, c == 4)
 
     rest = []
@@ -633,16 +676,17 @@ def rank_program(g, core, T, topo):
         xcopy(0)
         comps(0, 0, 1)
         if t:
-            ts(r("o"), r("Ui"), -16384.0, OP.add)
+            for a, b in zip([0] + CUT, CUT):
+                ts(r("o", a, b), r("Ui", a, b), -16384.0, OP.add)
         gats(t, 128, 192)
         comps(0, 1)
         pmax(*CH[0])
         xcopy(1)
         vote(0)
-        act(r("fl"), r("o"), ACT.Identity, bias=r("fb"), scale=r("fs"))
-        gats(t, 192, 256)
+        for a in (0, 256):
+            act(r("fl", a, a + 256), r("o", a, a + 256), ACT.Identity, bias=r("fb"), scale=r("fs"))
+        gats(t, 192, 320)
         over(0)
-        gats(t, 256, 320)
         comps(1, 0, 1)
         mm(bank(6), r("BCn"), r("fl"), True, False)
         for j in range(1, 5):
@@ -651,21 +695,17 @@ def rank_program(g, core, T, topo):
         pmax(*CH[1])
         xcopy(2)
         vote(1)
-        tt(r("T1"), bank(6), r("Ui"), OP.mult)
-        gats(t, 320, 384)
+        for a in (0, 256):
+            tt(r("T1", a, a + 256), bank(6, a, a + 256), r("Ui", a, a + 256), OP.mult)
+        gats(t, 320, 448)
         over(1)
-        gats(t, 384, 448)
         mm(bank(6), one("zer", 128), one("hA", 512), True, False)
         comps(2, 0, 1)
         up(0, 1)
         comps(2, 1, 2)
-        kconst(0, L0)
-        kwrap(0, L0)
         comps(2, 2, 3)
         up(2, 3)
-        comps(2, 3, 4)
-        cp(r("lu", 0, c0), bank(4, 0, c0))
-        comps(2, 4)
+        comps(2, 3)
         pmax(*CH[2])
         xcopy(3)
         vote(2)
@@ -673,17 +713,16 @@ def rank_program(g, core, T, topo):
         up(4, 5)
         gats(t, 448, 480)
         over(2)
-        pick(0, L0)
         gats(t, 480, 512)
-        kconst(L0, L1)
+        kconst(0, L1)
         comps(3, 0, 1)
-        kwrap(L0, L1)
-        less(0, L0, 7)
+        kwrap(0, L1)
+        up(6, 7)
+        mm(bank(6, 0, L1), r("MB"), r("X", 0, L1), False, False)
         comps(3, 1, 2)
         tt(r("FZ", 0, c1), bank(4, 0, c1), r("il8", 0, c1), OP.is_ge)
-        cp(r("lu", c0, c1), bank(4, c0, c1))
+        cp(r("lu", 0, c1), bank(4, 0, c1))
         sums(0, c1, 4, "UP")
-        act(r("y", 0, L0), bank(7, 0, L0), ACT.Abs)
         signs(3)
         xcopy(4)
         comps(3, 2, 3)
@@ -705,27 +744,24 @@ def rank_program(g, core, T, topo):
         mm(bank(1, 0, 4), r("ID8"), r("cb", 0, 4), True, False)
         kconst(L1, 512)
         vote(4)
-        pick(L0, L1)
-        passing(3)
+        pick(0, L1)
+        passing(t, 3)
         gtt(r("ind"), r("ri", 0, 40), r("cu"), r("nr"), OP.is_le)
         pmax(*CH[4])
-        ms(r("PM", 16 * L1, 8192, 16), 255.0)
+        ms(r("PM", 16 * L1, 8192, 16), 256.0)
         flags(4)
         over(4)
-        less(L0, L1, 5)
-        wrap(bank(1, 0, 4), "W", "ind", 0, 64, range(6), False)
+        less(0, L1, 5)
+        wrap(bank(1, 0, 4), "W", "ind", 0, 64, False)
         kwrap(L1, 512)
-        passing(4)
+        passing(t, 4)
+        send(r("cn%d" % t, 184, 192), r("rf%d" % t), to, frm, "aF%d" % t)
+        passed(t, 3)
+        passed(t, 4)
         rowsum(r("ac"), r("acc"))
-        ts(r("zo"), r("nb"), r("cn", 191, 192), OP.is_gt, 8192.0, OP.mult)
-        tt(r("tf%d" % t), r("zo"), r("nd"), OP.min)
-        send(r("tf%d" % t), r("rf%d" % t), to, frm, "aF%d" % t)
         ts(r("LA"), r("BOd"), r("ac"), OP.mult, r("s2"), OP.add)
-        act(r("y", L0, L1), bank(5, L0, L1), ACT.Abs)
-        passed(3)
+        act(r("y", 0, L1), bank(5, 0, L1), ACT.Abs)
         v = places(0, L1, 7)
-        wrap(bank(1, 0, 4), "W", "ind", 0, 64, range(6, 16), False)
-        passed(4)
         cp(r("lu", c1, 32), bank(4, c1, 32))
         tt(r("FZ", 40, 72), bank(4, 0, 32), r("il"), OP.is_equal)
         gtt(r("y", L1, 512), r("PM", 16 * L1, 8192), r("lu", c1, 32), r("P", 16 * L1, 8192, 16), OP.subtract)
@@ -738,15 +774,16 @@ def rank_program(g, core, T, topo):
         gather("S", r("ty%d" % t), r("y"), r("idu"), ACT.Abs)
         send(r("ty%d" % t), r("ry%d" % t), to, frm, "aY%d" % t)
         act(r("y", L1, 512), r("y", L1, 512), ACT.Abs)
-        up(6, 7)
-        mm(bank(6), r("MB"), r("X"), False, False)
+        mm(bank(6, L1, 512), r("MB"), r("X", L1, 512), False, False)
         ranks(1, 32, 3)
         under(r("sc", 40, 72), r("cb", 4), 128)
         v = places(L1, 512, 0)
         s0 = SL if last else S0
         mm(bank(6), r("LA"), r("hB"), False, True)
         ra(0, s0)
-        own(0, 160)
+        lin(r("y33", 0, L1), r("y", 0, L1), 1.0, 33.0)
+        own(0, L1)
+        lin(r("y33", L1, 512), r("y", L1, 512), 1.0, 33.0)
         v[0]()
         ts(r("cz"), r("cb", 4, 8), 0.5, OP.mult, 16.0, OP.add)
         x = stacks(0, s0, last)
@@ -755,29 +792,31 @@ def rank_program(g, core, T, topo):
         v[1]()
         x[1]()
         v[2]()
-        own(160, L1)
         gtt(r("iz"), r("ri", 40, 80), r("cz"), r("nh"), OP.is_equal)
         x[2]()
         gtt(r("vz"), r("vi"), r("cz"), r("iz"), OP.mult)
-        tt(r("izn"), r("iz"), r("nn"), OP.mult)
         zb = bank(3, 256, 320)
-        mm(zb, one("ones", 128), one("n64", 64), True, False)
-        mm(zb, one("ones", 128), one("k4", 64), False, False)
+        mm(zb, one("ones", 128), one("k4", 64), True, False)
         mm(zb, r("BOm"), r("iz"), False, False)
-        mm(zb, r("BOf"), r("vz"), False, False)
-        mm(zb, r("BO"), r("izn"), False, True)
+        mm(zb, r("BOf"), r("vz"), False, True)
         x[3]()
         if last:
             dma("S", T.yo[:, 0:s0], ap(r("o", 0, s0)), "dyo0", [r("o", 0, s0)], [])
-        own(L1, 416)
+        own(L1, 512)
         tt(r("zm"), zb, r("M16"), OP.mult)
-        own(416, 512)
-        rest = stacks(s0, 512, last)
+        rest = [f for fs in zip(*[stacks(a, b, last) for a, b in zip(CUT, CUT[1:]) if a >= s0]) for f in fs]
         scan(r("zs"), r("R16"), r("zm"), OP.mult, OP.add)
         rest.pop(0)()
-        tt(r("zo"), r("zs", 15, 64, 16), r("rf%d" % t), OP.max)
-        cp(r("zu"), r("zo"))
-        scatter(r("bl"), r("zu"), r("ry%d" % t))
+        ts(r("zf"), r("nb"), r("rf%d" % t, 7, 8), OP.is_gt, 8192.0, OP.mult)
+        for j in range(4):
+            ts(r("zu", j, j + 1), r("zs", 16 * j + 15, 16 * j + 16), r("zf", j, j + 1), OP.max, r("nd", j, j + 1), OP.min)
+        if last:
+            ts(r("bl", 0, 768), r("bf", 0, 768), 1.5 * 2 ** 23 - 33, OP.add, -1.5 * 2 ** 23, OP.add)
+            lin(r("y33", 0, 256), r("bf", 768, 1024), 1.0, 1.5 * 2 ** 23 - 33)
+            lin(r("bl", 768, 1024), r("y33", 0, 256), 1.0, -1.5 * 2 ** 23)
+            scatter("V", r("bl"), r("zu"), r("ry%d" % t))
+        else:
+            scatter("V", r("bf"), r("zu"), r("ry%d" % t), 33.0)
     dma("Y", T.yb[:, :], ap(r("bl", 0, 1024)), "dyb", [r("bl", 0, 1024)], [])
     for f in rest:
         f()

from concourse.mybir import AluOpType, ActivationFunctionType, AxisListType

F, B, I, U = "float32", "bfloat16", "int32", "uint16"


def sb(n, d):
    return ("sbuf", [128, n], d)


SCRATCH = {
    "bl": sb(4160, B), "bf": sb(4160, F), "P": sb(8192, B), "PM": sb(8192, B), "C": sb(3840, B),
    "Ui": sb(512, I), "off": sb(512, U), "o": sb(512, F), "w": sb(1, B),
    "cP": sb(1, F), "cQ": sb(1, F), "cG": sb(1, B), "cA": sb(1, F), "c15": sb(1, F), "z": sb(3, F), "dm": sb(1, F), "wi": sb(1, I),
    "wf": sb(1, F), "bo": sb(1, F), "bv": sb(1, F), "fs": sb(1, F), "fb": sb(1, F), "s2": sb(1, F), "u": sb(16, F),
    "rG": sb(128, B), "rA": sb(128, B), "rP": sb(144, B), "ones": sb(128, B), "zer": sb(128, B), "cap": sb(128, B),
    "BO": sb(128, B), "BOf": sb(128, F), "BOd": sb(128, B), "BOm": sb(128, B), "M16": sb(64, B),
    "ID": sb(128, B), "IDn": sb(128, B), "ID8": sb(128, F), "IDh": sb(128, F), "TRI": sb(128, B), "T8": sb(128, B), "UP": sb(128, B),
    "UPz": sb(128, B), "W": sb(144, B), "Wh": sb(144, B), "Wk": sb(144, B), "Ww": sb(144, B), "SH": sb(128, B), "SHf": sb(128, F),
    "BC0": sb(128, F), "BCn": sb(128, B), "WS": sb(128, B), "MA": sb(128, B), "MB": sb(128, B), "m": sb(1024, B), "RM": sb(2048, B),
    "R16": sb(64, B), "hA": sb(512, B), "hB": sb(512, B), "hW": sb(32, B), "r256": sb(32, B), "a16": sb(128, B),
    "il": sb(32, F), "il8": sb(32, F), "nb": sb(4, F), "nd": sb(4, F), "nr": sb(64, F), "nh": sb(64, F), "k4": sb(64, B),
    "fl": sb(512, B), "T1": sb(512, F), "s1": sb(512, F), "sg": sb(512, B), "X": sb(512, B), "acc": sb(8, F), "ac": sb(1, F),
    "LA": sb(128, B), "lu": sb(32, U), "mx": sb(512, B), "y": sb(576, B), "y33": sb(512, F), "FZ": sb(80, B), "sc": sb(80, F),
    "ri": sb(80, F), "pf": sb(192, B), "ca": sb(8, F), "jk": sb(1024, B), "cb": sb(8, F), "cu": sb(4, U), "cz": sb(4, U),
    "ind": sb(64, B), "idu": sb(4, U), "vi": sb(40, I), "vu": sb(32, U),
    "iz": sb(64, B), "vz": sb(64, F), "zm": sb(64, F), "zs": sb(64, F), "zf": sb(4, F), "zu": sb(4, U),
}
for _t in range(3):
    SCRATCH["ty%d" % _t] = sb(64, B if _t == 2 else F)
    SCRATCH["ry%d" % _t] = sb(64, B if _t == 2 else F)
    SCRATCH["cn%d" % _t] = sb(192, B)
    SCRATCH["rf%d" % _t] = sb(8, B)
for _b in range(8):
    SCRATCH["b%d" % _b] = ("psum", [128, 512], F)

SEMAPHORES = ["sV", "sS", "sP", "sG", "dstk", "dstk2", "dball", "dwt", "dyo0", "dyo1", "dyb", "dbf0", "dbf1", "loc"]
for _t in range(3):
    SEMAPHORES += ["aY%d" % _t, "aF%d" % _t]

CH = [(0, 64), (64, 192), (192, 320), (320, 448), (448, 512)]
L1 = CH[3][0]
VG = [[(0, 32), (64, 96), (192, 208)], [(0, 32), (64, 96), (192, 208)], [(0, 32), (64, 96), (192, 208)]]
VD = [(1, 4), (2, 4), (3, 4), (4, 8), (8, 16)]
CUT = [128, 256, 384, 512]
S0, SL = 128, 256
SLOW = [1.0, 1.25]
MOVES = 30000
ORDER, PASSES = [], 2500
CYC, WAKE, DMA, REMOTE, FIRST, GATHER, SCATTER = 0.87, 150, 1800, 2970, 1500, 1.56, 3.8
FIX = {"V": 10, "S": 10, "G": 130}


def order(calls, meet, inside):
    n = len(calls)
    Q = [c[0] for c in calls]
    before = [{} for _ in calls]
    seen, lastq = {}, {}
    for i, (q, reads, writes, _, _, _) in enumerate(calls):
        for x, w in [(x, False) for x in reads] + [(x, True) for x in writes]:
            h = seen.setdefault(x[0], [])
            if SCRATCH[x[0]][0] == "psum":
                near = h[-1:] + [e for e in h[-20:] if (w or e[2]) and meet(x, e[1])]
            else:
                near = [e for e in h if (w or e[2]) and meet(x, e[1])]
                if w:
                    h[:] = [e for e in h if not inside(e[1], x)]
            for j, y, w2 in near:
                wait = Q[j] != q or ((w or w2) and meet(x, y))
                before[i][j] = before[i].get(j, False) or wait
            h.append((i, x, w))
        if q == "Y" and q in lastq:
            before[i].setdefault(lastq[q], False)
        lastq[q] = i
        before[i].pop(i, None)

    def costs(f):
        D = [c[4] * (f if c[4] == c[5] else 1) for c in calls]
        L = [c[5] * (f if c[4] == c[5] else 1) for c in calls]
        gb = [[(j, L[j] + (0 if Q[j] == Q[i] == "P" else WAKE) if w else D[j]) for j, w in before[i].items()] for i in range(n)]
        ga = [[] for _ in calls]
        for i in range(n):
            for j, t in gb[i]:
                ga[j].append((i, D[i] + t - D[j]))
        return D, L, gb, ga
    cases = [costs(f) for f in SLOW]
    seed = [1]

    def rnd():
        seed[0] = (seed[0] * 1103515245 + 12345) % 2147483648
        return seed[0] / 2147483648

    def place(seq, back, case):
        D, L, gb, ga = case
        at, busy = [0.0] * n, {q: ([], []) for q in set(Q)}
        for i in seq:
            d = D[i]
            e = L[i] - d if back else 0.0
            for j, w in (ga if back else gb)[i]:
                if at[j] + w > e:
                    e = at[j] + w
            s, f = busy[Q[i]]
            k = len(s)
            while k and f[k - 1] > e:
                k -= 1
            while k < len(s) and s[k] < e + d:
                e = max(e, f[k])
                k += 1
            s.insert(k, e)
            f.insert(k, e + d)
            at[i] = e
        return at

    def replay(seq, case, way=None):
        D, L, gb, _ = case
        at, free, last, why = [0.0] * n, {}, {}, [-1] * n
        for i in seq:
            q = Q[i]
            e, why[i] = free.get(q, 0.0), last.get(q, -1)
            for j, w in gb[i]:
                if at[j] + w >= e:
                    e, why[i] = at[j] + w, j
            at[i] = e
            free[q], last[q] = e + D[i], i
        i = max(range(n), key=lambda i: at[i] + L[i])
        if way is not None:
            k = i
            while why[k] >= 0:
                if why[k] not in before[k]:
                    way.append((why[k], k))
                k = why[k]
        return at[i] + L[i]

    def both(seq, case):
        D = case[0]
        at = place(seq, False, case)
        at = place(sorted(range(n), key=lambda i: (-at[i] - D[i], -i)), True, case)
        at = place(sorted(range(n), key=lambda i: (-at[i] - D[i], i)), False, case)
        seq = sorted(range(n), key=lambda i: (at[i], i))
        return sum(replay(seq, c) / f for c, f in zip(cases, SLOW)), at
    best = both(list(range(n)), cases[0])
    for it in range(PASSES):
        c, w, a = max(best[1]) * rnd(), 1000 + 4000 * rnd(), 2500 * rnd() ** 2
        key = [best[1][i] + (a * (rnd() - 0.5) if abs(best[1][i] - c) < w else 0) for i in range(n)]
        for i in range(n):
            for j in before[i]:
                if key[j] >= key[i]:
                    key[i] = key[j] + 1e-3
        new = both(sorted(range(n), key=lambda i: key[i]), cases[it % len(cases)])
        if new[0] <= best[0]:
            best = new
    seq = sorted(range(n), key=lambda i: (best[1][i], i))
    after = [set() for _ in calls]
    for i in range(n):
        for j in before[i]:
            after[j].add(i)
    now = best[0]
    for it in range(MOVES):
        if it % 20 == 0:
            way = []
            replay(seq, cases[it // 20 % len(cases)], way)
        step = 1 if rnd() < 0.5 else -1
        p = int(n * rnd()) if it % 2 else seq.index(way[int(len(way) * rnd())][step < 0])
        i, k = seq[p], p
        stop, left = after[i] if step > 0 else before[i], 1 + int(4 * rnd() ** 2)
        while left and 0 <= k + step < n and seq[k + step] not in stop:
            k += step
            left -= Q[seq[k]] == Q[i]
        if left:
            continue
        seq.insert(k, seq.pop(p))
        new = sum(replay(seq, c) / f for c, f in zip(cases, SLOW))
        if new <= now:
            now = new
        else:
            seq.insert(p, seq.pop(k))
    best = (now, [0] * n)
    for p, i in enumerate(seq):
        best[1][i] = p
    return sorted(range(n), key=lambda i: (best[1][i], i))


def rank_program(g, core, T, topo):
    rank = T.rank_of(core)
    if rank is None:
        return
    N = len(T.cores)
    OP, ACT = AluOpType, ActivationFunctionType
    eng = {"V": g.vector, "S": g.scalar, "P": g.tensor, "G": g, "Y": g.sync}
    cnt = {}
    known = {q: {} for q in eng}
    clk = {}
    part = [False]
    hist = {}

    def r(name, a=0, b=None, s=1, n=128, p=0):
        return (name, a, SCRATCH[name][1][1] if b is None else b, s, n, p)

    def ap(x):
        t = T[x[0]]
        if x[3] == 1:
            return t[:, x[1]:x[2]] if x[4] == 128 else t[x[5]:x[5] + x[4], x[1]:x[2]]
        return t[:, x[1]:x[2]:x[3]]

    def meet(x, y):
        if x[2] <= y[1] or y[2] <= x[1]:
            return False
        if x[3] == y[3] and x[3] > 1 and (x[1] - y[1]) % x[3]:
            return False
        return True

    def inside(x, y):
        return y[3] == 1 and y[4] == 128 and y[1] <= x[1] and x[2] <= y[2]

    def learn(q, sem, n):
        k = known[q]
        for e, v in clk.get((sem, n), {sem: n}).items():
            if v > k.get(e, 0):
                k[e] = v

    def need(q, sem, n):
        if known[q].get(sem, 0) < n:
            eng[q].wait_ge(T.sem[sem], n)
            learn(q, sem, n)

    def deps(q, reads, writes, group=False):
        want = {}
        for x, w in [(x, False) for x in reads] + [(x, True) for x in writes]:
            psum = SCRATCH[x[0]][0] == "psum"
            for (q2, sem, n, y, w2) in hist.get(x[0], []):
                if q2 == q and group:
                    continue
                if not (q2 != q and psum) and (not (w or w2) or not meet(x, y)):
                    continue
                want[sem] = max(want.get(sem, 0), n)
        for sem in sorted(want, key=lambda e: -want[e]):
            need(q, sem, want[sem])

    def note(q, sem, n, reads, writes):
        for x, w in [(x, False) for x in reads] + [(x, True) for x in writes]:
            h = hist.setdefault(x[0], [])
            if w:
                psum = SCRATCH[x[0]][0] == "psum"
                h[:] = [e for e in h if not (inside(e[3], x) and (not psum or e[0] == q or known[q].get(e[1], 0) >= e[2]))]
            else:
                h[:] = [e for e in h if not (e[0] == q and not e[4] and e[3] == x)]
            h.append((q, sem, n, x, w))
        c = dict(known[q])
        c[sem] = n
        clk[(sem, n)] = c

    def issue(q, reads, writes, call, group):
        deps(q, reads, writes, group)
        sem = "s" + q
        if q == "G":
            if part[0] or writes[0][4] < 128:
                need(q, sem, cnt.get(sem, 0))
            part[0] = writes[0][4] < 128
        cnt[sem] = cnt.get(sem, 0) + 1
        call().then_inc(T.sem[sem], 1)
        note(q, sem, cnt[sem], reads, writes)

    calls = []

    def size(x):
        return len(range(x[1], x[2], x[3]))

    def op(q, reads, writes, call, group=False, cyc=None):
        n = size(writes[0])
        if cyc is None:
            short = all(SCRATCH[x[0]][2] in (B, U) for x in reads + writes if size(x) > 1)
            cyc = n / 2 if short and q == "V" else n
        d = CYC * cyc / 2 if q == "P" else max(FIX[q] + CYC * cyc, 55)
        calls.append((q, reads, writes, lambda: issue(q, reads, writes, call, group), d, d))

    def join(k):
        x = calls[-k:]
        d = sum(c[4] for c in x)
        calls[-k:] = [(x[0][0], sum([c[1] for c in x], []), sum([c[2] for c in x], []), lambda: [c[3]() for c in x], d, d)]

    def isr(x):
        return isinstance(x, tuple)

    def val(x):
        return ap(x) if isr(x) else x

    def tt(out, a, b, o):
        op("V", [a, b], [out], lambda: g.vector.tensor_tensor(ap(out), ap(a), ap(b), o),
           cyc=size(out) * (1 if "psum" in (SCRATCH[a[0]][0], SCRATCH[b[0]][0]) else 2))

    def ts(out, a, s1, o0, s2=None, o1=None):
        rd = [a] + [x for x in (s1, s2) if isr(x)]
        if o1 is None:
            op("V", rd, [out], lambda: g.vector.tensor_scalar(ap(out), ap(a), val(s1), None, o0))
        else:
            op("V", rd, [out], lambda: g.vector.tensor_scalar(ap(out), ap(a), val(s1), val(s2), o0, o1))

    def cp(out, a):
        op("V", [a], [out], lambda: g.vector.tensor_copy(ap(out), ap(a)))

    def ms(out, v):
        op("V", [], [out], lambda: g.vector.memset(ap(out), v))

    def scan(out, d0, d1, o0, o1, first=0.0):
        op("V", [d0, d1] + [x for x in (first,) if isr(x)], [out],
           lambda: g.vector.tensor_tensor_scan(ap(out), ap(d0), ap(d1), val(first), o0, o1))

    def rowsum(out, a):
        op("V", [a], [out], lambda: g.vector.tensor_reduce(ap(out), ap(a), AxisListType.X, OP.add))

    def act(out, a, f, bias=0.0, scale=1.0, acc=None):
        rd = [a] + [x for x in (bias, scale) if isr(x)]
        if acc is None:
            op("S", rd, [out], lambda: g.scalar.activation(ap(out), ap(a), f, bias=val(bias), scale=val(scale)))
        else:
            op("S", rd, [out, acc], lambda: g.scalar.activation(ap(out), ap(a), f, bias=val(bias), scale=val(scale), accum_out=ap(acc)),
               cyc=max(size(out), 52) + 23)

    def lin(out, a, scale=1.0, bias=0.0):
        act(out, a, ACT.Identity, bias=bias, scale=scale)

    def mm(out, l, rhs, start=True, stop=True):
        op("P", [l, rhs], [out], lambda: g.tensor.matmul(ap(out), ap(l), ap(rhs), start, stop), group=not start,
           cyc=max(min(64, size(l)), size(rhs)) * (4 if SCRATCH[l[0]][2] == F else 1))

    def iota(out, pat, base=0, cm=0):
        op("G", [], [out], lambda: g.iota(ap(out), pat, base, cm, allow_small_or_imprecise_dtypes=True), cyc=2 * size(out))

    def keep(out, a, cmp, fill, sign):
        op("G", [a], [out], lambda: g.affine_select(ap(out), ap(a), [[sign, 128]], cmp, fill, 0, -sign), cyc=300)

    def gather(q, out, win, offs, f=ACT.Identity, add=0.0):
        if q == "V":
            op("V", [win, offs], [out], lambda: g.vector.tensor_scalar(ap(out), ap(win).indirect(ap(offs)), add, None, OP.add),
               cyc=55 + GATHER * size(out))
        else:
            op("S", [win, offs], [out], lambda: g.scalar.activation(ap(out), ap(win).indirect(ap(offs)), f, bias=add),
               cyc=60 + GATHER * size(out))

    def gtt(out, win, offs, b, o):
        op("V", [win, offs, b], [out], lambda: g.vector.tensor_tensor(ap(out), ap(win).indirect(ap(offs)), ap(b), o),
           cyc=55 + GATHER * size(out))

    def scatter(q, win, offs, a, add=None):
        if q == "S":
            call = lambda: g.scalar.activation(ap(win).indirect(ap(offs)), ap(a), ACT.Silu)
        elif add is None:
            call = lambda: g.vector.tensor_copy(ap(win).indirect(ap(offs)), ap(a))
        else:
            call = lambda: g.vector.tensor_scalar(ap(win).indirect(ap(offs)), ap(a), 1.0, add, OP.mult, OP.add)
        op(q, [a, offs], [win], call, cyc=50 + SCATTER * size(a))

    def dma(q, out, a, sem, rd, wr, **how):
        def go():
            deps(q, rd, wr)
            eng[q].dma_start(out, a, **how).then_inc(T.sem[sem], 16)
            cnt[sem] = 16
            for x, w in [(x, False) for x in rd] + [(x, True) for x in wr]:
                hist.setdefault(x[0], []).append((sem, sem, 16, x, w))
            c = dict(known[q])
            c[sem] = 16
            clk[(sem, 16)] = c
        x = (wr + rd)[0]
        calls.append((q, rd, wr, go, 1000 if q == "G" else 50, DMA + size(x) * (5 if q == "G" else 1 if SCRATCH[x[0]][2] == B else 2)))

    def send(src, dst, to, frm, sem):
        def go():
            deps("G", [src], [])
            rid, pid = topo.addr(to, core)
            g.remote_dma(ap(dst), ap(src), T.sem[sem], T.sem["loc"], pid, rid, topo.mask(core, to))
            cnt["loc"] = cnt.get("loc", 0) + len(topo.engines(core, to))
            cnt[sem] = len(topo.engines(frm, core))
            hist[dst[0]] = [(sem, sem, cnt[sem], dst, True)]
        more = FIRST if sem == "aF0" else 0
        calls.append(("G", [src], [dst], go, 500 + more, REMOTE + more + size(src) * (5 if SCRATCH[src[0]][2] == B else 10)))

    def bank(n, a=0, b=512, s=1):
        return r("b%d" % n, a, b, s)

    def one(name, n):
        return r(name, 0, n, 1, 1)

    dma("Y", ap(r("Ui", 0, 128)), T.stk[:, 0:128], "dstk", [], [r("Ui", 0, 128)])
    dma("S", ap(r("bl", 0, 4096)), T.ball[:, :], "dball", [], [r("bl", 0, 4096)])
    dma("Y", ap(r("w")), T.wt[:, :], "dwt", [], [r("w")])
    dma("S", ap(r("Ui", 128, 512)), T.stk[:, 128:512], "dstk2", [], [r("Ui", 128, 512)])

    c1 = L1 // 16
    U16, BIG = 65536.0, 1048576.0

    def u(j):
        return r("u", j, j + 1)

    def z(j):
        return r("z", j, j + 1)

    def m(j):
        return r("m", 128 * j, 128 * j + 128)

    def row(name, p):
        return r(name, 0, None, 1, 1, p)

    def total(out, n, parts):
        for j, x in enumerate(parts):
            mm(bank(n, 0, 128), r("ID"), x, j == 0, j == len(parts) - 1)
        lin(out, bank(n, 0, 128))

    iota(r("cP"), [[0, 1]], 0, 1)
    iota(r("cQ"), [[0, 1]], 2064, 1)
    iota(r("rA"), [[0, 8], [1, 16]])
    iota(r("rP"), [[1, 144]])
    iota(r("rG"), [[1, 8], [0, 16]], 129)
    for h in range(2):
        a, b = 2048 * h, 2048 * h + 2048
        for k in range(a, b, 512):
            iota(r("bf", k, k + 512), [[0, 512]], 33)
        dma("G", ap(r("bf", a, b)), T.ball[:, a:b], "dbf%d" % h, [r("bl", 0, 1)], [r("bf", a, b)], accum_op=OP.add)
    iota(r("r256", 0, c1), [[256, c1]])
    iota(r("r256", c1, 32), [[256, 32 - c1]])
    iota(r("nb"), [[16, 4]])
    iota(r("nr"), [[1, 64]])
    lin(r("k4"), r("nr"), 0.0, 8192.0)
    lin(r("a16"), r("rA"), 16.0)
    ms(r("ones"), 1.0)
    ms(r("RM"), 1.0)
    ts(r("cG"), r("cP"), 0.0625, OP.mult, 129.0 - 15.0 / 32, OP.add)
    ms(r("RM", 0, 2048, 16), 0.0)
    ts(r("cA"), r("cG"), -16.0, OP.mult, r("cQ"), OP.add)
    ts(r("c15"), r("cG"), 16.0, OP.mult, 15.0 - 2064, OP.add)
    ms(r("RM", 1, 2048, 16), 0.0)
    ts(r("z"), r("rA", 0, 3), r("cA"), OP.is_equal)
    ts(r("dm"), r("cA"), 1.0, OP.is_ge)
    ts(u(2), r("cA"), 1.0, OP.is_ge, -0.5, OP.mult)
    ts(u(3), r("cA"), 0.0, OP.is_equal, -BIG, OP.mult)
    ts(r("ID"), r("rP", 0, 128), r("cP"), OP.is_equal)
    ts(r("SH"), r("rP", 1, 129), r("cP"), OP.is_equal, r("dm"), OP.mult)
    ts(r("BO"), r("rG"), r("cG"), OP.is_equal)
    ts(r("W"), r("rP"), r("c15"), OP.is_equal)
    ts(r("M16"), r("rA", 0, 64), r("cA"), OP.is_equal)
    ts(r("wi"), r("w"), 4.0, OP.add)
    ms(r("y", 512, 576), 0.0)
    ts(r("wi"), r("wi"), 7, OP.bitwise_and)
    ms(r("FZ"), 0.0)
    ts(r("wf"), r("wi"), -4.0, OP.add, 512.0, OP.mult)
    ms(r("vi"), 0)
    lin(m(0), r("BO"), u(2))
    lin(m(1), r("BO"), -1.0)
    keep(r("TRI"), m(0), OP.is_ge, 0.0, 1)
    keep(r("UP"), m(1), OP.is_gt, 0.0, -1)
    keep(r("UPz"), r("UP"), OP.not_equal, 32.0, 1)
    lin(r("WS"), r("BO"), r("wf"))
    mm(bank(7, 0, 1), r("WS"), r("ones", 0, 1))
    for a, b in ((0, 128), (128, 512)):
        cp(r("off", a, b), r("Ui", a, b))
        ts(r("o", a, b), r("Ui", a, b), -16384.0, OP.add)
    ts(u(4), bank(7, 0, 1), -128.0, OP.mult, -96 * U16, OP.add)
    ms(r("acc"), 0.0)
    ms(r("s2"), 0.0)
    tt(u(4), u(4), z(0), OP.mult)
    ms(r("acc", 7, 8), -256.0)
    ms(row("s2", 0), 1.0 / 32)
    ms(row("s2", 32), 1.0)
    lin(u(5), r("cA"), 16.0)
    lin(r("il"), r("r256"), 1.0, u(5))
    lin(r("il8"), r("il"), 1.0, 8.0)
    ts(r("R16"), r("rA", 0, 64), 1.0, OP.is_ge)
    lin(r("nd"), r("nb"), 1.0, r("cA"))
    lin(r("nb"), r("nd"), 1.0, 0.5)
    lin(r("nd"), r("nd"), 1.0, 4096.0)
    lin(m(2), r("ID"), 192 * U16)
    lin(m(3), r("SH"), BIG)
    lin(r("BOm"), r("BO"), -8192.0)
    ts(u(10), r("cA"), 8.0, OP.is_le, u(2), OP.mult)
    ms(r("cap"), 255.0)
    act(r("cap"), r("cap"), ACT.Silu)
    ms(r("zer"), 0.0)
    ms(r("ri"), 1000.0)
    cp(r("wi"), r("cA"))
    ts(r("wi"), r("wi"), 3, OP.bitwise_and)
    ts(u(9), r("wi"), 0.0, OP.is_equal, -8.0, OP.mult)
    lin(r("fs"), z(0), 1.0 / 1024)
    lin(u(6), z(0), 144.5005, z(2))
    lin(u(7), z(0), 0.125)
    lin(u(8), z(2), 0.0625)
    lin(r("bo"), r("cA"), -0.5, 1.0)
    lin(r("fb"), z(1), 145.0, u(6))
    lin(u(11), z(1), 128.0, u(8))
    lin(u(12), z(0), -128.0, u(11))
    lin(r("BC0"), r("BO"), u(7))
    lin(r("BCn"), r("BO"), u(12))
    lin(m(5), r("SH"), -192 * U16)
    lin(m(6), r("BO"), u(4))
    lin(m(7), r("BO"), u(3))
    lin(r("Wk"), r("W"), r("dm"))
    lin(r("Ww"), r("W"), r("wf"))
    total(r("MA"), 6, [m(2), m(5), m(6)])
    total(r("MB"), 7, [m(3), m(7)])
    lin(r("ID8"), r("ID"), 8.0)
    lin(r("IDn"), r("ID"), -1.0)
    lin(r("IDh"), r("ID"), 0.5)
    lin(r("Wh"), r("W"), 0.5)
    lin(r("T8"), r("BO"), u(10))
    lin(r("bv"), u(9), 1.0, 8.5)
    lin(r("SHf"), r("SH"))
    lin(r("BOf"), r("BO"))
    lin(r("BOd"), r("BO"), r("dm"))
    lin(r("nh"), r("nr"), 1.0, 33.0)
    ms(r("hW"), 512.0)
    iota(row("hW", 0), [[512, 32]])
    ms(row("hW", 32), 0.0)
    ms(r("hA"), 512.0)
    ms(r("hA", 0, 256, 1, 1, 0), 0.0)
    ms(r("hA", 256, 512, 1, 1, 0), 8192.0)
    iota(row("hA", 32), [[0, 2], [1, 256]])
    ms(r("hB"), 1.0)
    ms(row("hB", 0), -15.0)
    ms(row("hB", 32), -4352.0)

    def gat(t, q, a, b):
        gather(q, r("P", 16 * a, 16 * b), r("bf" if t else "bl", 0, 4096), r("off", a, b), add=-32.0 if t else 1.0)

    def gats(t, a, b):
        for x, y in VG[t]:
            if x == a:
                gat(t, "V", x, y)
                a = y
        gat(t, "S", a, b)

    def wrap(out, name, src, a, b, stop=True):
        for j in range(16):
            mm(out, r(name, 15 - j, 143 - j), r(src, a + j, b, 16), False, stop and j == 15)
            if j % 8 == 7:
                join(8)

    def xcopy(c):
        a, b = CH[c]
        for j in range(4):
            mm(bank(c % 2, j, 4 * (b - a), 4), r("ID"), r("P", 16 * a, 16 * b, 16))
        join(4)

    done = {}

    def count(c, d, w, src):
        done[c] = done.get(c, 0) % 15 + 1
        mm(bank(2 + c % 2, 0, CH[c][1] - CH[c][0]), r(w, 15 - d, 143 - d), src, done[c] == 1, done[c] == 15)

    def comps(c, j0=0, j1=len(VD)):
        a, b = CH[c]
        for d0, s in VD[j0:j1]:
            n, k = b - a, 16 // s
            at = 1920 * (c % 2) + (512 * (d0 - 1) if d0 < 8 else 1792)
            tt(r("C", at, at + k * n), r("P", 16 * a + d0, 16 * b, s), bank(c % 2, 0, 4 * n, s // 4), OP.is_lt)
            for j in range(k):
                count(c, d0 + s * j, "W", r("C", at + j, at + k * n, k))
            join(k)

    def diffs(c):
        a, b = CH[c]
        n = b - a
        for j in range(3):
            o = bank(7 - 2 * (c % 2), n * j, n * j + n)
            mm(o, r("ID"), r("P", 16 * a, 16 * b, 16), True, False)
            mm(o, r("IDn"), r("P", 16 * a + 4 * j + 4, 16 * b, 16), False, True)
        join(6)

    def signs(c):
        n, at = CH[c][1] - CH[c][0], 1920 * (c % 2) + 1536
        act(r("C", at, at + 3 * n), bank(7 - 2 * (c % 2), 0, 3 * n), ACT.Sign, bias=-0.5)

    def scount(c):
        n, at = CH[c][1] - CH[c][0], 1920 * (c % 2) + 1536
        for j in range(3):
            count(c, 4 * j + 4, "Wh", r("C", at + n * j, at + n * j + n))
        join(3)

    def pmax(a, b):
        scan(r("PM", 16 * a, 16 * b), r("RM", 0, 16 * (b - a)), r("P", 16 * a, 16 * b), OP.mult, OP.max)
        if b <= L1:
            iota(r("PM", 16 * a, 16 * b, 16), [[0, b - a]], 256)

    def vote(c):
        a, b = CH[c]
        act(r("sg", a, b), bank(2 + c % 2, 0, b - a), ACT.Sign, bias=8.5 if c < 3 else r("bv"), scale=-1.0)
        if c > 2:
            mm(bank(2 + c % 2, 256, 256 + b - a), r("T8"), r("sg", a, b))
        mm(bank(2 + c % 2, 128, 128 + b - a), r("TRI"), r("sg", a, b))

    def over(c):
        a, b = CH[c]
        act(r("X", a, b), bank(2 + c % 2, 128, 128 + b - a), ACT.Relu, bias=r("bo"), acc=r("acc", c, c + 1))

    def kconst(a, b):
        o = bank(4, a // 16, b // 16)
        mm(o, one("ones", 128), r("r256", a // 16, b // 16, 1, 1), True, False)
        mm(o, one("a16", 128), one("ones", (b - a) // 16), False, False)
        join(2)

    def kwrap(a, b):
        wrap(bank(4, a // 16, b // 16), "Wk", "X", a, b)

    def pick(a, b):
        gather("S", r("mx", a, b), r("PM", 16 * a, 16 * b), r("lu", a // 16, b // 16))

    def less(a, b, n):
        mm(bank(n, a, b), r("IDn"), r("P", 16 * a, 16 * b, 16), True, False)
        mm(bank(n, a, b), r("ID"), r("mx", a, b), False, True)

    def places(a, b, n):
        a, b = a // 16, b // 16
        mm(bank(n, a, b), one("rA", 128), one("ones", b - a), True, False)
        mm(bank(n, a, b), r("LA"), r("hW", a, b), False, False)
        wrap(bank(n, a, b), "Ww", "y", 16 * a, 16 * b)
        return [lambda: cp(r("vi", a, b), bank(n, a, b)),
                lambda: ts(r("vi", a, b), r("vi", a, b), 4095, OP.bitwise_and),
                lambda: cp(r("vu", a, b), r("vi", a, b))]

    def own(a, b):
        scatter("S", r("bf", 0, 4096), r("vu", a // 16, b // 16), r("y33", a, b))

    def eq(*js):
        for j in js:
            mm(bank(6, 64 * j, 64 * j + 64), r("BC0"), r("o", 64 * j, 64 * j + 64), False, j == 7)

    def up(*js):
        for j in js:
            mm(bank(6, 64 * j, 64 * j + 64), r("SHf"), r("T1", 64 * j, 64 * j + 64), False, False)

    def ra(a, b):
        for j, (l, x) in enumerate((("MA", "X"), ("WS", "y"), ("LA", "hA"))):
            mm(bank(5, a, b), r(l), r(x, a, b), j == 0, j == 2)

    def stacks(a, b, last=False):
        return [lambda: tt(r("s1", a, b), bank(5, a, b), r("o", a, b), OP.max),
                lambda: tt(r("Ui", a, b), bank(6, a, b), r("s1", a, b), OP.max),
                lambda: ts(r("Ui", a, b), r("Ui", a, b), 4095, OP.bitwise_and),
                lambda: cp(r("o" if last else "off", a, b), r("Ui", a, b))]

    def under(src, out, at):
        k = size(src)
        for j in range(4):
            act(r("jk", at + k * j, at + k * j + k), src, ACT.Sign, bias=r("nb", j, j + 1), scale=-1.0,
                acc=r(out[0], out[1] + j, out[1] + j + 1))

    def sums(h, k, n, name):
        mm(bank(n, 64, 65 + k), r("BO"), r("FZ", 40 * h, 40 * h + k + 1))
        mm(bank(n, 128, 129 + k), r(name), r("FZ", 40 * h, 40 * h + k + 1))
        join(2)

    def ends(h, k, n):
        scan(r("sc", 40 * h, 40 * h + k + 1), r("ones", 0, k + 1), bank(n, 64, 65 + k), OP.mult, OP.add)

    def ranks(h, k, n):
        tt(r("ri", 40 * h, 40 * h + k + h), r("sc", 40 * h, 40 * h + k + h), bank(n, 128, 128 + k + h), OP.add)

    def flags(c):
        a, b = CH[c]
        act(r("pf", a - L1, b - L1), bank(2 + c % 2, 256, 256 + b - a), ACT.Relu, bias=-3.0)

    def passing(t, c):
        a, b = CH[c]
        scan(r("cn%d" % t, a - L1, b - L1), r("pf", a - L1, b - L1), r("cap", 0, b - a), OP.add, OP.min,
             r("sc", c1 - 1, c1) if a == L1 else r("cn%d" % t, a - L1 - 1, a - L1))

    def passed(t, c):
        a, b = CH[c]
        under(r("cn%d" % t, a - L1, b - L1), r("ca", 4 * (c - 3)), 256 + 4 * (a - L1))
        mm(bank(1, 0, 4), r("IDh"), r("ca", 4 * (c - 3), 4 * (c - 2)), False, c == 4)

    rest = []
    for t in range(3):
        last = t == 2
        to, frm = T.cores[(rank + t + 1) % N], T.cores[(rank - t - 1) % N]
        gats(t, 0, 64)
        gats(t, 64, 128)
        for f in rest:
            f()
        xcopy(0)
        comps(0, 0, 1)
        if t:
            for a, b in zip([0] + CUT, CUT):
                ts(r("o", a, b), r("Ui", a, b), -16384.0, OP.add)
        gats(t, 128, 192)
        comps(0, 1)
        pmax(*CH[0])
        xcopy(1)
        vote(0)
        for a in (0, 256):
            act(r("fl", a, a + 256), r("o", a, a + 256), ACT.Identity, bias=r("fb"), scale=r("fs"))
        gats(t, 192, 320)
        over(0)
        comps(1, 0, 1)
        mm(bank(6), r("BCn"), r("fl"), True, False)
        for j in range(1, 5):
            comps(1, j, j + 1)
            eq(2 * j - 2, 2 * j - 1)
        pmax(*CH[1])
        xcopy(2)
        vote(1)
        for a in (0, 256):
            tt(r("T1", a, a + 256), bank(6, a, a + 256), r("Ui", a, a + 256), OP.mult)
        gats(t, 320, 448)
        over(1)
        mm(bank(6), one("zer", 128), one("hA", 512), True, False)
        comps(2, 0, 1)
        up(0, 1)
        comps(2, 1, 2)
        comps(2, 2, 3)
        up(2, 3)
        comps(2, 3)
        pmax(*CH[2])
        xcopy(3)
        vote(2)
        diffs(3)
        up(4, 5)
        gats(t, 448, 480)
        over(2)
        gats(t, 480, 512)
        kconst(0, L1)
        comps(3, 0, 1)
        kwrap(0, L1)
        up(6, 7)
        mm(bank(6, 0, L1), r("MB"), r("X", 0, L1), False, False)
        comps(3, 1, 2)
        tt(r("FZ", 0, c1), bank(4, 0, c1), r("il8", 0, c1), OP.is_ge)
        cp(r("lu", 0, c1), bank(4, 0, c1))
        sums(0, c1, 4, "UP")
        signs(3)
        xcopy(4)
        comps(3, 2, 3)
        scount(3)
        diffs(4)
        ends(0, c1, 4)
        under(r("sc", 0, c1), r("cb", 0), 0)
        vote(3)
        signs(4)
        pmax(L1, 384)
        ranks(0, c1, 4)
        comps(4, 0, 2)
        scount(4)
        flags(3)
        over(3)
        comps(4, 2, 3)
        pmax(384, 448)
        ts(r("cu"), r("cb", 0, 4), 0.5, OP.mult, c1 / 2, OP.add)
        mm(bank(1, 0, 4), r("ID8"), r("cb", 0, 4), True, False)
        kconst(L1, 512)
        vote(4)
        pick(0, L1)
        passing(t, 3)
        gtt(r("ind"), r("ri", 0, 40), r("cu"), r("nr"), OP.is_le)
        pmax(*CH[4])
        ms(r("PM", 16 * L1, 8192, 16), 256.0)
        flags(4)
        over(4)
        less(0, L1, 5)
        wrap(bank(1, 0, 4), "W", "ind", 0, 64, False)
        kwrap(L1, 512)
        passing(t, 4)
        send(r("cn%d" % t, 184, 192), r("rf%d" % t), to, frm, "aF%d" % t)
        passed(t, 3)
        passed(t, 4)
        rowsum(r("ac"), r("acc"))
        ts(r("LA"), r("BOd"), r("ac"), OP.mult, r("s2"), OP.add)
        act(r("y", 0, L1), bank(5, 0, L1), ACT.Abs)
        v = places(0, L1, 7)
        cp(r("lu", c1, 32), bank(4, c1, 32))
        tt(r("FZ", 40, 72), bank(4, 0, 32), r("il"), OP.is_equal)
        gtt(r("y", L1, 512), r("PM", 16 * L1, 8192), r("lu", c1, 32), r("P", 16 * L1, 8192, 16), OP.subtract)
        v[0]()
        sums(1, 32, 3, "UPz")
        ends(1, 32, 3)
        v[1]()
        ts(r("idu"), bank(1, 0, 4), 8.0 * c1 + 96, OP.add)
        v[2]()
        gather("S", r("ty%d" % t), r("y"), r("idu"), ACT.Abs)
        send(r("ty%d" % t), r("ry%d" % t), to, frm, "aY%d" % t)
        act(r("y", L1, 512), r("y", L1, 512), ACT.Abs)
        mm(bank(6, L1, 512), r("MB"), r("X", L1, 512), False, False)
        ranks(1, 32, 3)
        under(r("sc", 40, 72), r("cb", 4), 128)
        v = places(L1, 512, 0)
        s0 = SL if last else S0
        mm(bank(6), r("LA"), r("hB"), False, True)
        ra(0, s0)
        lin(r("y33", 0, L1), r("y", 0, L1), 1.0, 33.0)
        own(0, L1)
        lin(r("y33", L1, 512), r("y", L1, 512), 1.0, 33.0)
        v[0]()
        ts(r("cz"), r("cb", 4, 8), 0.5, OP.mult, 16.0, OP.add)
        x = stacks(0, s0, last)
        x[0]()
        ra(s0, 512)
        v[1]()
        x[1]()
        v[2]()
        gtt(r("iz"), r("ri", 40, 80), r("cz"), r("nh"), OP.is_equal)
        x[2]()
        gtt(r("vz"), r("vi"), r("cz"), r("iz"), OP.mult)
        zb = bank(3, 256, 320)
        mm(zb, one("ones", 128), one("k4", 64), True, False)
        mm(zb, r("BOm"), r("iz"), False, False)
        mm(zb, r("BOf"), r("vz"), False, True)
        x[3]()
        if last:
            dma("S", T.yo[:, 0:s0], ap(r("o", 0, s0)), "dyo0", [r("o", 0, s0)], [])
        own(L1, 512)
        tt(r("zm"), zb, r("M16"), OP.mult)
        rest = [f for fs in zip(*[stacks(a, b, last) for a, b in zip(CUT, CUT[1:]) if a >= s0]) for f in fs]
        scan(r("zs"), r("R16"), r("zm"), OP.mult, OP.add)
        rest.pop(0)()
        ts(r("zf"), r("nb"), r("rf%d" % t, 7, 8), OP.is_gt, 8192.0, OP.mult)
        for j in range(4):
            ts(r("zu", j, j + 1), r("zs", 16 * j + 15, 16 * j + 16), r("zf", j, j + 1), OP.max, r("nd", j, j + 1), OP.min)
        if last:
            ts(r("bl", 0, 768), r("bf", 0, 768), 1.5 * 2 ** 23 - 33, OP.add, -1.5 * 2 ** 23, OP.add)
            lin(r("y33", 0, 256), r("bf", 768, 1024), 1.0, 1.5 * 2 ** 23 - 33)
            lin(r("bl", 768, 1024), r("y33", 0, 256), 1.0, -1.5 * 2 ** 23)
            scatter("V", r("bl"), r("zu"), r("ry%d" % t))
        else:
            scatter("V", r("bf"), r("zu"), r("ry%d" % t), 33.0)
    dma("Y", T.yb[:, :], ap(r("bl", 0, 1024)), "dyb", [r("bl", 0, 1024)], [])
    for f in rest:
        f()
    dma("S", T.yo[:, SL:512], ap(r("o", SL, 512)), "dyo1", [r("o", SL, 512)], [])
    if not ORDER:
        ORDER.extend(order(calls, meet, inside))
    for i in ORDER:
        calls[i][3]()
    for sem in cnt:
        need("Y", sem, cnt[sem])
